import numpy as np
import ml_dtypes


def mxq(x, axis, fmt="e4m3"):
    dtype, down = {"e4m3": (ml_dtypes.float8_e4m3fn, 7), "e5m2": (ml_dtypes.float8_e5m2, 14)}[fmt]
    v = np.moveaxis(np.asarray(x, np.float32).astype(ml_dtypes.bfloat16).astype(np.float64), axis, -1)
    blocks = v.reshape(v.shape[:-1] + (-1, 32))
    amax = np.abs(blocks).max(-1, keepdims=True)
    byte = np.maximum(np.where(amax > 0, np.frexp(amax)[1] - 1 + 127, 0) - down, 1)
    scale = np.exp2(byte - 127.0)
    codes = (blocks / scale).astype(np.float32).astype(dtype).astype(np.float64)
    return np.moveaxis((codes * scale).reshape(v.shape), -1, axis)


WIDE = False


def mx_kscale(k):
    if not WIDE:
        return np.ones(k)
    levels = np.array([10, -10, 5, -5, 0])
    if k % 512:
        return np.exp2(np.random.permutation(np.resize(levels, k // 32))).repeat(32)
    a = np.empty((k // 512, 16))
    for p in range(k // 512):
        a[p, :8] = np.random.permutation(np.resize(levels, 8))
        for g in range(8):
            far = levels[np.abs(levels - a[p, g]) >= 10]
            a[p, g + 8] = far[np.random.randint(len(far))]
    return np.exp2(a.ravel()).repeat(32)


def f64(x):
    return np.asarray(x).astype(np.float64)


def striped(idx):
    return np.tile(idx.reshape(-1, 16).T, (8, 1)).astype(np.uint16)


def unstriped(offs):
    return offs[:16].T.reshape(-1).astype(np.int64)


E2M1 = np.array([0.0, 0.5, 1.0, 1.5, 2.0, 3.0, 4.0, 6.0, -0.0, -0.5, -1.0, -1.5, -2.0, -3.0, -4.0, -6.0])


def pack_weight(w, fmt):
    k, n = w.shape
    w = f64(np.asarray(w, np.float32).astype(ml_dtypes.bfloat16)).reshape(k // 32, 32, n)
    amax = np.abs(w).max(1)
    if fmt == "e4m3":
        byte = np.frexp(amax)[1] - 1 + 127 - 7
    else:
        mant, ex = np.frexp(amax / 6.0)
        byte = np.where(mant > 0.5, ex, ex - 1) + 127
    byte = np.clip(np.where(amax > 0, byte, 1), 1, 254)
    scaled = (w * np.exp2(127.0 - byte)[:, None, :]).reshape(k, n).astype(np.float32)
    by_word = np.ascontiguousarray(scaled.reshape(k // 512, 128, 4, n).transpose(0, 1, 3, 2))
    if fmt == "e4m3":
        words = by_word.astype(ml_dtypes.float8_e4m3fn).view(np.uint8)
    else:
        c = by_word.astype(ml_dtypes.float4_e2m1fn).view(np.uint8) & 0xF
        words = (c[..., 0::2] | (c[..., 1::2] << 4)).reshape(k // 512, 128, 2 * n)
    return np.ascontiguousarray(words), np.ascontiguousarray(byte.astype(np.uint8).reshape(k // 512, 16, n))


def unpack_weight(words, scales, fmt):
    g, _, n = scales.shape
    words = np.ascontiguousarray(words).reshape(g, 128, n, -1)
    if fmt == "e4m3":
        vals = words.view(ml_dtypes.float8_e4m3fn).astype(np.float64)
    else:
        nib = np.empty((g, 128, n, 4), np.uint8)
        nib[..., 0::2] = words & 0xF
        nib[..., 1::2] = words >> 4
        vals = E2M1[nib]
    vals = vals * np.repeat(np.exp2(scales.astype(np.float64) - 127.0), 8, axis=1)[..., None]
    return vals.transpose(0, 1, 3, 2).reshape(g * 512, n)


def gelu(v):
    return 0.5 * v * (1.0 + np.tanh(np.sqrt(2.0 / np.pi) * (v + 0.044715 * v**3)))


K, K2, H, N, T, T2, S, P = 1024, 512, 1024, 512, 2048, 1024, 512, 512

def setup_inputs():
    n = np.random.standard_normal
    s = mx_kscale(K)[:, None]
    s2 = mx_kscale(K2)[:, None]
    u = mx_kscale(H)[:, None]
    tab_words, tab_scales = pack_weight(n((K, T)) * s, "e4m3")
    wb_words, wb_scales = pack_weight(n((K, H)) / np.sqrt(K) / s * u.T, "e2m1")
    wc_words, wc_scales = pack_weight(n((H, N)) / np.sqrt(H) / u, "e4m3")
    return {
        "tab_words": tab_words, "tab_scales": tab_scales,
        "offs": striped(np.random.permutation(T)[:P]),
        "base": (n((K2, T2)) * s2).astype(np.float32),
        "xs": (np.round(16 * n((K2, S))) / 16 * s2).astype(np.float32),
        "offs2": striped(np.random.permutation(T2)[:S]),
        "offs3": striped(np.random.permutation(T2)[:P]),
        "wp": (n((K2, H)) / np.sqrt(K2) / s2 * u.T).astype(np.float32),
        "wth": (0.5 * n((K, H)) / np.sqrt(K) / s).astype(np.float32),
        "wb_words": wb_words, "wb_scales": wb_scales,
        "wc_words": wc_words, "wc_scales": wc_scales,
    }

def reference(tab_words, tab_scales, offs, base, xs, offs2, offs3, wp, wth,
              wb_words, wb_scales, wc_words, wc_scales):
    page = f64(base).copy()
    page[:, unstriped(offs2)] = f64(xs)
    a = mxq(f64(wp), 0, "e4m3").T @ mxq(page, 0, "e4m3")
    x = a[:, unstriped(offs3)]
    v = unpack_weight(tab_words, tab_scales, "e4m3")[:, unstriped(offs)]
    b = unpack_weight(wb_words, wb_scales, "e2m1").T @ v
    th = mxq(f64(wth), 0, "e4m3").T @ v
    z = x * np.cos(th) + b * np.sin(th)
    return unpack_weight(wc_words, wc_scales, "e4m3").T @ mxq(z, 0, "e4m3")

@@ -1,0 +1,326 @@
+import math
+from contextlib import ExitStack
+
+import concourse.mybir as mybir
+from concourse.masks import make_identity
+
+F32 = mybir.dt.float32
+BF16 = mybir.dt.bfloat16
+I32 = mybir.dt.int32
+U32 = mybir.dt.uint32
+U16 = mybir.dt.uint16
+U8 = mybir.dt.uint8
+FP8X4 = mybir.dt.float8_e4m3fn_x4
+FP4X4 = mybir.dt.float4_e2m1fn_x4
+ACT = mybir.ActivationFunctionType
+MULT = mybir.AluOpType.mult
+
+P = 128
+PACK = 4
+BANK = 512
+K, K2, H, N, T, T2, S = 1024, 512, 1024, 512, 2048, 1024, 512
+FLOPS = 2 * (K2 * H * T2 + 2 * K * H * S + H * N * S)
+
+
+def tile_list_ion_pulse_compensation_kernel(
+    tc, tab_words, tab_scales, offs, base, xs, offs2, offs3, wp, wth,
+    wb_words, wb_scales, wc_words, wc_scales, out,
+):
+    nc = tc.nc
+    with ExitStack() as ctx:
+        lists = ctx.enter_context(tc.tile_pool(name="lists", bufs=1))
+        sb = ctx.enter_context(tc.tile_pool(name="sb", bufs=1))
+        ps = ctx.enter_context(tc.psum_pool(name="ps", bufs=1))
+
+        def tile(name, shape, dtype, tag=None, bufs=1):
+            return sb.tile(shape, dtype, name=name, tag=tag or name, bufs=bufs, align_bytes=64)
+
+        def bank(name, tag, bufs):
+            return ps.tile([P, BANK], F32, name=name, tag=tag, bufs=bufs)
+
+        def load_list(name, src):
+            t = lists.tile([P, S // 16], U16, name=name, tag=name)
+            nc.sync.dma_start(t[:], src)
+            return t
+
+        def load_scales(name, src, width):
+            t = tile(name, [P, 2 * width], U8)
+            words = t[:].bitcast(I32)
+            nc.vector.memset(words, 0)
+            rows = src.bitcast(I32)
+            for q in range(4):
+                nc.gpsimd.dma_start(
+                    out=words[32 * q : 32 * q + 4, :].rearrange("p (a c) -> p a c", a=2),
+                    in_=rows[:, 4 * q : 4 * q + 4, :].rearrange("a q c -> q a c"),
+                )
+            return t
+
+        def load_plane(t):
+            page = tile("page%d" % t, [P, T2], F32, tag="a", bufs=8)
+            new = tile("new%d" % t, [P, S], F32, tag="new%d" % t)
+            nc.sync.dma_start(out=page[:], in_=base.rearrange("(p t) c -> p t c", t=PACK)[:, t, :])
+            nc.sync.dma_start(out=new[:], in_=xs.rearrange("(p t) c -> p t c", t=PACK)[:, t, :])
+            return page, new
+
+        def load_raw(name, src, a, g):
+            raw = tile(name, [P, PACK, BANK], F32, tag="raw", bufs=4)
+            rows = src[BANK * a : BANK * (a + 1), BANK * g : BANK * (g + 1)]
+            nc.sync.dma_start(out=raw[:], in_=rows.rearrange("(p t) c -> p t c", t=PACK))
+            return raw
+
+        def load_table(a):
+            words = tile("tab%d" % a, [P, T], U32)
+            nc.sync.dma_start(
+                out=words[:].bitcast(I32),
+                in_=tab_words[a].rearrange("p t i -> p (t i)").bitcast(I32),
+            )
+            return words
+
+        def quantise(name, rounded, width):
+            codes = tile(name + "_codes", [P, width], U32, tag={"wp0": "new3", "wth00": "new2"}.get(name))
+            scales = tile(name + "_scales", [P, width], U8)
+            nc.vector.quantize_mx(out=codes[:].bitcast(FP8X4), scales=scales[:], in_=rounded[:])
+            return codes, scales
+
+        def round_weights(name, raw, copy):
+            rounded = tile(name + "_bf", [P, PACK * BANK], BF16, tag="rounded", bufs=4)
+            copy(
+                out=rounded[:].rearrange("p (c i t) -> p c t i", i=4, t=PACK),
+                in_=raw[:].rearrange("p t (c i) -> p c t i", i=4),
+            )
+            return quantise(name, rounded, BANK)
+
+        warm = tile("warm", [P, 8], F32)
+        nc.vector.memset(warm[:], 0.0)
+        warm2 = tile("warm2", [P, 8], F32)
+        nc.scalar.activation(warm2[:], warm[:], ACT.Sin)
+        ident = tile("ident", [P, P], F32)
+        make_identity(nc, ident[:])
+        tab_sc = load_scales("tab_sc", tab_scales, T)
+        wb_sc = load_scales("wb_sc", wb_scales, H)
+        wc_sc = load_scales("wc_sc", wc_scales, N)
+
+        planes, tab, wp_raw, wth_raw, wp_q, wth_q = {}, {}, {}, {}, {}, {}
+        list2 = load_list("list2", offs2)
+        planes[0] = load_plane(0)
+        planes[1] = load_plane(1)
+        wp_raw[0] = load_raw("wp_raw0", wp, 0, 0)
+        planes[2] = load_plane(2)
+        planes[3] = load_plane(3)
+        tab[0] = load_table(0)
+        list1 = load_list("list1", offs)
+        wth_raw[(0, 0)] = load_raw("wth_raw00", wth, 0, 0)
+        tab[1] = load_table(1)
+        wth_raw[(1, 0)] = load_raw("wth_raw10", wth, 1, 0)
+        list3 = load_list("list3", offs3)
+        wp_raw[1] = load_raw("wp_raw1", wp, 0, 1)
+        wth_raw[(0, 1)] = load_raw("wth_raw01", wth, 0, 1)
+        wth_raw[(1, 1)] = load_raw("wth_raw11", wth, 1, 1)
+        wb_w = tile("wb_w", [P, 2 * 2 * H], U8)
+        nc.sync.dma_start(
+            out=wb_w[:].bitcast(I32).rearrange("p (a c) -> p a c", a=2),
+            in_=wb_words.bitcast(I32).rearrange("a p c -> p a c"),
+        )
+        wc_w = tile("wc_w", [P, 2 * N], U32)
+        nc.sync.dma_start(
+            out=wc_w[:].bitcast(I32).rearrange("p (a c) -> p a c", a=2),
+            in_=wc_words.rearrange("a p c i -> p a (c i)").bitcast(I32),
+        )
+
+        def pool_copy(out, in_):
+            nc.gpsimd.tensor_scalar(out, in_, 1.0, 0.0, MULT, mybir.AluOpType.add)
+
+        pairs = [tile("pairs%d" % h, [P, 2, BANK, 2], BF16) for h in range(2)]
+
+        def scatter_plane(t):
+            page, new = planes[t]
+            nc.vector.tensor_copy(page[:].indirect(list2[:]), new[:])
+            for h in range(2):
+                nc.scalar.copy(out=pairs[h][:, t // 2, :, t % 2], in_=page[:, BANK * h : BANK * (h + 1)])
+
+        scatter_plane(0)
+        wp_q[0] = round_weights("wp0", wp_raw[0], nc.scalar.copy)
+        scatter_plane(1)
+        wth_q[(0, 0)] = round_weights("wth00", wth_raw[(0, 0)], nc.scalar.copy)
+        scatter_plane(2)
+        scatter_plane(3)
+        wth_q[(1, 0)] = round_weights("wth10", wth_raw[(1, 0)], nc.scalar.copy)
+
+        page_q = []
+
+        def merge(h):
+            rounded = tile("page_bf%d" % h, [P, PACK * BANK], BF16, tag="rounded", bufs=4)
+            nc.vector.tensor_copy(
+                out=rounded[:].bitcast(I32).rearrange("p (c u) -> p c u", u=2),
+                in_=pairs[h][:].rearrange("p u c e -> p u (c e)").bitcast(I32).rearrange("p u c -> p c u"),
+            )
+            page_q.append(quantise("page%d" % h, rounded, BANK))
+
+        v_codes, v_scales = [], []
+
+        def gather_table(a):
+            codes = tile("v_codes%d" % a, [P, S], U32)
+            nc.vector.tensor_copy(codes[:], tab[a][:].indirect(list1[:]))
+            scales = tile("v_scales%d" % a, [P, S], U8)
+            nc.vector.tensor_copy(scales[:], tab_sc[:, T * a : T * (a + 1)].indirect(list1[:]))
+            v_codes.append(codes)
+            v_scales.append(scales)
+
+        picked, a_rows = {}, {}
+
+        def project(i):
+            codes, scales = wp_q[i // 4]
+            cols = slice(P * (i % 4), P * (i % 4 + 1))
+            rows = tile("a%d" % i, [P, T2], F32, tag="a", bufs=8)
+            for h in range(2):
+                acc = bank("a_acc", "wide", 2)
+                nc.tensor.matmul_mx(
+                    out=acc[:], lhsT=codes[:, cols].bitcast(FP8X4), lhsT_scale=scales[:, cols],
+                    rhs=page_q[h][0][:].bitcast(FP8X4), rhs_scale=page_q[h][1][:],
+                    start=True, stop=True,
+                )
+                nc.scalar.copy(out=rows[:, BANK * h : BANK * (h + 1)], in_=acc[:])
+            a_rows[i] = rows
+
+        def pick(i):
+            picked[i] = tile("x%d" % i, [P, S], F32, tag="x", bufs=8)
+            nc.vector.tensor_copy(picked[i][:], a_rows[i][:].indirect(list3[:]))
+
+        def by_plane(acc):
+            return acc[:].rearrange("p (m t) -> p t m", t=PACK)
+
+        cosines, sines, terms_b = {}, {}, {}
+
+        def angles(g, jt):
+            js = slice(P * jt, P * (jt + 1))
+            th = bank("th", "t", 2)
+            for a in range(2):
+                nc.tensor.matmul_mx(
+                    out=th[:], lhsT=v_codes[a][:, js].bitcast(FP8X4), lhsT_scale=v_scales[a][:, js],
+                    rhs=wth_q[(a, g)][0][:].bitcast(FP8X4), rhs_scale=wth_q[(a, g)][1][:],
+                    start=(a == 0), stop=(a == 1),
+                )
+            sine = tile("sine", [P, PACK, P], F32, bufs=8)
+            nc.scalar.activation(sine[:], by_plane(th), ACT.Sin)
+            size = tile("size", [P, PACK, P], F32, bufs=2)
+            nc.scalar.activation(size[:], by_plane(th), ACT.Abs)
+            cosine = tile("cosine", [P, PACK, P], F32, bufs=8)
+            nc.scalar.activation(cosine[:], size[:], ACT.Sin, bias=math.pi / 2, scale=-1.0)
+            cosines[(g, jt)], sines[(g, jt)] = cosine, sine
+
+        def weigh_b(g, jt):
+            js = slice(P * jt, P * (jt + 1))
+            b = bank("b", "b", 1)
+            for a in range(2):
+                c0 = H * a + BANK * g
+                nc.tensor.matmul_mx(
+                    out=b[:], lhsT=v_codes[a][:, js].bitcast(FP8X4), lhsT_scale=v_scales[a][:, js],
+                    rhs=wb_w[:, 2 * c0 : 2 * (c0 + BANK)].bitcast(FP4X4), rhs_scale=wb_sc[:, c0 : c0 + BANK],
+                    start=(a == 0), stop=(a == 1),
+                )
+            terms_b[(g, jt)] = tile("term_b", [P, PACK, P], F32, bufs=3)
+            nc.vector.tensor_tensor(terms_b[(g, jt)][:], by_plane(b), sines[(g, jt)][:], MULT)
+
+        z_q, terms_x = {}, {}
+
+        def combine(g, jt):
+            js = slice(P * jt, P * (jt + 1))
+            xt = bank("xt", "x", 1)
+            for q in range(4):
+                nc.tensor.transpose(xt[:, P * q : P * (q + 1)], picked[4 * g + q][:, js], ident[:])
+            term_x = tile("term_x", [P, PACK, P], F32, bufs=3)
+            nc.vector.tensor_tensor(term_x[:], by_plane(xt), cosines[(g, jt)][:], MULT)
+            terms_x[(g, jt)] = term_x
+
+        def add_terms(g, jt):
+            term_x = terms_x[(g, jt)]
+            z = bank("z", "z", 2)
+            for t in range(PACK):
+                for first, term in ((True, term_x), (False, terms_b[(g, jt)])):
+                    nc.tensor.matmul(
+                        out=z[:, P * t : P * (t + 1)], lhsT=term[:, t, :], rhs=ident[:],
+                        start=first, stop=not first, is_transpose=True,
+                    )
+            rounded = tile("z_bf", [P, PACK * P], BF16, bufs=2)
+            nc.scalar.copy(
+                out=rounded[:].rearrange("p (j t) -> p j t", t=PACK),
+                in_=z[:].rearrange("p (t j) -> p j t", t=PACK),
+            )
+            z_q[(g, jt)] = quantise("z%d%d" % (g, jt), rounded, P)
+
+        def control(jt):
+            acc = bank("out_acc", "wide", 2)
+            for nt in range(4):
+                for g in range(2):
+                    c0 = N * g + P * nt
+                    nc.tensor.matmul_mx(
+                        out=acc[:, P * nt : P * (nt + 1)],
+                        lhsT=wc_w[:, c0 : c0 + P].bitcast(FP8X4), lhsT_scale=wc_sc[:, c0 : c0 + P],
+                        rhs=z_q[(g, jt)][0][:].bitcast(FP8X4), rhs_scale=z_q[(g, jt)][1][:],
+                        start=(g == 0), stop=(g == 1),
+                    )
+            result = tile("result%d" % jt, [P, 4, P], F32, tag="x", bufs=8)
+            (nc.vector.tensor_copy if jt in (1, 3) else nc.scalar.copy)(out=result[:].rearrange("p n j -> p (n j)"), in_=acc[:])
+            nc.sync.dma_start(
+                out=out.rearrange("(n p) j -> p n j", p=P)[:, :, P * jt : P * (jt + 1)], in_=result[:]
+            )
+
+        merge(0)
+        merge(1)
+        gather_table(0)
+        gather_table(1)
+        project(0)
+        project(1)
+        project(2)
+        project(3)
+        wp_q[1] = round_weights("wp1", wp_raw[1], nc.vector.tensor_copy)
+        angles(0, 0)
+        wth_q[(0, 1)] = round_weights("wth01", wth_raw[(0, 1)], nc.vector.tensor_copy)
+        angles(0, 1)
+        wth_q[(1, 1)] = round_weights("wth11", wth_raw[(1, 1)], nc.vector.tensor_copy)
+        pick(0)
+        pick(1)
+        pick(2)
+        pick(3)
+        angles(0, 2)
+        angles(0, 3)
+        project(4)
+        project(5)
+        project(6)
+        project(7)
+        weigh_b(0, 0)
+        combine(0, 0)
+        weigh_b(0, 1)
+        combine(0, 1)
+        add_terms(0, 0)
+        angles(1, 0)
+        pick(4)
+        weigh_b(0, 2)
+        combine(0, 2)
+        add_terms(0, 1)
+        angles(1, 1)
+        pick(5)
+        weigh_b(0, 3)
+        combine(0, 3)
+        add_terms(0, 2)
+        angles(1, 2)
+        pick(6)
+        add_terms(0, 3)
+        angles(1, 3)
+        pick(7)
+        weigh_b(1, 0)
+        combine(1, 0)
+        weigh_b(1, 1)
+        combine(1, 1)
+        add_terms(1, 0)
+        weigh_b(1, 2)
+        combine(1, 2)
+        add_terms(1, 1)
+        control(0)
+        weigh_b(1, 3)
+        combine(1, 3)
+        add_terms(1, 2)
+        control(1)
+        add_terms(1, 3)
+        control(2)
+        control(3)

@@ -2,7 +2,6 @@ import math
 from contextlib import ExitStack
 
 import concourse.mybir as mybir
-from concourse.masks import make_identity
 
 F32 = mybir.dt.float32
 BF16 = mybir.dt.bfloat16
@@ -14,6 +13,7 @@ FP8X4 = mybir.dt.float8_e4m3fn_x4
 FP4X4 = mybir.dt.float4_e2m1fn_x4
 ACT = mybir.ActivationFunctionType
 MULT = mybir.AluOpType.mult
+ADD = mybir.AluOpType.add
 
 P = 128
 PACK = 4
@@ -77,7 +77,7 @@ def tile_list_ion_pulse_compensation_kernel(
             return words
 
         def quantise(name, rounded, width):
-            codes = tile(name + "_codes", [P, width], U32, tag={"wp0": "new3", "wth00": "new2"}.get(name))
+            codes = tile(name + "_codes", [P, width], U32, tag={"wp0": "new3"}.get(name))
             scales = tile(name + "_scales", [P, width], U8)
             nc.vector.quantize_mx(out=codes[:].bitcast(FP8X4), scales=scales[:], in_=rounded[:])
             return codes, scales
@@ -85,8 +85,8 @@ def tile_list_ion_pulse_compensation_kernel(
         def round_weights(name, raw, copy):
             rounded = tile(name + "_bf", [P, PACK * BANK], BF16, tag="rounded", bufs=4)
             copy(
-                out=rounded[:].rearrange("p (c i t) -> p c t i", i=4, t=PACK),
-                in_=raw[:].rearrange("p t (c i) -> p c t i", i=4),
+                out=rounded[:].rearrange("p (t m k) -> p m k t", t=PACK, k=PACK),
+                in_=raw[:].rearrange("p k (m t) -> p m k t", t=PACK),
             )
             return quantise(name, rounded, BANK)
 
@@ -94,9 +94,15 @@ def tile_list_ion_pulse_compensation_kernel(
         nc.vector.memset(warm[:], 0.0)
         warm2 = tile("warm2", [P, 8], F32)
         nc.scalar.activation(warm2[:], warm[:], ACT.Sin)
-        ident = tile("ident", [P, P], F32)
-        make_identity(nc, ident[:])
-        tab_sc = load_scales("tab_sc", tab_scales, T)
+        tab_sc = tile("tab_sc", [P, T], U8)
+        nc.vector.memset(tab_sc[:].bitcast(I32), 0)
+        for q in range(4):
+            nc.gpsimd.dma_start(
+                out=tab_sc[:].bitcast(I32)[32 * q : 32 * q + 8, :],
+                in_=tab_scales.bitcast(I32)[:, 4 * q : 4 * q + 4, :],
+            )
+        v_sc1 = tile("v_sc1", [P, S], U8)
+        nc.vector.memset(v_sc1[:].bitcast(I32), 0)
         wb_sc = load_scales("wb_sc", wb_scales, H)
         wc_sc = load_scales("wc_sc", wc_scales, N)
 
@@ -106,21 +112,21 @@ def tile_list_ion_pulse_compensation_kernel(
         planes[1] = load_plane(1)
         wp_raw[0] = load_raw("wp_raw0", wp, 0, 0)
         planes[2] = load_plane(2)
+        wth_raw[(0, 0)] = load_raw("wth_raw00", wth, 0, 0)
         planes[3] = load_plane(3)
+        wth_raw[(1, 0)] = load_raw("wth_raw10", wth, 1, 0)
         tab[0] = load_table(0)
         list1 = load_list("list1", offs)
-        wth_raw[(0, 0)] = load_raw("wth_raw00", wth, 0, 0)
         tab[1] = load_table(1)
-        wth_raw[(1, 0)] = load_raw("wth_raw10", wth, 1, 0)
         list3 = load_list("list3", offs3)
-        wp_raw[1] = load_raw("wp_raw1", wp, 0, 1)
-        wth_raw[(0, 1)] = load_raw("wth_raw01", wth, 0, 1)
-        wth_raw[(1, 1)] = load_raw("wth_raw11", wth, 1, 1)
         wb_w = tile("wb_w", [P, 2 * 2 * H], U8)
         nc.sync.dma_start(
             out=wb_w[:].bitcast(I32).rearrange("p (a c) -> p a c", a=2),
             in_=wb_words.bitcast(I32).rearrange("a p c -> p a c"),
         )
+        wp_raw[1] = load_raw("wp_raw1", wp, 0, 1)
+        wth_raw[(0, 1)] = load_raw("wth_raw01", wth, 0, 1)
+        wth_raw[(1, 1)] = load_raw("wth_raw11", wth, 1, 1)
         wc_w = tile("wc_w", [P, 2 * N], U32)
         nc.sync.dma_start(
             out=wc_w[:].bitcast(I32).rearrange("p (a c) -> p a c", a=2),
@@ -156,17 +162,20 @@ def tile_list_ion_pulse_compensation_kernel(
             )
             page_q.append(quantise("page%d" % h, rounded, BANK))
 
-        v_codes, v_scales = [], []
+        v_codes = []
 
         def gather_table(a):
             codes = tile("v_codes%d" % a, [P, S], U32)
             nc.vector.tensor_copy(codes[:], tab[a][:].indirect(list1[:]))
-            scales = tile("v_scales%d" % a, [P, S], U8)
-            nc.vector.tensor_copy(scales[:], tab_sc[:, T * a : T * (a + 1)].indirect(list1[:]))
             v_codes.append(codes)
-            v_scales.append(scales)
 
-        picked, a_rows = {}, {}
+        v_sc = tile("v_sc", [P, S], U8)
+
+        def gather_scales():
+            nc.vector.tensor_copy(v_sc[:], tab_sc[:].indirect(list1[:]))
+            nc.gpsimd.dma_start(out=v_sc1[:].bitcast(I32)[0 : P - 4, :], in_=v_sc[:].bitcast(I32)[4:P, :])
+
+        a_rows = {}
 
         def project(i):
             codes, scales = wp_q[i // 4]
@@ -182,145 +191,138 @@ def tile_list_ion_pulse_compensation_kernel(
                 nc.scalar.copy(out=rows[:, BANK * h : BANK * (h + 1)], in_=acc[:])
             a_rows[i] = rows
 
-        def pick(i):
-            picked[i] = tile("x%d" % i, [P, S], F32, tag="x", bufs=8)
-            nc.vector.tensor_copy(picked[i][:], a_rows[i][:].indirect(list3[:]))
+        wb_p = tile("wb_p", [P, 2 * 2 * H], U8)
+        wb_sp = tile("wb_sp", [P, 2 * H], U8)
 
-        def by_plane(acc):
-            return acc[:].rearrange("p (m t) -> p t m", t=PACK)
+        def order_wb():
+            nc.vector.tensor_copy(
+                out=wb_p[:].bitcast(U16).rearrange("p (b t m) -> p b t m", b=4, t=PACK),
+                in_=wb_w[:].bitcast(U16).rearrange("p (b m t) -> p b t m", b=4, t=PACK),
+            )
+            nc.vector.tensor_copy(
+                out=wb_sp[:].rearrange("p (b t m) -> p b t m", b=4, t=PACK),
+                in_=wb_sc[:].rearrange("p (b m t) -> p b t m", b=4, t=PACK),
+            )
 
-        cosines, sines, terms_b = {}, {}, {}
+        terms_x = [tile("term_x%d" % g, [P, PACK, S], F32) for g in range(2)]
+        terms_b = [tile("term_b%d" % g, [P, PACK, S], F32) for g in range(2)]
 
-        def angles(g, jt):
-            js = slice(P * jt, P * (jt + 1))
-            th = bank("th", "t", 2)
+        sines, cosines = {}, {}
+
+        def rotate(i):
+            g, t = divmod(i, PACK)
+            cols = slice(P * t, P * (t + 1))
+            th = bank("th", "th", 3)
             for a in range(2):
                 nc.tensor.matmul_mx(
-                    out=th[:], lhsT=v_codes[a][:, js].bitcast(FP8X4), lhsT_scale=v_scales[a][:, js],
-                    rhs=wth_q[(a, g)][0][:].bitcast(FP8X4), rhs_scale=wth_q[(a, g)][1][:],
+                    out=th[:], lhsT=wth_q[(a, g)][0][:, cols].bitcast(FP8X4), lhsT_scale=wth_q[(a, g)][1][:, cols],
+                    rhs=v_codes[a][:].bitcast(FP8X4), rhs_scale=v_sc[4 * a : P, :],
                     start=(a == 0), stop=(a == 1),
                 )
-            sine = tile("sine", [P, PACK, P], F32, bufs=8)
-            nc.scalar.activation(sine[:], by_plane(th), ACT.Sin)
-            size = tile("size", [P, PACK, P], F32, bufs=2)
-            nc.scalar.activation(size[:], by_plane(th), ACT.Abs)
-            cosine = tile("cosine", [P, PACK, P], F32, bufs=8)
+            size = tile("size", [P, S], F32, bufs=2)
+            nc.scalar.activation(size[:], th[:], ACT.Abs)
+            sine = tile("sine", [P, S], F32, bufs=5)
+            nc.scalar.activation(sine[:], th[:], ACT.Sin)
+            cosine = tile("cosine", [P, S], F32, bufs=5)
             nc.scalar.activation(cosine[:], size[:], ACT.Sin, bias=math.pi / 2, scale=-1.0)
-            cosines[(g, jt)], sines[(g, jt)] = cosine, sine
+            sines[i], cosines[i] = sine, cosine
 
-        def weigh_b(g, jt):
-            js = slice(P * jt, P * (jt + 1))
-            b = bank("b", "b", 1)
+        def weigh_b(i):
+            g, t = divmod(i, PACK)
+            b = bank("b", "b", 3)
             for a in range(2):
-                c0 = H * a + BANK * g
+                c0 = H * a + P * i
                 nc.tensor.matmul_mx(
-                    out=b[:], lhsT=v_codes[a][:, js].bitcast(FP8X4), lhsT_scale=v_scales[a][:, js],
-                    rhs=wb_w[:, 2 * c0 : 2 * (c0 + BANK)].bitcast(FP4X4), rhs_scale=wb_sc[:, c0 : c0 + BANK],
+                    out=b[:], lhsT=wb_p[:, 2 * c0 : 2 * (c0 + P)].bitcast(FP4X4), lhsT_scale=wb_sp[:, c0 : c0 + P],
+                    rhs=v_codes[a][:].bitcast(FP8X4), rhs_scale=(v_sc, v_sc1)[a][:],
                     start=(a == 0), stop=(a == 1),
                 )
-            terms_b[(g, jt)] = tile("term_b", [P, PACK, P], F32, bufs=3)
-            nc.vector.tensor_tensor(terms_b[(g, jt)][:], by_plane(b), sines[(g, jt)][:], MULT)
+            nc.vector.tensor_tensor(terms_b[g][:, t, :], b[:], sines[i][:], MULT)
 
-        z_q, terms_x = {}, {}
-
-        def combine(g, jt):
-            js = slice(P * jt, P * (jt + 1))
-            xt = bank("xt", "x", 1)
-            for q in range(4):
-                nc.tensor.transpose(xt[:, P * q : P * (q + 1)], picked[4 * g + q][:, js], ident[:])
-            term_x = tile("term_x", [P, PACK, P], F32, bufs=3)
-            nc.vector.tensor_tensor(term_x[:], by_plane(xt), cosines[(g, jt)][:], MULT)
-            terms_x[(g, jt)] = term_x
-
-        def add_terms(g, jt):
-            term_x = terms_x[(g, jt)]
-            z = bank("z", "z", 2)
-            for t in range(PACK):
-                for first, term in ((True, term_x), (False, terms_b[(g, jt)])):
-                    nc.tensor.matmul(
-                        out=z[:, P * t : P * (t + 1)], lhsT=term[:, t, :], rhs=ident[:],
-                        start=first, stop=not first, is_transpose=True,
-                    )
-            rounded = tile("z_bf", [P, PACK * P], BF16, bufs=2)
-            nc.scalar.copy(
-                out=rounded[:].rearrange("p (j t) -> p j t", t=PACK),
-                in_=z[:].rearrange("p (t j) -> p j t", t=PACK),
+        def weigh_x(i, j0=0, j1=S):
+            g, t = divmod(i, PACK)
+            nc.vector.tensor_tensor(
+                terms_x[g][:, t, j0:j1], a_rows[i][:].indirect(list3[:, j0 // 16 : j1 // 16]), cosines[i][:, j0:j1], MULT
             )
-            z_q[(g, jt)] = quantise("z%d%d" % (g, jt), rounded, P)
 
-        def control(jt):
-            acc = bank("out_acc", "wide", 2)
-            for nt in range(4):
-                for g in range(2):
-                    c0 = N * g + P * nt
-                    nc.tensor.matmul_mx(
-                        out=acc[:, P * nt : P * (nt + 1)],
-                        lhsT=wc_w[:, c0 : c0 + P].bitcast(FP8X4), lhsT_scale=wc_sc[:, c0 : c0 + P],
-                        rhs=z_q[(g, jt)][0][:].bitcast(FP8X4), rhs_scale=z_q[(g, jt)][1][:],
-                        start=(g == 0), stop=(g == 1),
-                    )
-            result = tile("result%d" % jt, [P, 4, P], F32, tag="x", bufs=8)
-            (nc.vector.tensor_copy if jt in (1, 3) else nc.scalar.copy)(out=result[:].rearrange("p n j -> p (n j)"), in_=acc[:])
-            nc.sync.dma_start(
-                out=out.rearrange("(n p) j -> p n j", p=P)[:, :, P * jt : P * (jt + 1)], in_=result[:]
+        z_q = {}
+        HALF = S // 2
+
+        def combine(g, h):
+            js = slice(HALF * h, HALF * (h + 1))
+            rounded = tile("z_bf", [P, PACK * HALF], BF16, bufs=2)
+            nc.vector.tensor_tensor(
+                rounded[:].rearrange("p (c i t) -> p c t i", i=4, t=PACK),
+                terms_x[g][:, :, js].rearrange("p t (c i) -> p c t i", i=4),
+                terms_b[g][:, :, js].rearrange("p t (c i) -> p c t i", i=4),
+                ADD,
             )
+            z_q[(g, h)] = quantise("z%d%d" % (g, h), rounded, HALF)
+
+        def control(h):
+            for pair in range(2):
+                acc = bank("out_acc", "th" if pair == 0 else "b", 3)
+                for k in range(2):
+                    for g in range(2):
+                        c0 = N * g + P * (2 * pair + k)
+                        nc.tensor.matmul_mx(
+                            out=acc[:, HALF * k : HALF * (k + 1)],
+                            lhsT=wc_w[:, c0 : c0 + P].bitcast(FP8X4), lhsT_scale=wc_sc[:, c0 : c0 + P],
+                            rhs=z_q[(g, h)][0][:].bitcast(FP8X4), rhs_scale=z_q[(g, h)][1][:],
+                            start=(g == 0), stop=(g == 1),
+                        )
+                result = tile("result%d%d" % (h, pair), [P, 2, HALF], F32, tag="new%d" % (2 * h + pair))
+                (nc.vector.tensor_copy if pair == 1 else nc.scalar.copy)(out=result[:].rearrange("p n j -> p (n j)"), in_=acc[:])
+                nc.sync.dma_start(
+                    out=out.rearrange("(n p) j -> p n j", p=P)[:, 2 * pair : 2 * pair + 2, HALF * h : HALF * (h + 1)],
+                    in_=result[:],
+                )
 
         merge(0)
         merge(1)
+        gather_scales()
         gather_table(0)
         gather_table(1)
+        order_wb()
         project(0)
         project(1)
+        rotate(0)
+        weigh_x(0)
+        weigh_b(0)
         project(2)
+        rotate(1)
+        weigh_x(1)
+        weigh_b(1)
+        wp_q[1] = round_weights("wp1", wp_raw[1], nc.scalar.copy)
         project(3)
-        wp_q[1] = round_weights("wp1", wp_raw[1], nc.vector.tensor_copy)
-        angles(0, 0)
-        wth_q[(0, 1)] = round_weights("wth01", wth_raw[(0, 1)], nc.vector.tensor_copy)
-        angles(0, 1)
+        rotate(2)
+        weigh_x(2)
+        weigh_b(2)
+        wth_q[(0, 1)] = round_weights("wth01", wth_raw[(0, 1)], nc.scalar.copy)
+        rotate(3)
+        weigh_x(3)
+        weigh_b(3)
         wth_q[(1, 1)] = round_weights("wth11", wth_raw[(1, 1)], nc.vector.tensor_copy)
-        pick(0)
-        pick(1)
-        pick(2)
-        pick(3)
-        angles(0, 2)
-        angles(0, 3)
         project(4)
-        project(5)
-        project(6)
-        project(7)
-        weigh_b(0, 0)
+        rotate(4)
         combine(0, 0)
-        weigh_b(0, 1)
+        weigh_x(4)
+        weigh_b(4)
+        project(5)
+        rotate(5)
         combine(0, 1)
-        add_terms(0, 0)
-        angles(1, 0)
-        pick(4)
-        weigh_b(0, 2)
-        combine(0, 2)
-        add_terms(0, 1)
-        angles(1, 1)
-        pick(5)
-        weigh_b(0, 3)
-        combine(0, 3)
-        add_terms(0, 2)
-        angles(1, 2)
-        pick(6)
-        add_terms(0, 3)
-        angles(1, 3)
-        pick(7)
-        weigh_b(1, 0)
+        weigh_x(5)
+        weigh_b(5)
+        project(6)
+        rotate(6)
+        weigh_x(6)
+        weigh_b(6)
+        project(7)
+        rotate(7)
+        weigh_b(7)
+        weigh_x(7, 0, HALF)
         combine(1, 0)
-        weigh_b(1, 1)
+        weigh_x(7, HALF, S)
         combine(1, 1)
-        add_terms(1, 0)
-        weigh_b(1, 2)
-        combine(1, 2)
-        add_terms(1, 1)
         control(0)
-        weigh_b(1, 3)
-        combine(1, 3)
-        add_terms(1, 2)
         control(1)
-        add_terms(1, 3)
-        control(2)
-        control(3)

@@ -83,7 +83,7 @@ def tile_list_ion_pulse_compensation_kernel(
             return codes, scales
 
         def round_weights(name, raw, copy):
-            rounded = tile(name + "_bf", [P, PACK * BANK], BF16, tag="rounded", bufs=4)
+            rounded = tile(name + "_bf", [P, PACK * BANK], BF16, tag={"wth01": "page_bf1", "wth11": "page_bf1"}.get(name))
             copy(
                 out=rounded[:].rearrange("p (t m k) -> p m k t", t=PACK, k=PACK),
                 in_=raw[:].rearrange("p k (m t) -> p m k t", t=PACK),
@@ -110,13 +110,13 @@ def tile_list_ion_pulse_compensation_kernel(
         list2 = load_list("list2", offs2)
         planes[0] = load_plane(0)
         planes[1] = load_plane(1)
+        list1 = load_list("list1", offs)
         wp_raw[0] = load_raw("wp_raw0", wp, 0, 0)
         planes[2] = load_plane(2)
         wth_raw[(0, 0)] = load_raw("wth_raw00", wth, 0, 0)
         planes[3] = load_plane(3)
         wth_raw[(1, 0)] = load_raw("wth_raw10", wth, 1, 0)
         tab[0] = load_table(0)
-        list1 = load_list("list1", offs)
         tab[1] = load_table(1)
         list3 = load_list("list3", offs3)
         wb_w = tile("wb_w", [P, 2 * 2 * H], U8)
@@ -155,7 +155,7 @@ def tile_list_ion_pulse_compensation_kernel(
         page_q = []
 
         def merge(h):
-            rounded = tile("page_bf%d" % h, [P, PACK * BANK], BF16, tag="rounded", bufs=4)
+            rounded = tile("page_bf%d" % h, [P, PACK * BANK], BF16)
             nc.vector.tensor_copy(
                 out=rounded[:].bitcast(I32).rearrange("p (c u) -> p c u", u=2),
                 in_=pairs[h][:].rearrange("p u c e -> p u (c e)").bitcast(I32).rearrange("p u c -> p c u"),
@@ -165,15 +165,15 @@ def tile_list_ion_pulse_compensation_kernel(
         v_codes = []
 
         def gather_table(a):
-            codes = tile("v_codes%d" % a, [P, S], U32)
+            codes = tile("v_codes%d" % a, [P, S], U32, tag="pairs%d" % a)
             nc.vector.tensor_copy(codes[:], tab[a][:].indirect(list1[:]))
             v_codes.append(codes)
 
-        v_sc = tile("v_sc", [P, S], U8)
-
         def gather_scales():
+            v_sc = tile("v_sc", [P, S], U8, tag="wp0_bf")
             nc.vector.tensor_copy(v_sc[:], tab_sc[:].indirect(list1[:]))
             nc.gpsimd.dma_start(out=v_sc1[:].bitcast(I32)[0 : P - 4, :], in_=v_sc[:].bitcast(I32)[4:P, :])
+            return v_sc
 
         a_rows = {}
 
@@ -191,10 +191,9 @@ def tile_list_ion_pulse_compensation_kernel(
                 nc.scalar.copy(out=rows[:, BANK * h : BANK * (h + 1)], in_=acc[:])
             a_rows[i] = rows
 
-        wb_p = tile("wb_p", [P, 2 * 2 * H], U8)
-        wb_sp = tile("wb_sp", [P, 2 * H], U8)
-
         def order_wb():
+            wb_p = tile("wb_p", [P, 2 * 2 * H], U8, tag="page_bf0")
+            wb_sp = tile("wb_sp", [P, 2 * H], U8, tag="wth00_bf")
             nc.vector.tensor_copy(
                 out=wb_p[:].bitcast(U16).rearrange("p (b t m) -> p b t m", b=4, t=PACK),
                 in_=wb_w[:].bitcast(U16).rearrange("p (b m t) -> p b t m", b=4, t=PACK),
@@ -203,6 +202,7 @@ def tile_list_ion_pulse_compensation_kernel(
                 out=wb_sp[:].rearrange("p (b t m) -> p b t m", b=4, t=PACK),
                 in_=wb_sc[:].rearrange("p (b m t) -> p b t m", b=4, t=PACK),
             )
+            return wb_p, wb_sp
 
         terms_x = [tile("term_x%d" % g, [P, PACK, S], F32) for g in range(2)]
         terms_b = [tile("term_b%d" % g, [P, PACK, S], F32) for g in range(2)]
@@ -220,11 +220,14 @@ def tile_list_ion_pulse_compensation_kernel(
                     start=(a == 0), stop=(a == 1),
                 )
             size = tile("size", [P, S], F32, bufs=2)
-            nc.scalar.activation(size[:], th[:], ACT.Abs)
             sine = tile("sine", [P, S], F32, bufs=5)
-            nc.scalar.activation(sine[:], th[:], ACT.Sin)
             cosine = tile("cosine", [P, S], F32, bufs=5)
-            nc.scalar.activation(cosine[:], size[:], ACT.Sin, bias=math.pi / 2, scale=-1.0)
+            nc.scalar.activation(sine[:], th[:], ACT.Sin)
+            width = S // 2 if i == 7 else S
+            for j0 in range(0, S, width):
+                js = slice(j0, j0 + width)
+                nc.scalar.activation(size[:, js], th[:, js], ACT.Abs)
+                nc.scalar.activation(cosine[:, js], size[:, js], ACT.Sin, bias=math.pi / 2, scale=-1.0)
             sines[i], cosines[i] = sine, cosine
 
         def weigh_b(i):
@@ -278,31 +281,31 @@ def tile_list_ion_pulse_compensation_kernel(
                     in_=result[:],
                 )
 
+        v_sc = gather_scales()
         merge(0)
         merge(1)
-        gather_scales()
         gather_table(0)
         gather_table(1)
-        order_wb()
+        wb_p, wb_sp = order_wb()
         project(0)
         project(1)
         rotate(0)
+        wp_q[1] = round_weights("wp1", wp_raw[1], nc.scalar.copy)
         weigh_x(0)
         weigh_b(0)
         project(2)
         rotate(1)
+        wth_q[(0, 1)] = round_weights("wth01", wth_raw[(0, 1)], nc.vector.tensor_copy)
         weigh_x(1)
         weigh_b(1)
-        wp_q[1] = round_weights("wp1", wp_raw[1], nc.scalar.copy)
         project(3)
         rotate(2)
+        wth_q[(1, 1)] = round_weights("wth11", wth_raw[(1, 1)], nc.vector.tensor_copy)
         weigh_x(2)
         weigh_b(2)
-        wth_q[(0, 1)] = round_weights("wth01", wth_raw[(0, 1)], nc.scalar.copy)
         rotate(3)
         weigh_x(3)
         weigh_b(3)
-        wth_q[(1, 1)] = round_weights("wth11", wth_raw[(1, 1)], nc.vector.tensor_copy)
         project(4)
         rotate(4)
         combine(0, 0)

@@ -15,11 +15,22 @@ ACT = mybir.ActivationFunctionType
 MULT = mybir.AluOpType.mult
 ADD = mybir.AluOpType.add
 
-P = 128
-PACK = 4
-BANK = 512
 K, K2, H, N, T, T2, S = 1024, 512, 1024, 512, 2048, 1024, 512
 FLOPS = 2 * (K2 * H * T2 + 2 * K * H * S + H * N * S)
+
+P = 128
+PACK = 4
+PASS = P * PACK
+BANK = 512
+HALF = S // 2
+QUADRANTS = 4
+SHIFT_ROWS = 112
+
+RAW_BUFS = 3
+ROW_BUFS = 7
+TRIG_BUFS = 5
+SHARED_BANKS = 5
+B_BANKS = 3
 
 
 def tile_list_ion_pulse_compensation_kernel(
@@ -39,32 +50,35 @@ def tile_list_ion_pulse_compensation_kernel(
             return ps.tile([P, BANK], F32, name=name, tag=tag, bufs=bufs)
 
         def load_list(name, src):
-            t = lists.tile([P, S // 16], U16, name=name, tag=name)
-            nc.sync.dma_start(t[:], src)
-            return t
+            offsets = lists.tile([P, S // 16], U16, name=name, tag=name)
+            nc.sync.dma_start(offsets[:], src)
+            return offsets
 
-        def load_scales(name, src, width):
-            t = tile(name, [P, 2 * width], U8)
-            words = t[:].bitcast(I32)
-            nc.vector.memset(words, 0)
-            rows = src.bitcast(I32)
-            for q in range(4):
+        def zeroed(name, width):
+            scales = tile(name, [P, width], U8)
+            nc.vector.memset(scales[:].bitcast(I32), 0)
+            return scales
+
+        def load_scales(scales, src):
+            for q in range(QUADRANTS):
                 nc.gpsimd.dma_start(
-                    out=words[32 * q : 32 * q + 4, :].rearrange("p (a c) -> p a c", a=2),
-                    in_=rows[:, 4 * q : 4 * q + 4, :].rearrange("a q c -> q a c"),
+                    out=scales[:].bitcast(I32)[32 * q : 32 * q + 4, :].rearrange("p (a c) -> p a c", a=2),
+                    in_=src.bitcast(I32)[:, 4 * q : 4 * q + 4, :].rearrange("a q c -> q a c"),
                 )
-            return t
 
         def load_plane(t):
-            page = tile("page%d" % t, [P, T2], F32, tag="a", bufs=8)
-            new = tile("new%d" % t, [P, S], F32, tag="new%d" % t)
+            if t == PACK - 1:
+                page = tile("last_plane", [P, T2], F32)
+            else:
+                page = tile("page%d" % t, [P, T2], F32, tag="rows", bufs=ROW_BUFS)
+            new = tile("new%d" % t, [P, S], F32)
             nc.sync.dma_start(out=page[:], in_=base.rearrange("(p t) c -> p t c", t=PACK)[:, t, :])
             nc.sync.dma_start(out=new[:], in_=xs.rearrange("(p t) c -> p t c", t=PACK)[:, t, :])
             return page, new
 
         def load_raw(name, src, a, g):
-            raw = tile(name, [P, PACK, BANK], F32, tag="raw", bufs=4)
-            rows = src[BANK * a : BANK * (a + 1), BANK * g : BANK * (g + 1)]
+            raw = tile(name, [P, PACK, PASS], F32, tag="raw", bufs=RAW_BUFS)
+            rows = src[PASS * a : PASS * (a + 1), PASS * g : PASS * (g + 1)]
             nc.sync.dma_start(out=raw[:], in_=rows.rearrange("(p t) c -> p t c", t=PACK))
             return raw
 
@@ -76,195 +90,178 @@ def tile_list_ion_pulse_compensation_kernel(
             )
             return words
 
-        def quantise(name, rounded, width):
-            codes = tile(name + "_codes", [P, width], U32, tag={"wp0": "new3"}.get(name))
-            scales = tile(name + "_scales", [P, width], U8)
-            nc.vector.quantize_mx(out=codes[:].bitcast(FP8X4), scales=scales[:], in_=rounded[:])
-            return codes, scales
+        angle_zero = tile("angle_zero", [P, 8], F32)
+        nc.vector.memset(angle_zero[:], 0.0)
+        zero = tile("zero", [P, 8], F32)
+        nc.scalar.activation(zero[:], angle_zero[:], ACT.Sin)
 
-        def round_weights(name, raw, copy):
-            rounded = tile(name + "_bf", [P, PACK * BANK], BF16, tag={"wth01": "page_bf1", "wth11": "page_bf1"}.get(name))
-            copy(
-                out=rounded[:].rearrange("p (t m k) -> p m k t", t=PACK, k=PACK),
-                in_=raw[:].rearrange("p k (m t) -> p m k t", t=PACK),
-            )
-            return quantise(name, rounded, BANK)
-
-        warm = tile("warm", [P, 8], F32)
-        nc.vector.memset(warm[:], 0.0)
-        warm2 = tile("warm2", [P, 8], F32)
-        nc.scalar.activation(warm2[:], warm[:], ACT.Sin)
-        tab_sc = tile("tab_sc", [P, T], U8)
-        nc.vector.memset(tab_sc[:].bitcast(I32), 0)
-        for q in range(4):
+        tab_sc = zeroed("tab_sc", T)
+        wb_sc = zeroed("wb_sc", 2 * H)
+        v_sc_second = zeroed("v_sc_second", S)
+        wc_sc = zeroed("wc_sc", 2 * N)
+        for q in range(QUADRANTS):
             nc.gpsimd.dma_start(
                 out=tab_sc[:].bitcast(I32)[32 * q : 32 * q + 8, :],
                 in_=tab_scales.bitcast(I32)[:, 4 * q : 4 * q + 4, :],
             )
-        v_sc1 = tile("v_sc1", [P, S], U8)
-        nc.vector.memset(v_sc1[:].bitcast(I32), 0)
-        wb_sc = load_scales("wb_sc", wb_scales, H)
-        wc_sc = load_scales("wc_sc", wc_scales, N)
+        load_scales(wb_sc, wb_scales)
+        load_scales(wc_sc, wc_scales)
 
-        planes, tab, wp_raw, wth_raw, wp_q, wth_q = {}, {}, {}, {}, {}, {}
         list2 = load_list("list2", offs2)
-        planes[0] = load_plane(0)
-        planes[1] = load_plane(1)
+        planes = [load_plane(0), load_plane(1)]
+        wp_raw = [load_raw("wp_raw0", wp, 0, 0)]
         list1 = load_list("list1", offs)
-        wp_raw[0] = load_raw("wp_raw0", wp, 0, 0)
-        planes[2] = load_plane(2)
-        wth_raw[(0, 0)] = load_raw("wth_raw00", wth, 0, 0)
-        planes[3] = load_plane(3)
+        planes.append(load_plane(2))
+        wth_raw = {(0, 0): load_raw("wth_raw00", wth, 0, 0)}
+        planes.append(load_plane(3))
         wth_raw[(1, 0)] = load_raw("wth_raw10", wth, 1, 0)
-        tab[0] = load_table(0)
-        tab[1] = load_table(1)
+        tab = [load_table(a) for a in range(2)]
         list3 = load_list("list3", offs3)
+        wp_raw.append(load_raw("wp_raw1", wp, 0, 1))
         wb_w = tile("wb_w", [P, 2 * 2 * H], U8)
         nc.sync.dma_start(
             out=wb_w[:].bitcast(I32).rearrange("p (a c) -> p a c", a=2),
             in_=wb_words.bitcast(I32).rearrange("a p c -> p a c"),
         )
-        wp_raw[1] = load_raw("wp_raw1", wp, 0, 1)
-        wth_raw[(0, 1)] = load_raw("wth_raw01", wth, 0, 1)
-        wth_raw[(1, 1)] = load_raw("wth_raw11", wth, 1, 1)
+        for a in range(2):
+            wth_raw[(a, 1)] = load_raw("wth_raw%d1" % a, wth, a, 1)
         wc_w = tile("wc_w", [P, 2 * N], U32)
         nc.sync.dma_start(
             out=wc_w[:].bitcast(I32).rearrange("p (a c) -> p a c", a=2),
             in_=wc_words.rearrange("a p c i -> p a (c i)").bitcast(I32),
         )
 
-        def pool_copy(out, in_):
-            nc.gpsimd.tensor_scalar(out, in_, 1.0, 0.0, MULT, mybir.AluOpType.add)
+        def quantise(name, rounded, width, codes_tag=None):
+            codes = tile(name + "_codes", [P, width], U32, tag=codes_tag)
+            scales = tile(name + "_scales", [P, width], U8)
+            nc.vector.quantize_mx(out=codes[:].bitcast(FP8X4), scales=scales[:], in_=rounded[:])
+            return codes, scales
+
+        def round_weights(name, raw, copy, rounded_tag=None, codes_tag=None):
+            rounded = tile(name + "_bf", [P, PACK * PASS], BF16, tag=rounded_tag)
+            copy(
+                out=rounded[:].rearrange("p (t m k) -> p m k t", t=PACK, k=PACK),
+                in_=raw[:].rearrange("p k (m t) -> p m k t", t=PACK),
+            )
+            return quantise(name, rounded, PASS, codes_tag)
 
         pairs = [tile("pairs%d" % h, [P, 2, BANK, 2], BF16) for h in range(2)]
 
-        def scatter_plane(t):
-            page, new = planes[t]
+        wp_q = [round_weights("wp0", wp_raw[0], nc.scalar.copy, codes_tag="new3")]
+        wth_q = {(0, 0): round_weights("wth00", wth_raw[(0, 0)], nc.scalar.copy, codes_tag="wp0_bf")}
+        for t, (page, new) in enumerate(planes):
             nc.vector.tensor_copy(page[:].indirect(list2[:]), new[:])
             for h in range(2):
                 nc.scalar.copy(out=pairs[h][:, t // 2, :, t % 2], in_=page[:, BANK * h : BANK * (h + 1)])
-
-        scatter_plane(0)
-        wp_q[0] = round_weights("wp0", wp_raw[0], nc.scalar.copy)
-        scatter_plane(1)
-        wth_q[(0, 0)] = round_weights("wth00", wth_raw[(0, 0)], nc.scalar.copy)
-        scatter_plane(2)
-        scatter_plane(3)
-        wth_q[(1, 0)] = round_weights("wth10", wth_raw[(1, 0)], nc.scalar.copy)
+        wth_q[(1, 0)] = round_weights("wth10", wth_raw[(1, 0)], nc.scalar.copy, rounded_tag="last_plane")
 
         page_q = []
-
-        def merge(h):
-            rounded = tile("page_bf%d" % h, [P, PACK * BANK], BF16)
+        for h in range(2):
+            page_bf = tile("page_bf%d" % h, [P, PACK * BANK], BF16)
             nc.vector.tensor_copy(
-                out=rounded[:].bitcast(I32).rearrange("p (c u) -> p c u", u=2),
+                out=page_bf[:].bitcast(I32).rearrange("p (c u) -> p c u", u=2),
                 in_=pairs[h][:].rearrange("p u c e -> p u (c e)").bitcast(I32).rearrange("p u c -> p c u"),
             )
-            page_q.append(quantise("page%d" % h, rounded, BANK))
+            page_q.append(quantise("page%d" % h, page_bf, BANK))
 
+        v_sc = tile("v_sc", [P, S], U8, tag="new2")
+        nc.vector.tensor_copy(v_sc[:], tab_sc[:].indirect(list1[:]))
+        nc.gpsimd.dma_start(
+            out=v_sc_second[:].bitcast(I32)[0:SHIFT_ROWS, :], in_=v_sc[:].bitcast(I32)[4 : 4 + SHIFT_ROWS, :]
+        )
         v_codes = []
-
-        def gather_table(a):
+        for a in range(2):
             codes = tile("v_codes%d" % a, [P, S], U32, tag="pairs%d" % a)
             nc.vector.tensor_copy(codes[:], tab[a][:].indirect(list1[:]))
             v_codes.append(codes)
 
-        def gather_scales():
-            v_sc = tile("v_sc", [P, S], U8, tag="wp0_bf")
-            nc.vector.tensor_copy(v_sc[:], tab_sc[:].indirect(list1[:]))
-            nc.gpsimd.dma_start(out=v_sc1[:].bitcast(I32)[0 : P - 4, :], in_=v_sc[:].bitcast(I32)[4:P, :])
-            return v_sc
+        wb_sc_ordered = tile("wb_sc_ordered", [P, 2 * H], U8, tag="wth00_bf")
+        nc.vector.tensor_copy(
+            out=wb_sc_ordered[:].rearrange("p (b t m) -> p b t m", b=4, t=PACK),
+            in_=wb_sc[:].rearrange("p (b m t) -> p b t m", b=4, t=PACK),
+        )
+        wb_ordered = tile("wb_ordered", [P, 2 * 2 * H], U8, tag="tab0")
+        nc.vector.tensor_copy(
+            out=wb_ordered[:].bitcast(U16).rearrange("p (b t m) -> p b t m", b=4, t=PACK),
+            in_=wb_w[:].bitcast(U16).rearrange("p (b m t) -> p b t m", b=4, t=PACK),
+        )
+        wp_q.append(round_weights("wp1", wp_raw[1], nc.vector.tensor_copy))
 
-        a_rows = {}
+        a_rows, sines, sizes, z_q = {}, {}, {}, {}
+        terms_x = [tile("term_x%d" % g, [P, PACK, S], F32) for g in range(2)]
+        first_b = tile("term_b0", [P, PACK, S], F32)
+        terms_b = {(1, h): tile("term_b1%d" % h, [P, PACK, HALF], F32)[:] for h in range(2)}
+        terms_b.update({(0, h): first_b[:, :, HALF * h : HALF * (h + 1)] for h in range(2)})
 
         def project(i):
-            codes, scales = wp_q[i // 4]
-            cols = slice(P * (i % 4), P * (i % 4 + 1))
-            rows = tile("a%d" % i, [P, T2], F32, tag="a", bufs=8)
+            codes, scales = wp_q[i // PACK]
+            cols = slice(P * (i % PACK), P * (i % PACK + 1))
+            a_rows[i] = tile("a%d" % i, [P, T2], F32, tag="rows", bufs=ROW_BUFS)
             for h in range(2):
-                acc = bank("a_acc", "wide", 2)
+                acc = bank("a_acc", "shared", SHARED_BANKS)
                 nc.tensor.matmul_mx(
                     out=acc[:], lhsT=codes[:, cols].bitcast(FP8X4), lhsT_scale=scales[:, cols],
                     rhs=page_q[h][0][:].bitcast(FP8X4), rhs_scale=page_q[h][1][:],
                     start=True, stop=True,
                 )
-                nc.scalar.copy(out=rows[:, BANK * h : BANK * (h + 1)], in_=acc[:])
-            a_rows[i] = rows
+                nc.scalar.copy(out=a_rows[i][:, BANK * h : BANK * (h + 1)], in_=acc[:])
 
-        def order_wb():
-            wb_p = tile("wb_p", [P, 2 * 2 * H], U8, tag="page_bf0")
-            wb_sp = tile("wb_sp", [P, 2 * H], U8, tag="wth00_bf")
-            nc.vector.tensor_copy(
-                out=wb_p[:].bitcast(U16).rearrange("p (b t m) -> p b t m", b=4, t=PACK),
-                in_=wb_w[:].bitcast(U16).rearrange("p (b m t) -> p b t m", b=4, t=PACK),
-            )
-            nc.vector.tensor_copy(
-                out=wb_sp[:].rearrange("p (b t m) -> p b t m", b=4, t=PACK),
-                in_=wb_sc[:].rearrange("p (b m t) -> p b t m", b=4, t=PACK),
-            )
-            return wb_p, wb_sp
-
-        terms_x = [tile("term_x%d" % g, [P, PACK, S], F32) for g in range(2)]
-        terms_b = [tile("term_b%d" % g, [P, PACK, S], F32) for g in range(2)]
-
-        sines, cosines = {}, {}
-
-        def rotate(i):
+        def angles(i):
             g, t = divmod(i, PACK)
             cols = slice(P * t, P * (t + 1))
-            th = bank("th", "th", 3)
+            th = bank("th", "shared", SHARED_BANKS)
             for a in range(2):
+                codes, scales = wth_q[(a, g)]
                 nc.tensor.matmul_mx(
-                    out=th[:], lhsT=wth_q[(a, g)][0][:, cols].bitcast(FP8X4), lhsT_scale=wth_q[(a, g)][1][:, cols],
+                    out=th[:], lhsT=codes[:, cols].bitcast(FP8X4), lhsT_scale=scales[:, cols],
                     rhs=v_codes[a][:].bitcast(FP8X4), rhs_scale=v_sc[4 * a : P, :],
                     start=(a == 0), stop=(a == 1),
                 )
-            size = tile("size", [P, S], F32, bufs=2)
-            sine = tile("sine", [P, S], F32, bufs=5)
-            cosine = tile("cosine", [P, S], F32, bufs=5)
-            nc.scalar.activation(sine[:], th[:], ACT.Sin)
-            width = S // 2 if i == 7 else S
-            for j0 in range(0, S, width):
-                js = slice(j0, j0 + width)
-                nc.scalar.activation(size[:, js], th[:, js], ACT.Abs)
-                nc.scalar.activation(cosine[:, js], size[:, js], ACT.Sin, bias=math.pi / 2, scale=-1.0)
-            sines[i], cosines[i] = sine, cosine
+            sizes[i] = tile("size", [P, S], F32, bufs=2)
+            sines[i] = tile("sine", [P, S], F32, bufs=TRIG_BUFS)
+            nc.scalar.activation(sines[i][:], th[:], ACT.Sin)
+            nc.scalar.activation(sizes[i][:], th[:], ACT.Abs, bias=zero[:, 0:1])
+
+        def weigh_x(i, j0, j1, tag="cosine", bufs=TRIG_BUFS):
+            g, t = divmod(i, PACK)
+            cosine = tile("cosine", [P, j1 - j0], F32, tag=tag, bufs=bufs)
+            nc.scalar.activation(cosine[:], sizes[i][:, j0:j1], ACT.Sin, bias=math.pi / 2, scale=-1.0)
+            nc.vector.tensor_tensor(
+                terms_x[g][:, t, j0:j1], a_rows[i][:].indirect(list3[:, j0 // 16 : j1 // 16]), cosine[:], MULT
+            )
 
         def weigh_b(i):
             g, t = divmod(i, PACK)
-            b = bank("b", "b", 3)
+            b = bank("b", "b", B_BANKS)
             for a in range(2):
                 c0 = H * a + P * i
                 nc.tensor.matmul_mx(
-                    out=b[:], lhsT=wb_p[:, 2 * c0 : 2 * (c0 + P)].bitcast(FP4X4), lhsT_scale=wb_sp[:, c0 : c0 + P],
-                    rhs=v_codes[a][:].bitcast(FP8X4), rhs_scale=(v_sc, v_sc1)[a][:],
+                    out=b[:],
+                    lhsT=wb_ordered[:, 2 * c0 : 2 * (c0 + P)].bitcast(FP4X4),
+                    lhsT_scale=wb_sc_ordered[:, c0 : c0 + P],
+                    rhs=v_codes[a][:].bitcast(FP8X4), rhs_scale=(v_sc, v_sc_second)[a][:],
                     start=(a == 0), stop=(a == 1),
                 )
-            nc.vector.tensor_tensor(terms_b[g][:, t, :], b[:], sines[i][:], MULT)
-
-        def weigh_x(i, j0=0, j1=S):
-            g, t = divmod(i, PACK)
-            nc.vector.tensor_tensor(
-                terms_x[g][:, t, j0:j1], a_rows[i][:].indirect(list3[:, j0 // 16 : j1 // 16]), cosines[i][:, j0:j1], MULT
-            )
-
-        z_q = {}
-        HALF = S // 2
+            if g == 0:
+                nc.vector.tensor_tensor(first_b[:, t, :], b[:], sines[i][:], MULT)
+            else:
+                for h in range(2):
+                    js = slice(HALF * h, HALF * (h + 1))
+                    nc.vector.tensor_tensor(terms_b[(g, h)][:, t, :], b[:, js], sines[i][:, js], MULT)
 
         def combine(g, h):
-            js = slice(HALF * h, HALF * (h + 1))
-            rounded = tile("z_bf", [P, PACK * HALF], BF16, bufs=2)
+            z_bf = tile("z_bf", [P, PACK * HALF], BF16, bufs=2)
             nc.vector.tensor_tensor(
-                rounded[:].rearrange("p (c i t) -> p c t i", i=4, t=PACK),
-                terms_x[g][:, :, js].rearrange("p t (c i) -> p c t i", i=4),
-                terms_b[g][:, :, js].rearrange("p t (c i) -> p c t i", i=4),
+                z_bf[:].rearrange("p (c i t) -> p c t i", i=4, t=PACK),
+                terms_x[g][:, :, HALF * h : HALF * (h + 1)].rearrange("p t (c i) -> p c t i", i=4),
+                terms_b[(g, h)].rearrange("p t (c i) -> p c t i", i=4),
                 ADD,
             )
-            z_q[(g, h)] = quantise("z%d%d" % (g, h), rounded, HALF)
+            z_q[(g, h)] = quantise("z%d%d" % (g, h), z_bf, HALF)
 
         def control(h):
             for pair in range(2):
-                acc = bank("out_acc", "th" if pair == 0 else "b", 3)
+                acc = bank("out_acc", "shared", SHARED_BANKS)
                 for k in range(2):
                     for g in range(2):
                         c0 = N * g + P * (2 * pair + k)
@@ -274,58 +271,41 @@ def tile_list_ion_pulse_compensation_kernel(
                             rhs=z_q[(g, h)][0][:].bitcast(FP8X4), rhs_scale=z_q[(g, h)][1][:],
                             start=(g == 0), stop=(g == 1),
                         )
-                result = tile("result%d%d" % (h, pair), [P, 2, HALF], F32, tag="new%d" % (2 * h + pair))
-                (nc.vector.tensor_copy if pair == 1 else nc.scalar.copy)(out=result[:].rearrange("p n j -> p (n j)"), in_=acc[:])
+                result = tile("result%d%d" % (h, pair), [P, 2, HALF], F32)
+                copy = nc.vector.tensor_copy if (h, pair) == (1, 1) else nc.scalar.copy
+                copy(out=result[:].rearrange("p n j -> p (n j)"), in_=acc[:])
                 nc.sync.dma_start(
                     out=out.rearrange("(n p) j -> p n j", p=P)[:, 2 * pair : 2 * pair + 2, HALF * h : HALF * (h + 1)],
                     in_=result[:],
                 )
 
-        v_sc = gather_scales()
-        merge(0)
-        merge(1)
-        gather_table(0)
-        gather_table(1)
-        wb_p, wb_sp = order_wb()
+        late_copies = (nc.scalar.copy, nc.vector.tensor_copy)
         project(0)
-        project(1)
-        rotate(0)
-        wp_q[1] = round_weights("wp1", wp_raw[1], nc.scalar.copy)
-        weigh_x(0)
-        weigh_b(0)
-        project(2)
-        rotate(1)
-        wth_q[(0, 1)] = round_weights("wth01", wth_raw[(0, 1)], nc.vector.tensor_copy)
-        weigh_x(1)
-        weigh_b(1)
-        project(3)
-        rotate(2)
-        wth_q[(1, 1)] = round_weights("wth11", wth_raw[(1, 1)], nc.vector.tensor_copy)
-        weigh_x(2)
-        weigh_b(2)
-        rotate(3)
-        weigh_x(3)
-        weigh_b(3)
-        project(4)
-        rotate(4)
-        combine(0, 0)
-        weigh_x(4)
-        weigh_b(4)
-        project(5)
-        rotate(5)
-        combine(0, 1)
-        weigh_x(5)
-        weigh_b(5)
-        project(6)
-        rotate(6)
-        weigh_x(6)
-        weigh_b(6)
-        project(7)
-        rotate(7)
-        weigh_b(7)
-        weigh_x(7, 0, HALF)
+        for t in range(PACK):
+            if t + 1 < PACK:
+                project(t + 1)
+            angles(t)
+            weigh_x(t, 0, S)
+            if t >= 2:
+                a = t - 2
+                wth_q[(a, 1)] = round_weights(
+                    "wth%d1" % a, wth_raw[(a, 1)], late_copies[a], rounded_tag="page_bf%d" % (1 - a)
+                )
+            weigh_b(t)
+        for t in range(PACK - 1):
+            project(PACK + t)
+            angles(PACK + t)
+            weigh_x(PACK + t, 0, S)
+            if t < 2:
+                combine(0, t)
+            weigh_b(PACK + t)
+        last = 2 * PACK - 1
+        project(last)
+        angles(last)
+        weigh_b(last)
+        weigh_x(last, 0, HALF)
         combine(1, 0)
-        weigh_x(7, HALF, S)
+        weigh_x(last, HALF, S, tag="term_b10", bufs=1)
         combine(1, 1)
-        control(0)
-        control(1)
+        for h in range(2):
+            control(h)

@@ -26,10 +26,10 @@ HALF = S // 2
 QUADRANTS = 4
 SHIFT_ROWS = 112
 
-RAW_BUFS = 3
 ROW_BUFS = 7
-TRIG_BUFS = 5
-SHARED_BANKS = 5
+TRIG_BUFS = 4
+A_BANKS = 3
+TH_BANKS = 2
 B_BANKS = 3
 
 
@@ -54,31 +54,30 @@ def tile_list_ion_pulse_compensation_kernel(
             nc.sync.dma_start(offsets[:], src)
             return offsets
 
-        def zeroed(name, width):
+        def zeroed(name, width, engine=nc.vector):
             scales = tile(name, [P, width], U8)
-            nc.vector.memset(scales[:].bitcast(I32), 0)
+            engine.memset(scales[:].bitcast(I32), 0)
             return scales
 
-        def load_scales(scales, src):
+        def load_scales(queue, scales, src):
             for q in range(QUADRANTS):
-                nc.gpsimd.dma_start(
+                queue.dma_start(
                     out=scales[:].bitcast(I32)[32 * q : 32 * q + 4, :].rearrange("p (a c) -> p a c", a=2),
                     in_=src.bitcast(I32)[:, 4 * q : 4 * q + 4, :].rearrange("a q c -> q a c"),
                 )
 
-        def load_plane(t):
-            if t == PACK - 1:
-                page = tile("last_plane", [P, T2], F32)
-            else:
-                page = tile("page%d" % t, [P, T2], F32, tag="rows", bufs=ROW_BUFS)
+        def load_plane(t, between=None):
+            page = tile("page%d" % t, [P, T2], F32, tag="rows", bufs=ROW_BUFS)
             new = tile("new%d" % t, [P, S], F32)
             nc.sync.dma_start(out=page[:], in_=base.rearrange("(p t) c -> p t c", t=PACK)[:, t, :])
+            if between:
+                between()
             nc.sync.dma_start(out=new[:], in_=xs.rearrange("(p t) c -> p t c", t=PACK)[:, t, :])
             return page, new
 
-        def load_raw(name, src, a, g):
-            raw = tile(name, [P, PACK, PASS], F32, tag="raw", bufs=RAW_BUFS)
-            rows = src[PASS * a : PASS * (a + 1), PASS * g : PASS * (g + 1)]
+        def load_raw(name, src, a, c0, width):
+            raw = tile(name, [P, PACK, width], F32)
+            rows = src[PASS * a : PASS * (a + 1), c0 : c0 + width]
             nc.sync.dma_start(out=raw[:], in_=rows.rearrange("(p t) c -> p t c", t=PACK))
             return raw
 
@@ -90,106 +89,145 @@ def tile_list_ion_pulse_compensation_kernel(
             )
             return words
 
+        wb_sc = zeroed("wb_sc", 2 * H, nc.gpsimd)
+        list2 = load_list("list2", offs2)
+        list1 = load_list("list1", offs)
+        load_scales(nc.sync, wb_sc, wb_scales)
         angle_zero = tile("angle_zero", [P, 8], F32)
         nc.vector.memset(angle_zero[:], 0.0)
         zero = tile("zero", [P, 8], F32)
         nc.scalar.activation(zero[:], angle_zero[:], ACT.Sin)
 
         tab_sc = zeroed("tab_sc", T)
-        wb_sc = zeroed("wb_sc", 2 * H)
         v_sc_second = zeroed("v_sc_second", S)
         wc_sc = zeroed("wc_sc", 2 * N)
+
+        planes = [load_plane(0)]
+        halves = {("wp", 0): load_raw("wp_raw0a", wp, 0, 0, HALF)}
+        planes.append(load_plane(1))
         for q in range(QUADRANTS):
-            nc.gpsimd.dma_start(
+            nc.sync.dma_start(
                 out=tab_sc[:].bitcast(I32)[32 * q : 32 * q + 8, :],
                 in_=tab_scales.bitcast(I32)[:, 4 * q : 4 * q + 4, :],
             )
-        load_scales(wb_sc, wb_scales)
-        load_scales(wc_sc, wc_scales)
-
-        list2 = load_list("list2", offs2)
-        planes = [load_plane(0), load_plane(1)]
-        wp_raw = [load_raw("wp_raw0", wp, 0, 0)]
-        list1 = load_list("list1", offs)
+        halves[("wp", 1)] = load_raw("wp_raw0b", wp, 0, HALF, HALF)
         planes.append(load_plane(2))
-        wth_raw = {(0, 0): load_raw("wth_raw00", wth, 0, 0)}
-        planes.append(load_plane(3))
-        wth_raw[(1, 0)] = load_raw("wth_raw10", wth, 1, 0)
+        halves[(0, 0)] = load_raw("wth_raw00a", wth, 0, 0, HALF)
+        halves[(0, 1)] = load_raw("wth_raw00b", wth, 0, HALF, HALF)
+        planes.append(load_plane(3, lambda: halves.update({(1, 0): load_raw("wth_raw10a", wth, 1, 0, HALF)})))
+        halves[(1, 1)] = load_raw("wth_raw10b", wth, 1, HALF, HALF)
         tab = [load_table(a) for a in range(2)]
-        list3 = load_list("list3", offs3)
-        wp_raw.append(load_raw("wp_raw1", wp, 0, 1))
+
+        def quantise(name, rounded, width, codes_tag=None, codes=None):
+            if codes is None:
+                codes = tile(name + "_codes", [P, width], U32, tag=codes_tag)[:]
+            scales = tile(name + "_scales", [P, width], U8)
+            nc.vector.quantize_mx(out=codes.bitcast(FP8X4), scales=scales[:], in_=rounded[:])
+            return codes, scales[:]
+
+        def round_weights(rounded, raw, m0, copy):
+            count = raw.shape[2] // PACK
+            copy(
+                out=rounded.rearrange("p (t m k) -> p m k t", t=PACK, k=PACK)[:, m0 : m0 + count],
+                in_=raw[:].rearrange("p k (m t) -> p m k t", t=PACK),
+            )
+
+        def rounded_tile(name):
+            return tile(name, [P, PACK * PASS], BF16, tag="rounded", bufs=2)
+
+        wb_sc_ordered = tile("wb_sc_ordered", [P, 2 * H], U8)
+        nc.vector.tensor_copy(
+            out=wb_sc_ordered[:].rearrange("p (b t m) -> p b t m", b=4, t=PACK),
+            in_=wb_sc[:].rearrange("p (b m t) -> p b t m", b=4, t=PACK),
+        )
+
+        def scatter(t):
+            page, new = planes[t]
+            nc.vector.tensor_copy(page[:].indirect(list2[:]), new[:])
+
+        def round_plane(t, which=(0, 1)):
+            for h in which:
+                nc.scalar.copy(out=pairs[:, h, t // 2, :, t % 2], in_=planes[t][0][:, BANK * h : BANK * (h + 1)])
+
+        wp_bf = rounded_tile("wp0_bf")
+        wth_bf = tile("wth_bf", [P, 2 * PACK * PASS], BF16)
+        early = {"wp": wp_bf[:], 0: wth_bf[:, 0 : PACK * PASS], 1: wth_bf[:, PACK * PASS :]}
+
+        def round_half(key, half):
+            round_weights(early[key], halves[(key, half)], half * P // 2, nc.scalar.copy)
+
+        def gather_words(a):
+            codes = tile("v_codes%d" % a, [P, S], U32)
+            nc.vector.tensor_copy(codes[:], tab[a][:].indirect(list1[:]))
+            return codes
+
+        scatter(0)
+        round_half("wp", 0)
+        scatter(1)
+        round_half("wp", 1)
+        pairs = tile("pairs", [P, 2, 2, BANK, 2], BF16, tag="wp_raw0b")
+        round_plane(0)
+        v_sc = tile("v_sc", [P, S], U8)
+        nc.vector.tensor_copy(v_sc[:], tab_sc[:].indirect(list1[:]))
+        nc.sync.dma_start(
+            out=v_sc_second[:].bitcast(I32)[0:SHIFT_ROWS, :], in_=v_sc[:].bitcast(I32)[4 : 4 + SHIFT_ROWS, :]
+        )
         wb_w = tile("wb_w", [P, 2 * 2 * H], U8)
         nc.sync.dma_start(
             out=wb_w[:].bitcast(I32).rearrange("p (a c) -> p a c", a=2),
             in_=wb_words.bitcast(I32).rearrange("a p c -> p a c"),
         )
-        for a in range(2):
-            wth_raw[(a, 1)] = load_raw("wth_raw%d1" % a, wth, a, 1)
+        list3 = load_list("list3", offs3)
+        wth_mid = load_raw("wth_raw01", wth, 0, PASS, PASS)
+        wp_late = load_raw("wp_raw1", wp, 0, PASS, PASS)
+        wth_late = load_raw("wth_raw11", wth, 1, PASS, PASS)
         wc_w = tile("wc_w", [P, 2 * N], U32)
         nc.sync.dma_start(
             out=wc_w[:].bitcast(I32).rearrange("p (a c) -> p a c", a=2),
             in_=wc_words.rearrange("a p c i -> p a (c i)").bitcast(I32),
         )
+        load_scales(nc.sync, wc_sc, wc_scales)
 
-        def quantise(name, rounded, width, codes_tag=None):
-            codes = tile(name + "_codes", [P, width], U32, tag=codes_tag)
-            scales = tile(name + "_scales", [P, width], U8)
-            nc.vector.quantize_mx(out=codes[:].bitcast(FP8X4), scales=scales[:], in_=rounded[:])
-            return codes, scales
-
-        def round_weights(name, raw, copy, rounded_tag=None, codes_tag=None):
-            rounded = tile(name + "_bf", [P, PACK * PASS], BF16, tag=rounded_tag)
-            copy(
-                out=rounded[:].rearrange("p (t m k) -> p m k t", t=PACK, k=PACK),
-                in_=raw[:].rearrange("p k (m t) -> p m k t", t=PACK),
-            )
-            return quantise(name, rounded, PASS, codes_tag)
-
-        pairs = [tile("pairs%d" % h, [P, 2, BANK, 2], BF16) for h in range(2)]
-
-        wp_q = [round_weights("wp0", wp_raw[0], nc.scalar.copy, codes_tag="new3")]
-        wth_q = {(0, 0): round_weights("wth00", wth_raw[(0, 0)], nc.scalar.copy, codes_tag="wp0_bf")}
-        for t, (page, new) in enumerate(planes):
-            nc.vector.tensor_copy(page[:].indirect(list2[:]), new[:])
-            for h in range(2):
-                nc.scalar.copy(out=pairs[h][:, t // 2, :, t % 2], in_=page[:, BANK * h : BANK * (h + 1)])
-        wth_q[(1, 0)] = round_weights("wth10", wth_raw[(1, 0)], nc.scalar.copy, rounded_tag="last_plane")
-
-        page_q = []
+        scatter(2)
+        round_plane(1)
+        round_half(0, 0)
+        round_half(0, 1)
+        scatter(3)
+        round_plane(2)
+        round_half(1, 0)
+        round_half(1, 1)
+        page_bf = [tile("page_bf%d" % h, [P, PACK * BANK], BF16) for h in range(2)]
         for h in range(2):
-            page_bf = tile("page_bf%d" % h, [P, PACK * BANK], BF16)
-            nc.vector.tensor_copy(
-                out=page_bf[:].bitcast(I32).rearrange("p (c u) -> p c u", u=2),
-                in_=pairs[h][:].rearrange("p u c e -> p u (c e)").bitcast(I32).rearrange("p u c -> p c u"),
+            round_plane(3, (h,))
+            nc.scalar.copy(
+                out=page_bf[h][:].bitcast(U32).rearrange("p (c u) -> p c u", u=2),
+                in_=pairs[:, h].rearrange("p u c e -> p u (c e)").bitcast(U32).rearrange("p u c -> p c u"),
             )
-            page_q.append(quantise("page%d" % h, page_bf, BANK))
-
-        v_sc = tile("v_sc", [P, S], U8, tag="new2")
-        nc.vector.tensor_copy(v_sc[:], tab_sc[:].indirect(list1[:]))
-        nc.gpsimd.dma_start(
-            out=v_sc_second[:].bitcast(I32)[0:SHIFT_ROWS, :], in_=v_sc[:].bitcast(I32)[4 : 4 + SHIFT_ROWS, :]
-        )
-        v_codes = []
-        for a in range(2):
-            codes = tile("v_codes%d" % a, [P, S], U32, tag="pairs%d" % a)
-            nc.vector.tensor_copy(codes[:], tab[a][:].indirect(list1[:]))
-            v_codes.append(codes)
-
-        wb_sc_ordered = tile("wb_sc_ordered", [P, 2 * H], U8, tag="wth00_bf")
-        nc.vector.tensor_copy(
-            out=wb_sc_ordered[:].rearrange("p (b t m) -> p b t m", b=4, t=PACK),
-            in_=wb_sc[:].rearrange("p (b m t) -> p b t m", b=4, t=PACK),
-        )
-        wb_ordered = tile("wb_ordered", [P, 2 * 2 * H], U8, tag="tab0")
+        v_codes = [gather_words(0)]
+        wp_q = [quantise("wp0", wp_bf, PASS, codes_tag="tab0")]
+        v_codes.append(gather_words(1))
+        held = tile("held_codes", [P, 3 * PASS], U32, tag="tab1")
+        codes, scales = quantise("wth_early", wth_bf, 2 * PASS, codes=held[:, 0 : 2 * PASS])
+        wth_q = {(a, 0): (codes[:, PASS * a : PASS * (a + 1)], scales[:, PASS * a : PASS * (a + 1)]) for a in range(2)}
+        page_q = [quantise("page0", page_bf[0], BANK, codes=held[:, 2 * PASS :])]
+        wb_ordered = tile("wb_ordered", [P, 2 * 2 * H], U8)
         nc.vector.tensor_copy(
             out=wb_ordered[:].bitcast(U16).rearrange("p (b t m) -> p b t m", b=4, t=PACK),
             in_=wb_w[:].bitcast(U16).rearrange("p (b m t) -> p b t m", b=4, t=PACK),
         )
-        wp_q.append(round_weights("wp1", wp_raw[1], nc.vector.tensor_copy))
+        page_q.append(quantise("page1", page_bf[1], BANK, codes_tag="wb_w"))
+
+        def late_weights(name, raw, copy):
+            rounded = rounded_tile(name + "_bf")
+            round_weights(rounded[:], raw, 0, copy)
+            return quantise(name, rounded, PASS)
+
+        wth_q[(0, 1)] = late_weights("wth01", wth_mid, nc.vector.tensor_copy)
+        wp_q.append(late_weights("wp1", wp_late, nc.vector.tensor_copy))
 
         a_rows, sines, sizes, z_q = {}, {}, {}, {}
-        terms_x = [tile("term_x%d" % g, [P, PACK, S], F32) for g in range(2)]
-        first_b = tile("term_b0", [P, PACK, S], F32)
+        terms_x = [tile("term_x%d" % g, [P, PACK, S], F32, tag=("term_x0", "tab0")[g]) for g in range(2)]
+        first_b = tile("term_b0", [P, PACK, S], F32, tag="wth_raw01")
         terms_b = {(1, h): tile("term_b1%d" % h, [P, PACK, HALF], F32)[:] for h in range(2)}
         terms_b.update({(0, h): first_b[:, :, HALF * h : HALF * (h + 1)] for h in range(2)})
 
@@ -198,10 +236,10 @@ def tile_list_ion_pulse_compensation_kernel(
             cols = slice(P * (i % PACK), P * (i % PACK + 1))
             a_rows[i] = tile("a%d" % i, [P, T2], F32, tag="rows", bufs=ROW_BUFS)
             for h in range(2):
-                acc = bank("a_acc", "shared", SHARED_BANKS)
+                acc = bank("a_acc", "a", A_BANKS)
                 nc.tensor.matmul_mx(
                     out=acc[:], lhsT=codes[:, cols].bitcast(FP8X4), lhsT_scale=scales[:, cols],
-                    rhs=page_q[h][0][:].bitcast(FP8X4), rhs_scale=page_q[h][1][:],
+                    rhs=page_q[h][0].bitcast(FP8X4), rhs_scale=page_q[h][1],
                     start=True, stop=True,
                 )
                 nc.scalar.copy(out=a_rows[i][:, BANK * h : BANK * (h + 1)], in_=acc[:])
@@ -209,7 +247,7 @@ def tile_list_ion_pulse_compensation_kernel(
         def angles(i):
             g, t = divmod(i, PACK)
             cols = slice(P * t, P * (t + 1))
-            th = bank("th", "shared", SHARED_BANKS)
+            th = bank("th", "th", TH_BANKS)
             for a in range(2):
                 codes, scales = wth_q[(a, g)]
                 nc.tensor.matmul_mx(
@@ -261,17 +299,17 @@ def tile_list_ion_pulse_compensation_kernel(
 
         def control(h):
             for pair in range(2):
-                acc = bank("out_acc", "shared", SHARED_BANKS)
-                for k in range(2):
-                    for g in range(2):
+                acc = bank("out_acc", "a", A_BANKS) if h == 0 else bank("out_acc", "th", TH_BANKS)
+                for g in range(2):
+                    for k in range(2):
                         c0 = N * g + P * (2 * pair + k)
                         nc.tensor.matmul_mx(
                             out=acc[:, HALF * k : HALF * (k + 1)],
                             lhsT=wc_w[:, c0 : c0 + P].bitcast(FP8X4), lhsT_scale=wc_sc[:, c0 : c0 + P],
-                            rhs=z_q[(g, h)][0][:].bitcast(FP8X4), rhs_scale=z_q[(g, h)][1][:],
-                            start=(g == 0), stop=(g == 1),
+                            rhs=z_q[(g, h)][0].bitcast(FP8X4), rhs_scale=z_q[(g, h)][1],
+                            start=(g == 0 and k == 0), stop=(g == 1 and k == 1),
                         )
-                result = tile("result%d%d" % (h, pair), [P, 2, HALF], F32)
+                result = tile("result%d%d" % (h, pair), [P, 2, HALF], F32, tag=("new0", "new1", "new2", "result")[2 * h + pair])
                 copy = nc.vector.tensor_copy if (h, pair) == (1, 1) else nc.scalar.copy
                 copy(out=result[:].rearrange("p n j -> p (n j)"), in_=acc[:])
                 nc.sync.dma_start(
@@ -279,18 +317,14 @@ def tile_list_ion_pulse_compensation_kernel(
                     in_=result[:],
                 )
 
-        late_copies = (nc.scalar.copy, nc.vector.tensor_copy)
         project(0)
         for t in range(PACK):
             if t + 1 < PACK:
                 project(t + 1)
             angles(t)
             weigh_x(t, 0, S)
-            if t >= 2:
-                a = t - 2
-                wth_q[(a, 1)] = round_weights(
-                    "wth%d1" % a, wth_raw[(a, 1)], late_copies[a], rounded_tag="page_bf%d" % (1 - a)
-                )
+            if t == 1:
+                wth_q[(1, 1)] = late_weights("wth11", wth_late, nc.vector.tensor_copy)
             weigh_b(t)
         for t in range(PACK - 1):
             project(PACK + t)
@@ -303,9 +337,9 @@ def tile_list_ion_pulse_compensation_kernel(
         project(last)
         angles(last)
         weigh_b(last)
-        weigh_x(last, 0, HALF)
+        weigh_x(last, 0, HALF, tag="last_cosine", bufs=1)
         combine(1, 0)
-        weigh_x(last, HALF, S, tag="term_b10", bufs=1)
+        weigh_x(last, HALF, S, tag="last_cosine", bufs=1)
         combine(1, 1)
         for h in range(2):
             control(h)

@@ -111,9 +111,9 @@ def tile_list_ion_pulse_compensation_kernel(
                 in_=tab_scales.bitcast(I32)[:, 4 * q : 4 * q + 4, :],
             )
         halves[("wp", 1)] = load_raw("wp_raw0b", wp, 0, HALF, HALF)
-        planes.append(load_plane(2))
-        halves[(0, 0)] = load_raw("wth_raw00a", wth, 0, 0, HALF)
-        halves[(0, 1)] = load_raw("wth_raw00b", wth, 0, HALF, HALF)
+        planes.append(
+            load_plane(2, lambda: halves.update({(0, k): load_raw("wth_raw00%d" % k, wth, 0, HALF * k, HALF) for k in range(2)}))
+        )
         planes.append(load_plane(3, lambda: halves.update({(1, 0): load_raw("wth_raw10a", wth, 1, 0, HALF)})))
         halves[(1, 1)] = load_raw("wth_raw10b", wth, 1, HALF, HALF)
         tab = [load_table(a) for a in range(2)]
@@ -147,7 +147,11 @@ def tile_list_ion_pulse_compensation_kernel(
 
         def round_plane(t, which=(0, 1)):
             for h in which:
-                nc.scalar.copy(out=pairs[:, h, t // 2, :, t % 2], in_=planes[t][0][:, BANK * h : BANK * (h + 1)])
+                rounded, source = pairs[:, h, t // 2, :, t % 2], planes[t][0][:, BANK * h : BANK * (h + 1)]
+                if t < 2:
+                    nc.gpsimd.tensor_scalar(rounded, source, 1.0, 0.0, MULT, ADD)
+                else:
+                    nc.scalar.copy(out=rounded, in_=source)
 
         wp_bf = rounded_tile("wp0_bf")
         wth_bf = tile("wth_bf", [P, 2 * PACK * PASS], BF16)
@@ -165,7 +169,7 @@ def tile_list_ion_pulse_compensation_kernel(
         round_half("wp", 0)
         scatter(1)
         round_half("wp", 1)
-        pairs = tile("pairs", [P, 2, 2, BANK, 2], BF16, tag="wp_raw0b")
+        pairs = tile("pairs", [P, 2, 2, BANK, 2], BF16)
         round_plane(0)
         v_sc = tile("v_sc", [P, S], U8)
         nc.vector.tensor_copy(v_sc[:], tab_sc[:].indirect(list1[:]))
@@ -188,6 +192,7 @@ def tile_list_ion_pulse_compensation_kernel(
         )
         load_scales(nc.sync, wc_sc, wc_scales)
 
+        wp_q = [quantise("wp0", wp_bf, PASS)]
         scatter(2)
         round_plane(1)
         round_half(0, 0)
@@ -204,7 +209,6 @@ def tile_list_ion_pulse_compensation_kernel(
                 in_=pairs[:, h].rearrange("p u c e -> p u (c e)").bitcast(U32).rearrange("p u c -> p c u"),
             )
         v_codes = [gather_words(0)]
-        wp_q = [quantise("wp0", wp_bf, PASS, codes_tag="tab0")]
         v_codes.append(gather_words(1))
         held = tile("held_codes", [P, 3 * PASS], U32, tag="tab1")
         codes, scales = quantise("wth_early", wth_bf, 2 * PASS, codes=held[:, 0 : 2 * PASS])

@@ -26,11 +26,10 @@ HALF = S // 2
 QUADRANTS = 4
 SHIFT_ROWS = 112
 
-ROW_BUFS = 7
+ROW_BUFS = 8
 TRIG_BUFS = 4
 A_BANKS = 3
-TH_BANKS = 2
-B_BANKS = 3
+PAIR_BANKS = 5
 
 
 def tile_list_ion_pulse_compensation_kernel(
@@ -102,27 +101,35 @@ def tile_list_ion_pulse_compensation_kernel(
         v_sc_second = zeroed("v_sc_second", S)
         wc_sc = zeroed("wc_sc", 2 * N)
 
+        halves = {}
+
+        def load_half(name, a, g, k):
+            src = {"wp": wp, "wth": wth}[name]
+            halves[(name, a, g, k)] = load_raw("%s_raw%d%d%d" % (name, a, g, k), src, a, PASS * g + HALF * k, HALF)
+
         planes = [load_plane(0)]
-        halves = {("wp", 0): load_raw("wp_raw0a", wp, 0, 0, HALF)}
+        load_half("wp", 0, 0, 0)
         planes.append(load_plane(1))
+        load_half("wp", 0, 0, 1)
+        planes.append(load_plane(2, lambda: load_half("wp", 0, 1, 0)))
+        load_half("wp", 0, 1, 1)
+        planes.append(load_plane(3, lambda: load_half("wth", 0, 0, 0)))
         for q in range(QUADRANTS):
             nc.sync.dma_start(
                 out=tab_sc[:].bitcast(I32)[32 * q : 32 * q + 8, :],
                 in_=tab_scales.bitcast(I32)[:, 4 * q : 4 * q + 4, :],
             )
-        halves[("wp", 1)] = load_raw("wp_raw0b", wp, 0, HALF, HALF)
-        planes.append(
-            load_plane(2, lambda: halves.update({(0, k): load_raw("wth_raw00%d" % k, wth, 0, HALF * k, HALF) for k in range(2)}))
-        )
-        planes.append(load_plane(3, lambda: halves.update({(1, 0): load_raw("wth_raw10a", wth, 1, 0, HALF)})))
-        halves[(1, 1)] = load_raw("wth_raw10b", wth, 1, HALF, HALF)
+        load_half("wth", 0, 0, 1)
+        load_half("wth", 1, 0, 0)
+        load_half("wth", 1, 0, 1)
+        list3 = load_list("list3", offs3)
         tab = [load_table(a) for a in range(2)]
 
         def quantise(name, rounded, width, codes_tag=None, codes=None):
             if codes is None:
                 codes = tile(name + "_codes", [P, width], U32, tag=codes_tag)[:]
             scales = tile(name + "_scales", [P, width], U8)
-            nc.vector.quantize_mx(out=codes.bitcast(FP8X4), scales=scales[:], in_=rounded[:])
+            nc.vector.quantize_mx(out=codes.bitcast(FP8X4), scales=scales[:], in_=rounded)
             return codes, scales[:]
 
         def round_weights(rounded, raw, m0, copy):
@@ -132,45 +139,41 @@ def tile_list_ion_pulse_compensation_kernel(
                 in_=raw[:].rearrange("p k (m t) -> p m k t", t=PACK),
             )
 
-        def rounded_tile(name):
-            return tile(name, [P, PACK * PASS], BF16, tag="rounded", bufs=2)
-
         wb_sc_ordered = tile("wb_sc_ordered", [P, 2 * H], U8)
         nc.vector.tensor_copy(
             out=wb_sc_ordered[:].rearrange("p (b t m) -> p b t m", b=4, t=PACK),
             in_=wb_sc[:].rearrange("p (b m t) -> p b t m", b=4, t=PACK),
         )
 
+        pairs = tile("pairs", [P, 2, 2, BANK, 2], BF16)
+
         def scatter(t):
             page, new = planes[t]
             nc.vector.tensor_copy(page[:].indirect(list2[:]), new[:])
+            for h in range(2):
+                nc.gpsimd.tensor_scalar(
+                    pairs[:, h, t // 2, :, t % 2], page[:, BANK * h : BANK * (h + 1)], 1.0, 0.0, MULT, ADD
+                )
 
-        def round_plane(t, which=(0, 1)):
-            for h in which:
-                rounded, source = pairs[:, h, t // 2, :, t % 2], planes[t][0][:, BANK * h : BANK * (h + 1)]
-                if t < 2:
-                    nc.gpsimd.tensor_scalar(rounded, source, 1.0, 0.0, MULT, ADD)
-                else:
-                    nc.scalar.copy(out=rounded, in_=source)
+        def round_two(name, keys, copy, tag):
+            rounded = tile(name, [P, 2, PACK * PASS], BF16, tag=tag, bufs=2)
+            for n, key in enumerate(keys):
+                for k in range(2):
+                    round_weights(rounded[:, n], halves[key + (k,)], k * P // 2, copy)
+            return rounded[:].rearrange("p n c -> p (n c)")
 
-        wp_bf = rounded_tile("wp0_bf")
-        wth_bf = tile("wth_bf", [P, 2 * PACK * PASS], BF16)
-        early = {"wp": wp_bf[:], 0: wth_bf[:, 0 : PACK * PASS], 1: wth_bf[:, PACK * PASS :]}
-
-        def round_half(key, half):
-            round_weights(early[key], halves[(key, half)], half * P // 2, nc.scalar.copy)
+        def pieces(codes, scales):
+            return [(codes[:, PASS * n : PASS * (n + 1)], scales[:, PASS * n : PASS * (n + 1)]) for n in range(2)]
 
         def gather_words(a):
             codes = tile("v_codes%d" % a, [P, S], U32)
             nc.vector.tensor_copy(codes[:], tab[a][:].indirect(list1[:]))
             return codes
 
-        scatter(0)
-        round_half("wp", 0)
-        scatter(1)
-        round_half("wp", 1)
-        pairs = tile("pairs", [P, 2, 2, BANK, 2], BF16)
-        round_plane(0)
+        for t in range(3):
+            scatter(t)
+        wp_q = pieces(*quantise("wp", round_two("wp_bf", [("wp", 0, 0), ("wp", 0, 1)], nc.scalar.copy, "rounded"), 2 * PASS))
+        scatter(3)
         v_sc = tile("v_sc", [P, S], U8)
         nc.vector.tensor_copy(v_sc[:], tab_sc[:].indirect(list1[:]))
         nc.sync.dma_start(
@@ -181,10 +184,9 @@ def tile_list_ion_pulse_compensation_kernel(
             out=wb_w[:].bitcast(I32).rearrange("p (a c) -> p a c", a=2),
             in_=wb_words.bitcast(I32).rearrange("a p c -> p a c"),
         )
-        list3 = load_list("list3", offs3)
-        wth_mid = load_raw("wth_raw01", wth, 0, PASS, PASS)
-        wp_late = load_raw("wp_raw1", wp, 0, PASS, PASS)
-        wth_late = load_raw("wth_raw11", wth, 1, PASS, PASS)
+        for a in range(2):
+            for k in range(2):
+                load_half("wth", a, 1, k)
         wc_w = tile("wc_w", [P, 2 * N], U32)
         nc.sync.dma_start(
             out=wc_w[:].bitcast(I32).rearrange("p (a c) -> p a c", a=2),
@@ -192,54 +194,24 @@ def tile_list_ion_pulse_compensation_kernel(
         )
         load_scales(nc.sync, wc_sc, wc_scales)
 
-        wp_q = [quantise("wp0", wp_bf, PASS)]
-        scatter(2)
-        round_plane(1)
-        round_half(0, 0)
-        round_half(0, 1)
-        scatter(3)
-        round_plane(2)
-        round_half(1, 0)
-        round_half(1, 1)
-        page_bf = [tile("page_bf%d" % h, [P, PACK * BANK], BF16) for h in range(2)]
+        wth_q = [pieces(*quantise("wth0", round_two("wth0_bf", [("wth", 0, 0), ("wth", 1, 0)], nc.scalar.copy, "rounded"), 2 * PASS))]
+        page_bf = tile("page_bf", [P, 2, PACK * BANK], BF16, tag="wth_raw101")
         for h in range(2):
-            round_plane(3, (h,))
             nc.scalar.copy(
-                out=page_bf[h][:].bitcast(U32).rearrange("p (c u) -> p c u", u=2),
+                out=page_bf[:, h].bitcast(U32).rearrange("p (c u) -> p c u", u=2),
                 in_=pairs[:, h].rearrange("p u c e -> p u (c e)").bitcast(U32).rearrange("p u c -> p c u"),
             )
+        page_q = [quantise("page0", page_bf[:, 0], BANK)]
         v_codes = [gather_words(0)]
-        v_codes.append(gather_words(1))
-        held = tile("held_codes", [P, 3 * PASS], U32, tag="tab1")
-        codes, scales = quantise("wth_early", wth_bf, 2 * PASS, codes=held[:, 0 : 2 * PASS])
-        wth_q = {(a, 0): (codes[:, PASS * a : PASS * (a + 1)], scales[:, PASS * a : PASS * (a + 1)]) for a in range(2)}
-        page_q = [quantise("page0", page_bf[0], BANK, codes=held[:, 2 * PASS :])]
-        wb_ordered = tile("wb_ordered", [P, 2 * 2 * H], U8)
-        nc.vector.tensor_copy(
-            out=wb_ordered[:].bitcast(U16).rearrange("p (b t m) -> p b t m", b=4, t=PACK),
-            in_=wb_w[:].bitcast(U16).rearrange("p (b m t) -> p b t m", b=4, t=PACK),
-        )
-        page_q.append(quantise("page1", page_bf[1], BANK, codes_tag="wb_w"))
+        page_q.append(quantise("page1", page_bf[:, 1], BANK))
+        a_rows = {}
 
-        def late_weights(name, raw, copy):
-            rounded = rounded_tile(name + "_bf")
-            round_weights(rounded[:], raw, 0, copy)
-            return quantise(name, rounded, PASS)
-
-        wth_q[(0, 1)] = late_weights("wth01", wth_mid, nc.vector.tensor_copy)
-        wp_q.append(late_weights("wp1", wp_late, nc.vector.tensor_copy))
-
-        a_rows, sines, sizes, z_q = {}, {}, {}, {}
-        terms_x = [tile("term_x%d" % g, [P, PACK, S], F32, tag=("term_x0", "tab0")[g]) for g in range(2)]
-        first_b = tile("term_b0", [P, PACK, S], F32, tag="wth_raw01")
-        terms_b = {(1, h): tile("term_b1%d" % h, [P, PACK, HALF], F32)[:] for h in range(2)}
-        terms_b.update({(0, h): first_b[:, :, HALF * h : HALF * (h + 1)] for h in range(2)})
-
-        def project(i):
+        def project(i, which=(0, 1)):
             codes, scales = wp_q[i // PACK]
             cols = slice(P * (i % PACK), P * (i % PACK + 1))
-            a_rows[i] = tile("a%d" % i, [P, T2], F32, tag="rows", bufs=ROW_BUFS)
-            for h in range(2):
+            if i not in a_rows:
+                a_rows[i] = tile("a%d" % i, [P, T2], F32, tag="rows", bufs=ROW_BUFS)
+            for h in which:
                 acc = bank("a_acc", "a", A_BANKS)
                 nc.tensor.matmul_mx(
                     out=acc[:], lhsT=codes[:, cols].bitcast(FP8X4), lhsT_scale=scales[:, cols],
@@ -248,102 +220,116 @@ def tile_list_ion_pulse_compensation_kernel(
                 )
                 nc.scalar.copy(out=a_rows[i][:, BANK * h : BANK * (h + 1)], in_=acc[:])
 
-        def angles(i):
+        v_codes.append(gather_words(1))
+        wb_ordered = tile("wb_ordered", [P, 2 * 2 * H], U8)
+        nc.vector.tensor_copy(
+            out=wb_ordered[:].bitcast(U16).rearrange("p (b t m) -> p b t m", b=4, t=PACK),
+            in_=wb_w[:].bitcast(U16).rearrange("p (b m t) -> p b t m", b=4, t=PACK),
+        )
+
+        z_q = [(tile("z_codes%d" % g, [P, S], U32), tile("z_scales%d" % g, [P, S], U8)) for g in range(2)]
+        first_terms = tile("first_terms", [P, 2, PACK, S], F32, tag="wth_raw111")
+        late_bf = tile("late_bf", [P, 2, PACK * PASS], BF16, tag="tab0")
+        terms_x = [first_terms[:, 0], tile("term_x1", [P, PACK, S], F32, tag="tab0")[:]]
+        terms_b = [first_terms[:, 1], tile("term_b1", [P, PACK, S], F32, tag="tab1")[:]]
+
+        def pick(i):
+            g, t = divmod(i, PACK)
+            nc.vector.tensor_copy(terms_x[g][:, t, :], a_rows[i][:].indirect(list3[:]))
+
+        def weigh(i, j0, j1):
             g, t = divmod(i, PACK)
             cols = slice(P * t, P * (t + 1))
-            th = bank("th", "th", TH_BANKS)
+            js = slice(j0, j1)
+            width = j1 - j0
+            th = bank("th", "pair", PAIR_BANKS)
             for a in range(2):
-                codes, scales = wth_q[(a, g)]
+                codes, scales = wth_q[g][a]
                 nc.tensor.matmul_mx(
-                    out=th[:], lhsT=codes[:, cols].bitcast(FP8X4), lhsT_scale=scales[:, cols],
-                    rhs=v_codes[a][:].bitcast(FP8X4), rhs_scale=v_sc[4 * a : P, :],
+                    out=th[:, 0:width], lhsT=codes[:, cols].bitcast(FP8X4), lhsT_scale=scales[:, cols],
+                    rhs=v_codes[a][:, js].bitcast(FP8X4), rhs_scale=v_sc[4 * a : P, js],
                     start=(a == 0), stop=(a == 1),
                 )
-            sizes[i] = tile("size", [P, S], F32, bufs=2)
-            sines[i] = tile("sine", [P, S], F32, bufs=TRIG_BUFS)
-            nc.scalar.activation(sines[i][:], th[:], ACT.Sin)
-            nc.scalar.activation(sizes[i][:], th[:], ACT.Abs, bias=zero[:, 0:1])
+            b = bank("b", "pair", PAIR_BANKS)
+            step = width if width == S else P
+            for s0 in range(0, width, step):
+                for a in range(2):
+                    c0 = H * a + P * i
+                    nc.tensor.matmul_mx(
+                        out=b[:, s0 : s0 + step],
+                        lhsT=wb_ordered[:, 2 * c0 : 2 * (c0 + P)].bitcast(FP4X4),
+                        lhsT_scale=wb_sc_ordered[:, c0 : c0 + P],
+                        rhs=v_codes[a][:, j0 + s0 : j0 + s0 + step].bitcast(FP8X4),
+                        rhs_scale=(v_sc, v_sc_second)[a][:, j0 + s0 : j0 + s0 + step],
+                        start=(a == 0), stop=(a == 1),
+                    )
+            size = tile("size", [P, width], F32, bufs=2)
+            sine = tile("sine", [P, width], F32, bufs=TRIG_BUFS)
+            cosine = tile("cosine", [P, width], F32, bufs=TRIG_BUFS)
+            nc.scalar.activation(sine[:], th[:, 0:width], ACT.Sin)
+            nc.scalar.activation(size[:], th[:, 0:width], ACT.Abs, bias=zero[:, 0:1])
+            nc.scalar.activation(cosine[:], size[:], ACT.Sin, bias=math.pi / 2, scale=-1.0)
+            nc.vector.tensor_tensor(terms_b[g][:, t, js], b[:, 0:width], sine[:], MULT)
+            return cosine
 
-        def weigh_x(i, j0, j1, tag="cosine", bufs=TRIG_BUFS):
-            g, t = divmod(i, PACK)
-            cosine = tile("cosine", [P, j1 - j0], F32, tag=tag, bufs=bufs)
-            nc.scalar.activation(cosine[:], sizes[i][:, j0:j1], ACT.Sin, bias=math.pi / 2, scale=-1.0)
-            nc.vector.tensor_tensor(
-                terms_x[g][:, t, j0:j1], a_rows[i][:].indirect(list3[:, j0 // 16 : j1 // 16]), cosine[:], MULT
-            )
+        def turn(i, cosine, j0, j1, engine):
+            x = terms_x[i // PACK][:, i % PACK, j0:j1]
+            engine.tensor_tensor(x, x, cosine[:, j0:j1], MULT)
 
-        def weigh_b(i):
-            g, t = divmod(i, PACK)
-            b = bank("b", "b", B_BANKS)
-            for a in range(2):
-                c0 = H * a + P * i
-                nc.tensor.matmul_mx(
-                    out=b[:],
-                    lhsT=wb_ordered[:, 2 * c0 : 2 * (c0 + P)].bitcast(FP4X4),
-                    lhsT_scale=wb_sc_ordered[:, c0 : c0 + P],
-                    rhs=v_codes[a][:].bitcast(FP8X4), rhs_scale=(v_sc, v_sc_second)[a][:],
-                    start=(a == 0), stop=(a == 1),
-                )
-            if g == 0:
-                nc.vector.tensor_tensor(first_b[:, t, :], b[:], sines[i][:], MULT)
-            else:
-                for h in range(2):
-                    js = slice(HALF * h, HALF * (h + 1))
-                    nc.vector.tensor_tensor(terms_b[(g, h)][:, t, :], b[:, js], sines[i][:, js], MULT)
-
-        def combine(g, h):
-            z_bf = tile("z_bf", [P, PACK * HALF], BF16, bufs=2)
+        def combine(g, j0, j1):
+            z_bf = tile("z_bf", [P, PACK * (j1 - j0)], BF16, bufs=2)
             nc.vector.tensor_tensor(
                 z_bf[:].rearrange("p (c i t) -> p c t i", i=4, t=PACK),
-                terms_x[g][:, :, HALF * h : HALF * (h + 1)].rearrange("p t (c i) -> p c t i", i=4),
-                terms_b[(g, h)].rearrange("p t (c i) -> p c t i", i=4),
+                terms_x[g][:, :, j0:j1].rearrange("p t (c i) -> p c t i", i=4),
+                terms_b[g][:, :, j0:j1].rearrange("p t (c i) -> p c t i", i=4),
                 ADD,
             )
-            z_q[(g, h)] = quantise("z%d%d" % (g, h), z_bf, HALF)
+            codes, scales = z_q[g]
+            nc.vector.quantize_mx(out=codes[:, j0:j1].bitcast(FP8X4), scales=scales[:, j0:j1], in_=z_bf[:])
 
-        def control(h):
-            for pair in range(2):
-                acc = bank("out_acc", "a", A_BANKS) if h == 0 else bank("out_acc", "th", TH_BANKS)
+        def control(j0, j1):
+            width = j1 - j0
+            per_bank = BANK // width
+            for n0 in range(0, N // P, per_bank):
+                acc = bank("out_acc", "pair", PAIR_BANKS)
                 for g in range(2):
-                    for k in range(2):
-                        c0 = N * g + P * (2 * pair + k)
+                    for k in range(per_bank):
+                        c0 = N * g + P * (n0 + k)
                         nc.tensor.matmul_mx(
-                            out=acc[:, HALF * k : HALF * (k + 1)],
+                            out=acc[:, width * k : width * (k + 1)],
                             lhsT=wc_w[:, c0 : c0 + P].bitcast(FP8X4), lhsT_scale=wc_sc[:, c0 : c0 + P],
-                            rhs=z_q[(g, h)][0].bitcast(FP8X4), rhs_scale=z_q[(g, h)][1],
-                            start=(g == 0 and k == 0), stop=(g == 1 and k == 1),
+                            rhs=z_q[g][0][:, j0:j1].bitcast(FP8X4), rhs_scale=z_q[g][1][:, j0:j1],
+                            start=(g == 0 and k == 0), stop=(g == 1 and k == per_bank - 1),
                         )
-                result = tile("result%d%d" % (h, pair), [P, 2, HALF], F32, tag=("new0", "new1", "new2", "result")[2 * h + pair])
-                copy = nc.vector.tensor_copy if (h, pair) == (1, 1) else nc.scalar.copy
+                result = tile("result", [P, per_bank, width], F32, bufs=4)
+                copy = nc.vector.tensor_copy if j1 == S else nc.scalar.copy
                 copy(out=result[:].rearrange("p n j -> p (n j)"), in_=acc[:])
                 nc.sync.dma_start(
-                    out=out.rearrange("(n p) j -> p n j", p=P)[:, 2 * pair : 2 * pair + 2, HALF * h : HALF * (h + 1)],
-                    in_=result[:],
+                    out=out.rearrange("(n p) j -> p n j", p=P)[:, n0 : n0 + per_bank, j0:j1], in_=result[:]
                 )
 
-        project(0)
+        def round_late(a):
+            for k in range(2):
+                round_weights(late_bf[:, a], halves[("wth", a, 1, k)], k * P // 2, nc.vector.tensor_copy)
+
+        round_late(0)
+        round_late(1)
+        wth_q.append(pieces(*quantise("wth1", late_bf[:].rearrange("p n c -> p (n c)"), 2 * PASS)))
         for t in range(PACK):
-            if t + 1 < PACK:
-                project(t + 1)
-            angles(t)
-            weigh_x(t, 0, S)
-            if t == 1:
-                wth_q[(1, 1)] = late_weights("wth11", wth_late, nc.vector.tensor_copy)
-            weigh_b(t)
-        for t in range(PACK - 1):
-            project(PACK + t)
-            angles(PACK + t)
-            weigh_x(PACK + t, 0, S)
-            if t < 2:
-                combine(0, t)
-            weigh_b(PACK + t)
-        last = 2 * PACK - 1
-        project(last)
-        angles(last)
-        weigh_b(last)
-        weigh_x(last, 0, HALF, tag="last_cosine", bufs=1)
-        combine(1, 0)
-        weigh_x(last, HALF, S, tag="last_cosine", bufs=1)
-        combine(1, 1)
-        for h in range(2):
-            control(h)
+            project(t, (0,))
+        project(0, (1,))
+        pick(0)
+        for i in range(2 * PACK - 1):
+            project(i + 1, (1,) if i + 1 < PACK else (0, 1))
+            pick(i + 1)
+            turn(i, weigh(i, 0, S), 0, S, nc.gpsimd)
+            if i == PACK:
+                combine(0, 0, S)
+        cuts = (0, 256, 384, 512)
+        cosine = weigh(2 * PACK - 1, 0, S)
+        turn(2 * PACK - 1, cosine, 0, HALF, nc.gpsimd)
+        turn(2 * PACK - 1, cosine, HALF, S, nc.vector)
+        for c in range(len(cuts) - 1):
+            combine(1, cuts[c], cuts[c + 1])
+        for c in range(len(cuts) - 1):
+            control(cuts[c], cuts[c + 1])

@@ -26,7 +26,8 @@ HALF = S // 2
 QUADRANTS = 4
 SHIFT_ROWS = 112
 
-ROW_BUFS = 8
+ROW_BYTES = 4 * T2
+ROW_BUFS = 4
 TRIG_BUFS = 4
 A_BANKS = 3
 PAIR_BANKS = 5
@@ -40,6 +41,7 @@ def tile_list_ion_pulse_compensation_kernel(
     with ExitStack() as ctx:
         lists = ctx.enter_context(tc.tile_pool(name="lists", bufs=1))
         sb = ctx.enter_context(tc.tile_pool(name="sb", bufs=1))
+        laid = ctx.enter_context(tc.tile_pool(name="laid", bufs=1))
         ps = ctx.enter_context(tc.psum_pool(name="ps", bufs=1))
 
         def tile(name, shape, dtype, tag=None, bufs=1):
@@ -65,23 +67,27 @@ def tile_list_ion_pulse_compensation_kernel(
                     in_=src.bitcast(I32)[:, 4 * q : 4 * q + 4, :].rearrange("a q c -> q a c"),
                 )
 
-        def load_plane(t, between=None):
+        def load_plane(t):
             page = tile("page%d" % t, [P, T2], F32, tag="rows", bufs=ROW_BUFS)
             new = tile("new%d" % t, [P, S], F32)
             nc.sync.dma_start(out=page[:], in_=base.rearrange("(p t) c -> p t c", t=PACK)[:, t, :])
-            if between:
-                between()
             nc.sync.dma_start(out=new[:], in_=xs.rearrange("(p t) c -> p t c", t=PACK)[:, t, :])
             return page, new
 
-        def load_raw(name, src, a, c0, width):
-            raw = tile(name, [P, PACK, width], F32)
-            rows = src[PASS * a : PASS * (a + 1), c0 : c0 + width]
-            nc.sync.dma_start(out=raw[:], in_=rows.rearrange("(p t) c -> p t c", t=PACK))
-            return raw
+        raws = {}
+
+        def load_raw(name, a, g, planes=slice(0, PACK)):
+            key = (name, a, g)
+            if key not in raws:
+                if key == ("wth", 1, 0):
+                    raws[key] = laid.tile([P, PACK, PASS], F32, name="wth_raw10", align_bytes=64, offset=ROW_BYTES // 2)
+                else:
+                    raws[key] = tile("%s_raw%d%d" % key, [P, PACK, PASS], F32)
+            rows = {"wp": wp, "wth": wth}[name][PASS * a : PASS * (a + 1), PASS * g : PASS * (g + 1)]
+            nc.sync.dma_start(out=raws[key][:, planes], in_=rows.rearrange("(p t) c -> p t c", t=PACK)[:, planes])
 
         def load_table(a):
-            words = tile("tab%d" % a, [P, T], U32)
+            words = laid.tile([P, T], U32, name="tab%d" % a, align_bytes=64, offset=ROW_BYTES * (4 + 2 * a))
             nc.sync.dma_start(
                 out=words[:].bitcast(I32),
                 in_=tab_words[a].rearrange("p t i -> p (t i)").bitcast(I32),
@@ -101,43 +107,44 @@ def tile_list_ion_pulse_compensation_kernel(
         v_sc_second = zeroed("v_sc_second", S)
         wc_sc = zeroed("wc_sc", 2 * N)
 
-        halves = {}
-
-        def load_half(name, a, g, k):
-            src = {"wp": wp, "wth": wth}[name]
-            halves[(name, a, g, k)] = load_raw("%s_raw%d%d%d" % (name, a, g, k), src, a, PASS * g + HALF * k, HALF)
-
-        planes = [load_plane(0)]
-        load_half("wp", 0, 0, 0)
-        planes.append(load_plane(1))
-        load_half("wp", 0, 0, 1)
-        planes.append(load_plane(2, lambda: load_half("wp", 0, 1, 0)))
-        load_half("wp", 0, 1, 1)
-        planes.append(load_plane(3, lambda: load_half("wth", 0, 0, 0)))
         for q in range(QUADRANTS):
-            nc.sync.dma_start(
+            nc.gpsimd.dma_start(
                 out=tab_sc[:].bitcast(I32)[32 * q : 32 * q + 8, :],
                 in_=tab_scales.bitcast(I32)[:, 4 * q : 4 * q + 4, :],
             )
-        load_half("wth", 0, 0, 1)
-        load_half("wth", 1, 0, 0)
-        load_half("wth", 1, 0, 1)
+
+        planes = []
+        for t in range(PACK):
+            planes.append(load_plane(t))
+            load_raw("wp", 0, t // 2, slice(2 * (t % 2), 2 * (t % 2) + 2))
+        for a in range(2):
+            load_raw("wth", a, 0)
         list3 = load_list("list3", offs3)
         tab = [load_table(a) for a in range(2)]
 
-        def quantise(name, rounded, width, codes_tag=None, codes=None):
+        def quantise(name, rounded, width, codes_tag=None, codes=None, offset=None):
+            if offset is not None:
+                codes = laid.tile([P, width], U32, name=name + "_codes", align_bytes=64, offset=offset)[:]
             if codes is None:
                 codes = tile(name + "_codes", [P, width], U32, tag=codes_tag)[:]
             scales = tile(name + "_scales", [P, width], U8)
             nc.vector.quantize_mx(out=codes.bitcast(FP8X4), scales=scales[:], in_=rounded)
             return codes, scales[:]
 
-        def round_weights(rounded, raw, m0, copy):
-            count = raw.shape[2] // PACK
-            copy(
-                out=rounded.rearrange("p (t m k) -> p m k t", t=PACK, k=PACK)[:, m0 : m0 + count],
-                in_=raw[:].rearrange("p k (m t) -> p m k t", t=PACK),
+        def round_on_scalar(rounded, raw):
+            nc.scalar.copy(
+                out=rounded.rearrange("p (t m k) -> p m k t", t=PACK, k=PACK),
+                in_=raw[:, :].rearrange("p k (m t) -> p m k t", t=PACK),
             )
+
+        def round_on_gpsimd(rounded, raw):
+            for half in range(2):
+                ms = slice(half * P // 2, (half + 1) * P // 2)
+                nc.gpsimd.tensor_scalar(
+                    rounded.rearrange("p (t m k) -> p m t k", t=PACK, k=PACK)[:, ms],
+                    raw[:, :].rearrange("p k (m t) -> p m t k", t=PACK)[:, ms],
+                    1.0, 0.0, MULT, ADD,
+                )
 
         wb_sc_ordered = tile("wb_sc_ordered", [P, 2 * H], U8)
         nc.vector.tensor_copy(
@@ -155,13 +162,6 @@ def tile_list_ion_pulse_compensation_kernel(
                     pairs[:, h, t // 2, :, t % 2], page[:, BANK * h : BANK * (h + 1)], 1.0, 0.0, MULT, ADD
                 )
 
-        def round_two(name, keys, copy, tag):
-            rounded = tile(name, [P, 2, PACK * PASS], BF16, tag=tag, bufs=2)
-            for n, key in enumerate(keys):
-                for k in range(2):
-                    round_weights(rounded[:, n], halves[key + (k,)], k * P // 2, copy)
-            return rounded[:].rearrange("p n c -> p (n c)")
-
         def pieces(codes, scales):
             return [(codes[:, PASS * n : PASS * (n + 1)], scales[:, PASS * n : PASS * (n + 1)]) for n in range(2)]
 
@@ -170,11 +170,14 @@ def tile_list_ion_pulse_compensation_kernel(
             nc.vector.tensor_copy(codes[:], tab[a][:].indirect(list1[:]))
             return codes
 
+        wp_bf = [tile("wp_bf%d" % g, [P, PACK * PASS], BF16) for g in range(2)]
         for t in range(3):
             scatter(t)
-        wp_q = pieces(*quantise("wp", round_two("wp_bf", [("wp", 0, 0), ("wp", 0, 1)], nc.scalar.copy, "rounded"), 2 * PASS))
+        round_on_scalar(wp_bf[0][:], raws[("wp", 0, 0)])
+        wp_q = [quantise("wp0", wp_bf[0][:], PASS, codes_tag="new2")]
         scatter(3)
-        v_sc = tile("v_sc", [P, S], U8)
+        round_on_scalar(wp_bf[1][:], raws[("wp", 0, 1)])
+        v_sc = tile("v_sc", [P, S], U8, tag="new3")
         nc.vector.tensor_copy(v_sc[:], tab_sc[:].indirect(list1[:]))
         nc.sync.dma_start(
             out=v_sc_second[:].bitcast(I32)[0:SHIFT_ROWS, :], in_=v_sc[:].bitcast(I32)[4 : 4 + SHIFT_ROWS, :]
@@ -184,9 +187,10 @@ def tile_list_ion_pulse_compensation_kernel(
             out=wb_w[:].bitcast(I32).rearrange("p (a c) -> p a c", a=2),
             in_=wb_words.bitcast(I32).rearrange("a p c -> p a c"),
         )
+        late = tile("late", [P, 13 * S], F32)
         for a in range(2):
-            for k in range(2):
-                load_half("wth", a, 1, k)
+            raws[("wth", a, 1)] = late[:, PACK * PASS * a : PACK * PASS * (a + 1)].rearrange("p (t c) -> p t c", t=PACK)
+            load_raw("wth", a, 1)
         wc_w = tile("wc_w", [P, 2 * N], U32)
         nc.sync.dma_start(
             out=wc_w[:].bitcast(I32).rearrange("p (a c) -> p a c", a=2),
@@ -194,23 +198,30 @@ def tile_list_ion_pulse_compensation_kernel(
         )
         load_scales(nc.sync, wc_sc, wc_scales)
 
-        wth_q = [pieces(*quantise("wth0", round_two("wth0_bf", [("wth", 0, 0), ("wth", 1, 0)], nc.scalar.copy, "rounded"), 2 * PASS))]
-        page_bf = tile("page_bf", [P, 2, PACK * BANK], BF16, tag="wth_raw101")
+        page_bf = tile("page_bf", [P, 2, PACK * BANK], BF16)
+        page_q = []
         for h in range(2):
-            nc.scalar.copy(
-                out=page_bf[:, h].bitcast(U32).rearrange("p (c u) -> p c u", u=2),
-                in_=pairs[:, h].rearrange("p u c e -> p u (c e)").bitcast(U32).rearrange("p u c -> p c u"),
+            nc.vector.tensor_copy(
+                out=page_bf[:, h].bitcast(I32).rearrange("p (c u) -> p c u", u=2),
+                in_=pairs[:, h].rearrange("p u c e -> p u (c e)").bitcast(I32).rearrange("p u c -> p c u"),
             )
-        page_q = [quantise("page0", page_bf[:, 0], BANK)]
+        for h in range(2):
+            page_q.append(quantise("page%d" % h, page_bf[:, h], BANK))
+        early_bf = tile("early_bf", [P, 2, PACK * PASS], BF16)
+        for a in range(2):
+            round_on_scalar(early_bf[:, a], raws[("wth", a, 0)])
         v_codes = [gather_words(0)]
-        page_q.append(quantise("page1", page_bf[:, 1], BANK))
+        wth_q = [pieces(*quantise("wth0", early_bf[:].rearrange("p n c -> p (n c)"), 2 * PASS, offset=4 * ROW_BYTES))]
         a_rows = {}
 
         def project(i, which=(0, 1)):
             codes, scales = wp_q[i // PACK]
             cols = slice(P * (i % PACK), P * (i % PACK + 1))
             if i not in a_rows:
-                a_rows[i] = tile("a%d" % i, [P, T2], F32, tag="rows", bufs=ROW_BUFS)
+                if i < PACK:
+                    a_rows[i] = laid.tile([P, T2], F32, name="a%d" % i, align_bytes=64, offset=ROW_BYTES * i)
+                else:
+                    a_rows[i] = tile("a%d" % i, [P, T2], F32, tag="rows", bufs=ROW_BUFS)
             for h in which:
                 acc = bank("a_acc", "a", A_BANKS)
                 nc.tensor.matmul_mx(
@@ -227,15 +238,19 @@ def tile_list_ion_pulse_compensation_kernel(
             in_=wb_w[:].bitcast(U16).rearrange("p (b m t) -> p b t m", b=4, t=PACK),
         )
 
+        wp_q.append(quantise("wp1", wp_bf[1][:], PASS, codes_tag="wb_w"))
         z_q = [(tile("z_codes%d" % g, [P, S], U32), tile("z_scales%d" % g, [P, S], U8)) for g in range(2)]
-        first_terms = tile("first_terms", [P, 2, PACK, S], F32, tag="wth_raw111")
-        late_bf = tile("late_bf", [P, 2, PACK * PASS], BF16, tag="tab0")
-        terms_x = [first_terms[:, 0], tile("term_x1", [P, PACK, S], F32, tag="tab0")[:]]
-        terms_b = [first_terms[:, 1], tile("term_b1", [P, PACK, S], F32, tag="tab1")[:]]
+        late_bf = late[:, 9 * S : 13 * S].bitcast(BF16).rearrange("p (n c) -> p n c", n=2)
+        first_terms = tile("first_terms", [P, 2, PACK, S], F32, tag="wp_bf1")
+        terms_x = [
+            late[:, S : 13 * S].rearrange("p (t c) -> p t c", t=PACK)[:, :, 2 * S : 3 * S],
+            late[:, 9 * S : 13 * S].rearrange("p (t c) -> p t c", t=PACK),
+        ]
+        picked = [first_terms[:, 0, t] for t in range(PACK)] + [late[:, 8 * S : 9 * S]] + [terms_x[1][:, t] for t in range(1, PACK)]
+        terms_b = [first_terms[:, 1], tile("term_b1", [P, PACK, S], F32, tag="wp_bf1")[:]]
 
         def pick(i):
-            g, t = divmod(i, PACK)
-            nc.vector.tensor_copy(terms_x[g][:, t, :], a_rows[i][:].indirect(list3[:]))
+            nc.vector.tensor_copy(picked[i], a_rows[i][:].indirect(list3[:]))
 
         def weigh(i, j0, j1):
             g, t = divmod(i, PACK)
@@ -273,8 +288,8 @@ def tile_list_ion_pulse_compensation_kernel(
             return cosine
 
         def turn(i, cosine, j0, j1, engine):
-            x = terms_x[i // PACK][:, i % PACK, j0:j1]
-            engine.tensor_tensor(x, x, cosine[:, j0:j1], MULT)
+            g, t = divmod(i, PACK)
+            engine.tensor_tensor(terms_x[g][:, t, j0:j1], picked[i][:, j0:j1], cosine[:, j0:j1], MULT)
 
         def combine(g, j0, j1):
             z_bf = tile("z_bf", [P, PACK * (j1 - j0)], BF16, bufs=2)
@@ -284,12 +299,15 @@ def tile_list_ion_pulse_compensation_kernel(
                 terms_b[g][:, :, j0:j1].rearrange("p t (c i) -> p c t i", i=4),
                 ADD,
             )
+            return z_bf
+
+        def quantise_z(g, j0, j1, z_bf):
             codes, scales = z_q[g]
             nc.vector.quantize_mx(out=codes[:, j0:j1].bitcast(FP8X4), scales=scales[:, j0:j1], in_=z_bf[:])
 
         def control(j0, j1):
             width = j1 - j0
-            per_bank = BANK // width
+            per_bank = 2 if j1 == S else BANK // width
             for n0 in range(0, N // P, per_bank):
                 acc = bank("out_acc", "pair", PAIR_BANKS)
                 for g in range(2):
@@ -301,20 +319,13 @@ def tile_list_ion_pulse_compensation_kernel(
                             rhs=z_q[g][0][:, j0:j1].bitcast(FP8X4), rhs_scale=z_q[g][1][:, j0:j1],
                             start=(g == 0 and k == 0), stop=(g == 1 and k == per_bank - 1),
                         )
-                result = tile("result", [P, per_bank, width], F32, bufs=4)
-                copy = nc.vector.tensor_copy if j1 == S else nc.scalar.copy
-                copy(out=result[:].rearrange("p n j -> p (n j)"), in_=acc[:])
+                result = tile("result", [P, per_bank, width], F32, bufs=5)
+                copy = nc.vector.tensor_copy if j1 == S and n0 > 0 else nc.scalar.copy
+                copy(out=result[:].rearrange("p n j -> p (n j)"), in_=acc[:, 0 : per_bank * width])
                 nc.sync.dma_start(
                     out=out.rearrange("(n p) j -> p n j", p=P)[:, n0 : n0 + per_bank, j0:j1], in_=result[:]
                 )
 
-        def round_late(a):
-            for k in range(2):
-                round_weights(late_bf[:, a], halves[("wth", a, 1, k)], k * P // 2, nc.vector.tensor_copy)
-
-        round_late(0)
-        round_late(1)
-        wth_q.append(pieces(*quantise("wth1", late_bf[:].rearrange("p n c -> p (n c)"), 2 * PASS)))
         for t in range(PACK):
             project(t, (0,))
         project(0, (1,))
@@ -322,14 +333,18 @@ def tile_list_ion_pulse_compensation_kernel(
         for i in range(2 * PACK - 1):
             project(i + 1, (1,) if i + 1 < PACK else (0, 1))
             pick(i + 1)
-            turn(i, weigh(i, 0, S), 0, S, nc.gpsimd)
+            if i < 2:
+                round_on_gpsimd(late_bf[:, i], raws[("wth", i, 1)])
+            if i == 1:
+                wth_q.append(pieces(*quantise("wth1", late_bf.rearrange("p n c -> p (n c)"), 2 * PASS)))
             if i == PACK:
-                combine(0, 0, S)
+                first_z = combine(0, 0, S)
+            turn(i, weigh(i, 0, S), 0, S, nc.gpsimd)
         cuts = (0, 256, 384, 512)
         cosine = weigh(2 * PACK - 1, 0, S)
-        turn(2 * PACK - 1, cosine, 0, HALF, nc.gpsimd)
-        turn(2 * PACK - 1, cosine, HALF, S, nc.vector)
+        quantise_z(0, 0, S, first_z)
+        turn(2 * PACK - 1, cosine, 0, S, nc.vector)
         for c in range(len(cuts) - 1):
-            combine(1, cuts[c], cuts[c + 1])
+            quantise_z(1, cuts[c], cuts[c + 1], combine(1, cuts[c], cuts[c + 1]))
         for c in range(len(cuts) - 1):
             control(cuts[c], cuts[c + 1])

@@ -131,20 +131,11 @@ def tile_list_ion_pulse_compensation_kernel(
             nc.vector.quantize_mx(out=codes.bitcast(FP8X4), scales=scales[:], in_=rounded)
             return codes, scales[:]
 
-        def round_on_scalar(rounded, raw):
-            nc.scalar.copy(
+        def round_weights(rounded, raw, copy=nc.scalar.copy):
+            copy(
                 out=rounded.rearrange("p (t m k) -> p m k t", t=PACK, k=PACK),
                 in_=raw[:, :].rearrange("p k (m t) -> p m k t", t=PACK),
             )
-
-        def round_on_gpsimd(rounded, raw):
-            for half in range(2):
-                ms = slice(half * P // 2, (half + 1) * P // 2)
-                nc.gpsimd.tensor_scalar(
-                    rounded.rearrange("p (t m k) -> p m t k", t=PACK, k=PACK)[:, ms],
-                    raw[:, :].rearrange("p k (m t) -> p m t k", t=PACK)[:, ms],
-                    1.0, 0.0, MULT, ADD,
-                )
 
         wb_sc_ordered = tile("wb_sc_ordered", [P, 2 * H], U8)
         nc.vector.tensor_copy(
@@ -173,10 +164,10 @@ def tile_list_ion_pulse_compensation_kernel(
         wp_bf = [tile("wp_bf%d" % g, [P, PACK * PASS], BF16) for g in range(2)]
         for t in range(3):
             scatter(t)
-        round_on_scalar(wp_bf[0][:], raws[("wp", 0, 0)])
+        round_weights(wp_bf[0][:], raws[("wp", 0, 0)])
         wp_q = [quantise("wp0", wp_bf[0][:], PASS, codes_tag="new2")]
         scatter(3)
-        round_on_scalar(wp_bf[1][:], raws[("wp", 0, 1)])
+        round_weights(wp_bf[1][:], raws[("wp", 0, 1)])
         v_sc = tile("v_sc", [P, S], U8, tag="new3")
         nc.vector.tensor_copy(v_sc[:], tab_sc[:].indirect(list1[:]))
         nc.sync.dma_start(
@@ -187,9 +178,7 @@ def tile_list_ion_pulse_compensation_kernel(
             out=wb_w[:].bitcast(I32).rearrange("p (a c) -> p a c", a=2),
             in_=wb_words.bitcast(I32).rearrange("a p c -> p a c"),
         )
-        late = tile("late", [P, 13 * S], F32)
         for a in range(2):
-            raws[("wth", a, 1)] = late[:, PACK * PASS * a : PACK * PASS * (a + 1)].rearrange("p (t c) -> p t c", t=PACK)
             load_raw("wth", a, 1)
         wc_w = tile("wc_w", [P, 2 * N], U32)
         nc.sync.dma_start(
@@ -209,7 +198,7 @@ def tile_list_ion_pulse_compensation_kernel(
             page_q.append(quantise("page%d" % h, page_bf[:, h], BANK))
         early_bf = tile("early_bf", [P, 2, PACK * PASS], BF16)
         for a in range(2):
-            round_on_scalar(early_bf[:, a], raws[("wth", a, 0)])
+            round_weights(early_bf[:, a], raws[("wth", a, 0)])
         v_codes = [gather_words(0)]
         wth_q = [pieces(*quantise("wth0", early_bf[:].rearrange("p n c -> p (n c)"), 2 * PASS, offset=4 * ROW_BYTES))]
         a_rows = {}
@@ -240,17 +229,14 @@ def tile_list_ion_pulse_compensation_kernel(
 
         wp_q.append(quantise("wp1", wp_bf[1][:], PASS, codes_tag="wb_w"))
         z_q = [(tile("z_codes%d" % g, [P, S], U32), tile("z_scales%d" % g, [P, S], U8)) for g in range(2)]
-        late_bf = late[:, 9 * S : 13 * S].bitcast(BF16).rearrange("p (n c) -> p n c", n=2)
-        first_terms = tile("first_terms", [P, 2, PACK, S], F32, tag="wp_bf1")
-        terms_x = [
-            late[:, S : 13 * S].rearrange("p (t c) -> p t c", t=PACK)[:, :, 2 * S : 3 * S],
-            late[:, 9 * S : 13 * S].rearrange("p (t c) -> p t c", t=PACK),
-        ]
-        picked = [first_terms[:, 0, t] for t in range(PACK)] + [late[:, 8 * S : 9 * S]] + [terms_x[1][:, t] for t in range(1, PACK)]
-        terms_b = [first_terms[:, 1], tile("term_b1", [P, PACK, S], F32, tag="wp_bf1")[:]]
-
-        def pick(i):
-            nc.vector.tensor_copy(picked[i], a_rows[i][:].indirect(list3[:]))
+        late_bf = tile("late_bf", [P, 2, PACK * PASS], BF16, tag="early_bf")
+        for a in range(2):
+            round_weights(late_bf[:, a], raws[("wth", a, 1)], nc.vector.tensor_copy)
+        wth_q.append(pieces(*quantise("wth1", late_bf[:].rearrange("p n c -> p (n c)"), 2 * PASS)))
+        first_terms = tile("first_terms", [P, 2, PACK, S], F32, tag="wth_raw01")
+        last_terms = tile("last_terms", [P, PACK, S], F32, tag="early_bf")
+        terms_x = [first_terms[:, 0], last_terms[:]]
+        terms_b = [first_terms[:, 1], tile("term_b1", [P, PACK, S], F32, tag="wth_raw00")[:]]
 
         def weigh(i, j0, j1):
             g, t = divmod(i, PACK)
@@ -287,9 +273,11 @@ def tile_list_ion_pulse_compensation_kernel(
             nc.vector.tensor_tensor(terms_b[g][:, t, js], b[:, 0:width], sine[:], MULT)
             return cosine
 
-        def turn(i, cosine, j0, j1, engine):
+        def turn(i, cosine, j0, j1):
             g, t = divmod(i, PACK)
-            engine.tensor_tensor(terms_x[g][:, t, j0:j1], picked[i][:, j0:j1], cosine[:, j0:j1], MULT)
+            nc.vector.tensor_tensor(
+                terms_x[g][:, t, j0:j1], a_rows[i][:].indirect(list3[:, j0 // 16 : j1 // 16]), cosine[:, j0:j1], MULT
+            )
 
         def combine(g, j0, j1):
             z_bf = tile("z_bf", [P, PACK * (j1 - j0)], BF16, bufs=2)
@@ -329,22 +317,15 @@ def tile_list_ion_pulse_compensation_kernel(
         for t in range(PACK):
             project(t, (0,))
         project(0, (1,))
-        pick(0)
         for i in range(2 * PACK - 1):
             project(i + 1, (1,) if i + 1 < PACK else (0, 1))
-            pick(i + 1)
-            if i < 2:
-                round_on_gpsimd(late_bf[:, i], raws[("wth", i, 1)])
-            if i == 1:
-                wth_q.append(pieces(*quantise("wth1", late_bf.rearrange("p n c -> p (n c)"), 2 * PASS)))
             if i == PACK:
-                first_z = combine(0, 0, S)
-            turn(i, weigh(i, 0, S), 0, S, nc.gpsimd)
+                quantise_z(0, 0, S, combine(0, 0, S))
+            turn(i, weigh(i, 0, S), 0, S)
         cuts = (0, 256, 384, 512)
         cosine = weigh(2 * PACK - 1, 0, S)
-        quantise_z(0, 0, S, first_z)
-        turn(2 * PACK - 1, cosine, 0, S, nc.vector)
         for c in range(len(cuts) - 1):
+            turn(2 * PACK - 1, cosine, cuts[c], cuts[c + 1])
             quantise_z(1, cuts[c], cuts[c + 1], combine(1, cuts[c], cuts[c + 1]))
         for c in range(len(cuts) - 1):
             control(cuts[c], cuts[c + 1])

@@ -27,7 +27,7 @@ QUADRANTS = 4
 SHIFT_ROWS = 112
 
 ROW_BYTES = 4 * T2
-ROW_BUFS = 4
+ROW_BUFS = 8
 TRIG_BUFS = 4
 A_BANKS = 3
 PAIR_BANKS = 5
@@ -79,15 +79,12 @@ def tile_list_ion_pulse_compensation_kernel(
         def load_raw(name, a, g, planes=slice(0, PACK)):
             key = (name, a, g)
             if key not in raws:
-                if key == ("wth", 1, 0):
-                    raws[key] = laid.tile([P, PACK, PASS], F32, name="wth_raw10", align_bytes=64, offset=ROW_BYTES // 2)
-                else:
-                    raws[key] = tile("%s_raw%d%d" % key, [P, PACK, PASS], F32)
+                raws[key] = tile("%s_raw%d%d" % key, [P, PACK, PASS], F32)
             rows = {"wp": wp, "wth": wth}[name][PASS * a : PASS * (a + 1), PASS * g : PASS * (g + 1)]
             nc.sync.dma_start(out=raws[key][:, planes], in_=rows.rearrange("(p t) c -> p t c", t=PACK)[:, planes])
 
         def load_table(a):
-            words = laid.tile([P, T], U32, name="tab%d" % a, align_bytes=64, offset=ROW_BYTES * (4 + 2 * a))
+            words = laid.tile([P, T], U32, name="tab%d" % a, align_bytes=64, offset=4 * T * a)
             nc.sync.dma_start(
                 out=words[:].bitcast(I32),
                 in_=tab_words[a].rearrange("p t i -> p (t i)").bitcast(I32),
@@ -116,9 +113,10 @@ def tile_list_ion_pulse_compensation_kernel(
         planes = []
         for t in range(PACK):
             planes.append(load_plane(t))
-            load_raw("wp", 0, t // 2, slice(2 * (t % 2), 2 * (t % 2) + 2))
-        for a in range(2):
-            load_raw("wth", a, 0)
+            if t < 2:
+                load_raw("wp", 0, 0, slice(2 * t, 2 * t + 2))
+            else:
+                load_raw("wth", t - 2, 0)
         list3 = load_list("list3", offs3)
         tab = [load_table(a) for a in range(2)]
 
@@ -162,13 +160,11 @@ def tile_list_ion_pulse_compensation_kernel(
             return codes
 
         wp_bf = [tile("wp_bf%d" % g, [P, PACK * PASS], BF16) for g in range(2)]
-        for t in range(3):
-            scatter(t)
-        round_weights(wp_bf[0][:], raws[("wp", 0, 0)])
-        wp_q = [quantise("wp0", wp_bf[0][:], PASS, codes_tag="new2")]
-        scatter(3)
-        round_weights(wp_bf[1][:], raws[("wp", 0, 1)])
-        v_sc = tile("v_sc", [P, S], U8, tag="new3")
+        early_bf = tile("early_bf", [P, 2, PACK * PASS], BF16)
+        scatter(0)
+        scatter(1)
+        scatter(2)
+        v_sc = tile("v_sc", [P, S], U8, tag="new2")
         nc.vector.tensor_copy(v_sc[:], tab_sc[:].indirect(list1[:]))
         nc.sync.dma_start(
             out=v_sc_second[:].bitcast(I32)[0:SHIFT_ROWS, :], in_=v_sc[:].bitcast(I32)[4 : 4 + SHIFT_ROWS, :]
@@ -178,6 +174,7 @@ def tile_list_ion_pulse_compensation_kernel(
             out=wb_w[:].bitcast(I32).rearrange("p (a c) -> p a c", a=2),
             in_=wb_words.bitcast(I32).rearrange("a p c -> p a c"),
         )
+        load_raw("wp", 0, 1)
         for a in range(2):
             load_raw("wth", a, 1)
         wc_w = tile("wc_w", [P, 2 * N], U32)
@@ -187,30 +184,28 @@ def tile_list_ion_pulse_compensation_kernel(
         )
         load_scales(nc.sync, wc_sc, wc_scales)
 
-        page_bf = tile("page_bf", [P, 2, PACK * BANK], BF16)
-        page_q = []
-        for h in range(2):
-            nc.vector.tensor_copy(
-                out=page_bf[:, h].bitcast(I32).rearrange("p (c u) -> p c u", u=2),
-                in_=pairs[:, h].rearrange("p u c e -> p u (c e)").bitcast(I32).rearrange("p u c -> p c u"),
-            )
-        for h in range(2):
-            page_q.append(quantise("page%d" % h, page_bf[:, h], BANK))
-        early_bf = tile("early_bf", [P, 2, PACK * PASS], BF16)
+
+        round_weights(wp_bf[0][:], raws[("wp", 0, 0)])
+        wp_q = [quantise("wp0", wp_bf[0][:], PASS)]
+        scatter(3)
         for a in range(2):
             round_weights(early_bf[:, a], raws[("wth", a, 0)])
-        v_codes = [gather_words(0)]
-        wth_q = [pieces(*quantise("wth0", early_bf[:].rearrange("p n c -> p (n c)"), 2 * PASS, offset=4 * ROW_BYTES))]
+        page_bf = tile("page_bf", [P, 2, PACK * BANK], BF16, tag="wth_raw10")
+        for h in range(2):
+            nc.scalar.copy(
+                out=page_bf[:, h].bitcast(U32).rearrange("p (c u) -> p c u", u=2),
+                in_=pairs[:, h].rearrange("p u c e -> p u (c e)").bitcast(U32).rearrange("p u c -> p c u"),
+            )
+        v_codes = [gather_words(a) for a in range(2)]
+        wth_q = [pieces(*quantise("wth0", early_bf[:].rearrange("p n c -> p (n c)"), 2 * PASS, offset=4 * T))]
+        page_q = [quantise("page%d" % h, page_bf[:, h], BANK, offset=4 * (T + 2 * PASS + BANK * h)) for h in range(2)]
         a_rows = {}
 
         def project(i, which=(0, 1)):
             codes, scales = wp_q[i // PACK]
             cols = slice(P * (i % PACK), P * (i % PACK + 1))
             if i not in a_rows:
-                if i < PACK:
-                    a_rows[i] = laid.tile([P, T2], F32, name="a%d" % i, align_bytes=64, offset=ROW_BYTES * i)
-                else:
-                    a_rows[i] = tile("a%d" % i, [P, T2], F32, tag="rows", bufs=ROW_BUFS)
+                a_rows[i] = tile("a%d" % i, [P, T2], F32, tag="rows", bufs=ROW_BUFS)
             for h in which:
                 acc = bank("a_acc", "a", A_BANKS)
                 nc.tensor.matmul_mx(
@@ -220,14 +215,14 @@ def tile_list_ion_pulse_compensation_kernel(
                 )
                 nc.scalar.copy(out=a_rows[i][:, BANK * h : BANK * (h + 1)], in_=acc[:])
 
-        v_codes.append(gather_words(1))
         wb_ordered = tile("wb_ordered", [P, 2 * 2 * H], U8)
         nc.vector.tensor_copy(
             out=wb_ordered[:].bitcast(U16).rearrange("p (b t m) -> p b t m", b=4, t=PACK),
             in_=wb_w[:].bitcast(U16).rearrange("p (b m t) -> p b t m", b=4, t=PACK),
         )
 
-        wp_q.append(quantise("wp1", wp_bf[1][:], PASS, codes_tag="wb_w"))
+        round_weights(wp_bf[1][:], raws[("wp", 0, 1)], nc.vector.tensor_copy)
+        wp_q.append(quantise("wp1", wp_bf[1][:], PASS))
         z_q = [(tile("z_codes%d" % g, [P, S], U32), tile("z_scales%d" % g, [P, S], U8)) for g in range(2)]
         late_bf = tile("late_bf", [P, 2, PACK * PASS], BF16, tag="early_bf")
         for a in range(2):
@@ -314,14 +309,12 @@ def tile_list_ion_pulse_compensation_kernel(
                     out=out.rearrange("(n p) j -> p n j", p=P)[:, n0 : n0 + per_bank, j0:j1], in_=result[:]
                 )
 
-        for t in range(PACK):
-            project(t, (0,))
-        project(0, (1,))
+        project(0)
         for i in range(2 * PACK - 1):
-            project(i + 1, (1,) if i + 1 < PACK else (0, 1))
             if i == PACK:
                 quantise_z(0, 0, S, combine(0, 0, S))
             turn(i, weigh(i, 0, S), 0, S)
+            project(i + 1)
         cuts = (0, 256, 384, 512)
         cosine = weigh(2 * PACK - 1, 0, S)
         for c in range(len(cuts) - 1):

@@ -159,12 +159,13 @@ def tile_list_ion_pulse_compensation_kernel(
             nc.vector.tensor_copy(codes[:], tab[a][:].indirect(list1[:]))
             return codes
 
-        wp_bf = [tile("wp_bf%d" % g, [P, PACK * PASS], BF16) for g in range(2)]
+        wp_bf = tile("wp_bf", [P, PACK * PASS], BF16)
         early_bf = tile("early_bf", [P, 2, PACK * PASS], BF16)
         scatter(0)
         scatter(1)
         scatter(2)
-        v_sc = tile("v_sc", [P, S], U8, tag="new2")
+        round_weights(wp_bf[:], raws[("wp", 0, 0)])
+        v_sc = tile("v_sc", [P, S], U8, tag="wp_raw00")
         nc.vector.tensor_copy(v_sc[:], tab_sc[:].indirect(list1[:]))
         nc.sync.dma_start(
             out=v_sc_second[:].bitcast(I32)[0:SHIFT_ROWS, :], in_=v_sc[:].bitcast(I32)[4 : 4 + SHIFT_ROWS, :]
@@ -185,8 +186,7 @@ def tile_list_ion_pulse_compensation_kernel(
         load_scales(nc.sync, wc_sc, wc_scales)
 
 
-        round_weights(wp_bf[0][:], raws[("wp", 0, 0)])
-        wp_q = [quantise("wp0", wp_bf[0][:], PASS)]
+        wp_q = [quantise("wp0", wp_bf[:], PASS)]
         scatter(3)
         for a in range(2):
             round_weights(early_bf[:, a], raws[("wth", a, 0)])
@@ -197,8 +197,9 @@ def tile_list_ion_pulse_compensation_kernel(
                 in_=pairs[:, h].rearrange("p u c e -> p u (c e)").bitcast(U32).rearrange("p u c -> p c u"),
             )
         v_codes = [gather_words(a) for a in range(2)]
-        wth_q = [pieces(*quantise("wth0", early_bf[:].rearrange("p n c -> p (n c)"), 2 * PASS, offset=4 * T))]
-        page_q = [quantise("page%d" % h, page_bf[:, h], BANK, offset=4 * (T + 2 * PASS + BANK * h)) for h in range(2)]
+        page_q = [quantise("page0", page_bf[:, 0], BANK, offset=4 * T)]
+        wth_q = [pieces(*quantise("wth0", early_bf[:].rearrange("p n c -> p (n c)"), 2 * PASS, offset=4 * (T + BANK)))]
+        page_q.append(quantise("page1", page_bf[:, 1], BANK, offset=4 * (T + BANK + 2 * PASS)))
         a_rows = {}
 
         def project(i, which=(0, 1)):
@@ -221,31 +222,42 @@ def tile_list_ion_pulse_compensation_kernel(
             in_=wb_w[:].bitcast(U16).rearrange("p (b m t) -> p b t m", b=4, t=PACK),
         )
 
-        round_weights(wp_bf[1][:], raws[("wp", 0, 1)], nc.vector.tensor_copy)
-        wp_q.append(quantise("wp1", wp_bf[1][:], PASS))
-        z_q = [(tile("z_codes%d" % g, [P, S], U32), tile("z_scales%d" % g, [P, S], U8)) for g in range(2)]
         late_bf = tile("late_bf", [P, 2, PACK * PASS], BF16, tag="early_bf")
-        for a in range(2):
-            round_weights(late_bf[:, a], raws[("wth", a, 1)], nc.vector.tensor_copy)
-        wth_q.append(pieces(*quantise("wth1", late_bf[:].rearrange("p n c -> p (n c)"), 2 * PASS)))
+        for n, key in enumerate((("wp", 0, 1), ("wth", 0, 1))):
+            round_weights(late_bf[:, n], raws[key], nc.vector.tensor_copy)
+        late_q = pieces(*quantise("late", late_bf[:].rearrange("p n c -> p (n c)"), 2 * PASS))
+        wp_q.append(late_q[0])
+        z_q = [(tile("z_codes%d" % g, [P, S], U32), tile("z_scales%d" % g, [P, S], U8)) for g in range(2)]
+        last_bf = tile("last_bf", [P, PACK * PASS], BF16, tag="wp_bf")
+        round_weights(last_bf[:], raws[("wth", 1, 1)], nc.vector.tensor_copy)
+        wth_q.append([late_q[1], quantise("last", last_bf[:], PASS)])
         first_terms = tile("first_terms", [P, 2, PACK, S], F32, tag="wth_raw01")
         last_terms = tile("last_terms", [P, PACK, S], F32, tag="early_bf")
         terms_x = [first_terms[:, 0], last_terms[:]]
         terms_b = [first_terms[:, 1], tile("term_b1", [P, PACK, S], F32, tag="wth_raw00")[:]]
+
+        angles = {}
+
+        def angle(i):
+            g, t = divmod(i, PACK)
+            cols = slice(P * t, P * (t + 1))
+            angles[i] = th = bank("th", "pair", PAIR_BANKS)
+            for a in range(2):
+                codes, scales = wth_q[g][a]
+                nc.tensor.matmul_mx(
+                    out=th[:], lhsT=codes[:, cols].bitcast(FP8X4), lhsT_scale=scales[:, cols],
+                    rhs=v_codes[a][:].bitcast(FP8X4), rhs_scale=v_sc[4 * a : P, :],
+                    start=(a == 0), stop=(a == 1),
+                )
 
         def weigh(i, j0, j1):
             g, t = divmod(i, PACK)
             cols = slice(P * t, P * (t + 1))
             js = slice(j0, j1)
             width = j1 - j0
-            th = bank("th", "pair", PAIR_BANKS)
-            for a in range(2):
-                codes, scales = wth_q[g][a]
-                nc.tensor.matmul_mx(
-                    out=th[:, 0:width], lhsT=codes[:, cols].bitcast(FP8X4), lhsT_scale=scales[:, cols],
-                    rhs=v_codes[a][:, js].bitcast(FP8X4), rhs_scale=v_sc[4 * a : P, js],
-                    start=(a == 0), stop=(a == 1),
-                )
+            th = angles[i]
+            if i + 1 < 2 * PACK:
+                angle(i + 1)
             b = bank("b", "pair", PAIR_BANKS)
             step = width if width == S else P
             for s0 in range(0, width, step):
@@ -275,7 +287,7 @@ def tile_list_ion_pulse_compensation_kernel(
             )
 
         def combine(g, j0, j1):
-            z_bf = tile("z_bf", [P, PACK * (j1 - j0)], BF16, bufs=2)
+            z_bf = tile("z_bf", [P, PACK * (j1 - j0)], BF16, bufs=3)
             nc.vector.tensor_tensor(
                 z_bf[:].rearrange("p (c i t) -> p c t i", i=4, t=PACK),
                 terms_x[g][:, :, j0:j1].rearrange("p t (c i) -> p c t i", i=4),
@@ -309,16 +321,26 @@ def tile_list_ion_pulse_compensation_kernel(
                     out=out.rearrange("(n p) j -> p n j", p=P)[:, n0 : n0 + per_bank, j0:j1], in_=result[:]
                 )
 
-        project(0)
+        for i in range(A_BANKS):
+            project(i, (0,))
+        angle(0)
+        project(0, (1,))
         for i in range(2 * PACK - 1):
             if i == PACK:
                 quantise_z(0, 0, S, combine(0, 0, S))
             turn(i, weigh(i, 0, S), 0, S)
-            project(i + 1)
+            project(i + 1, (1,) if i + 1 < A_BANKS else (0, 1))
         cuts = (0, 256, 384, 512)
         cosine = weigh(2 * PACK - 1, 0, S)
-        for c in range(len(cuts) - 1):
-            turn(2 * PACK - 1, cosine, cuts[c], cuts[c + 1])
-            quantise_z(1, cuts[c], cuts[c + 1], combine(1, cuts[c], cuts[c + 1]))
+        last = 2 * PACK - 1
+        half, third, fourth = zip(cuts, cuts[1:])
+        turn(last, cosine, *half)
+        turn(last, cosine, *third)
+        z_half = combine(1, *half)
+        turn(last, cosine, *fourth)
+        quantise_z(1, *half, z_half)
+        z_rest = [combine(1, *cut) for cut in (third, fourth)]
+        for cut, z_bf in zip((third, fourth), z_rest):
+            quantise_z(1, *cut, z_bf)
         for c in range(len(cuts) - 1):
             control(cuts[c], cuts[c + 1])

@@ -165,17 +165,20 @@ def tile_list_ion_pulse_compensation_kernel(
         scatter(1)
         scatter(2)
         round_weights(wp_bf[:], raws[("wp", 0, 0)])
-        v_sc = tile("v_sc", [P, S], U8, tag="wp_raw00")
+        wp_q = [quantise("wp0", wp_bf[:], PASS)]
+        scatter(3)
+        round_weights(early_bf[:, 0], raws[("wth", 0, 0)])
+        v_sc = tile("v_sc", [P, S], U8, tag="wth_raw00")
         nc.vector.tensor_copy(v_sc[:], tab_sc[:].indirect(list1[:]))
-        nc.sync.dma_start(
-            out=v_sc_second[:].bitcast(I32)[0:SHIFT_ROWS, :], in_=v_sc[:].bitcast(I32)[4 : 4 + SHIFT_ROWS, :]
-        )
         wb_w = tile("wb_w", [P, 2 * 2 * H], U8)
         nc.sync.dma_start(
             out=wb_w[:].bitcast(I32).rearrange("p (a c) -> p a c", a=2),
             in_=wb_words.bitcast(I32).rearrange("a p c -> p a c"),
         )
         load_raw("wp", 0, 1)
+        nc.sync.dma_start(
+            out=v_sc_second[:].bitcast(I32)[0:SHIFT_ROWS, :], in_=v_sc[:].bitcast(I32)[4 : 4 + SHIFT_ROWS, :]
+        )
         for a in range(2):
             load_raw("wth", a, 1)
         wc_w = tile("wc_w", [P, 2 * N], U32)
@@ -186,20 +189,18 @@ def tile_list_ion_pulse_compensation_kernel(
         load_scales(nc.sync, wc_sc, wc_scales)
 
 
-        wp_q = [quantise("wp0", wp_bf[:], PASS)]
-        scatter(3)
-        for a in range(2):
-            round_weights(early_bf[:, a], raws[("wth", a, 0)])
+        round_weights(early_bf[:, 1], raws[("wth", 1, 0)])
         page_bf = tile("page_bf", [P, 2, PACK * BANK], BF16, tag="wth_raw10")
         for h in range(2):
             nc.scalar.copy(
                 out=page_bf[:, h].bitcast(U32).rearrange("p (c u) -> p c u", u=2),
                 in_=pairs[:, h].rearrange("p u c e -> p u (c e)").bitcast(U32).rearrange("p u c -> p c u"),
             )
-        v_codes = [gather_words(a) for a in range(2)]
-        page_q = [quantise("page0", page_bf[:, 0], BANK, offset=4 * T)]
-        wth_q = [pieces(*quantise("wth0", early_bf[:].rearrange("p n c -> p (n c)"), 2 * PASS, offset=4 * (T + BANK)))]
-        page_q.append(quantise("page1", page_bf[:, 1], BANK, offset=4 * (T + BANK + 2 * PASS)))
+        v_codes = [gather_words(0)]
+        page_q = [quantise("page0", page_bf[:, 0], BANK, offset=0)]
+        wth_q = [pieces(*quantise("wth0", early_bf[:].rearrange("p n c -> p (n c)"), 2 * PASS, offset=4 * BANK))]
+        page_q.append(quantise("page1", page_bf[:, 1], BANK, offset=4 * (BANK + 2 * PASS)))
+        v_codes.append(gather_words(1))
         a_rows = {}
 
         def project(i, which=(0, 1)):
@@ -234,7 +235,7 @@ def tile_list_ion_pulse_compensation_kernel(
         first_terms = tile("first_terms", [P, 2, PACK, S], F32, tag="wth_raw01")
         last_terms = tile("last_terms", [P, PACK, S], F32, tag="early_bf")
         terms_x = [first_terms[:, 0], last_terms[:]]
-        terms_b = [first_terms[:, 1], tile("term_b1", [P, PACK, S], F32, tag="wth_raw00")[:]]
+        terms_b = [first_terms[:, 1], tile("term_b1", [P, PACK, S], F32, tag="wp_raw00")[:]]
 
         angles = {}
 

@@ -159,6 +159,13 @@ def tile_list_ion_pulse_compensation_kernel(
             nc.vector.tensor_copy(codes[:], tab[a][:].indirect(list1[:]))
             return codes
 
+        def warm_up(acc, count):
+            for k in range(count):
+                nc.tensor.matmul_mx(
+                    out=acc[:], lhsT=wp_q[0][0][:, 0:P].bitcast(FP8X4), lhsT_scale=wp_q[0][1][:, 0:P],
+                    rhs=v_codes[0][:].bitcast(FP8X4), rhs_scale=v_sc[:], start=(k == 0), stop=(k == count - 1),
+                )
+
         wp_bf = tile("wp_bf", [P, PACK * PASS], BF16)
         early_bf = tile("early_bf", [P, 2, PACK * PASS], BF16)
         scatter(0)
@@ -197,6 +204,7 @@ def tile_list_ion_pulse_compensation_kernel(
                 in_=pairs[:, h].rearrange("p u c e -> p u (c e)").bitcast(U32).rearrange("p u c -> p c u"),
             )
         v_codes = [gather_words(0)]
+        warm_up(bank("warm", "pair", PAIR_BANKS), 2)
         page_q = [quantise("page0", page_bf[:, 0], BANK, offset=0)]
         wth_q = [pieces(*quantise("wth0", early_bf[:].rearrange("p n c -> p (n c)"), 2 * PASS, offset=4 * BANK))]
         page_q.append(quantise("page1", page_bf[:, 1], BANK, offset=4 * (BANK + 2 * PASS)))
@@ -306,6 +314,8 @@ def tile_list_ion_pulse_compensation_kernel(
             per_bank = 2 if j1 == S else BANK // width
             for n0 in range(0, N // P, per_bank):
                 acc = bank("out_acc", "pair", PAIR_BANKS)
+                if j1 == S and n0 > 0:
+                    warm_up(acc, 3)
                 for g in range(2):
                     for k in range(per_bank):
                         c0 = N * g + P * (n0 + k)

@@ -91,16 +91,16 @@ def tile_list_ion_pulse_compensation_kernel(
             )
             return words
 
-        wb_sc = zeroed("wb_sc", 2 * H, nc.gpsimd)
+        wb_sc = zeroed("wb_sc", 2 * H)
         list2 = load_list("list2", offs2)
         list1 = load_list("list1", offs)
-        load_scales(nc.sync, wb_sc, wb_scales)
+        load_scales(nc.scalar, wb_sc, wb_scales)
         angle_zero = tile("angle_zero", [P, 8], F32)
         nc.vector.memset(angle_zero[:], 0.0)
         zero = tile("zero", [P, 8], F32)
         nc.scalar.activation(zero[:], angle_zero[:], ACT.Sin)
 
-        tab_sc = zeroed("tab_sc", T)
+        tab_sc = zeroed("tab_sc", T, nc.gpsimd)
         v_sc_second = zeroed("v_sc_second", S)
         wc_sc = zeroed("wc_sc", 2 * N)
 
@@ -159,13 +159,6 @@ def tile_list_ion_pulse_compensation_kernel(
             nc.vector.tensor_copy(codes[:], tab[a][:].indirect(list1[:]))
             return codes
 
-        def warm_up(acc, count):
-            for k in range(count):
-                nc.tensor.matmul_mx(
-                    out=acc[:], lhsT=wp_q[0][0][:, 0:P].bitcast(FP8X4), lhsT_scale=wp_q[0][1][:, 0:P],
-                    rhs=v_codes[0][:].bitcast(FP8X4), rhs_scale=v_sc[:], start=(k == 0), stop=(k == count - 1),
-                )
-
         wp_bf = tile("wp_bf", [P, PACK * PASS], BF16)
         early_bf = tile("early_bf", [P, 2, PACK * PASS], BF16)
         scatter(0)
@@ -204,7 +197,6 @@ def tile_list_ion_pulse_compensation_kernel(
                 in_=pairs[:, h].rearrange("p u c e -> p u (c e)").bitcast(U32).rearrange("p u c -> p c u"),
             )
         v_codes = [gather_words(0)]
-        warm_up(bank("warm", "pair", PAIR_BANKS), 2)
         page_q = [quantise("page0", page_bf[:, 0], BANK, offset=0)]
         wth_q = [pieces(*quantise("wth0", early_bf[:].rearrange("p n c -> p (n c)"), 2 * PASS, offset=4 * BANK))]
         page_q.append(quantise("page1", page_bf[:, 1], BANK, offset=4 * (BANK + 2 * PASS)))
@@ -314,8 +306,6 @@ def tile_list_ion_pulse_compensation_kernel(
             per_bank = 2 if j1 == S else BANK // width
             for n0 in range(0, N // P, per_bank):
                 acc = bank("out_acc", "pair", PAIR_BANKS)
-                if j1 == S and n0 > 0:
-                    warm_up(acc, 3)
                 for g in range(2):
                     for k in range(per_bank):
                         c0 = N * g + P * (n0 + k)
@@ -341,17 +331,17 @@ def tile_list_ion_pulse_compensation_kernel(
                 quantise_z(0, 0, S, combine(0, 0, S))
             turn(i, weigh(i, 0, S), 0, S)
             project(i + 1, (1,) if i + 1 < A_BANKS else (0, 1))
-        cuts = (0, 256, 384, 512)
-        cosine = weigh(2 * PACK - 1, 0, S)
         last = 2 * PACK - 1
-        half, third, fourth = zip(cuts, cuts[1:])
-        turn(last, cosine, *half)
-        turn(last, cosine, *third)
-        z_half = combine(1, *half)
-        turn(last, cosine, *fourth)
-        quantise_z(1, *half, z_half)
-        z_rest = [combine(1, *cut) for cut in (third, fourth)]
-        for cut, z_bf in zip((third, fourth), z_rest):
-            quantise_z(1, *cut, z_bf)
-        for c in range(len(cuts) - 1):
-            control(cuts[c], cuts[c + 1])
+        cosine = weigh(last, 0, S)
+        quarters = [(j0, j0 + P) for j0 in range(0, S, P)]
+        turn(last, cosine, *quarters[0])
+        z_last = []
+        for n, cut in enumerate(quarters):
+            if n + 1 < len(quarters):
+                turn(last, cosine, *quarters[n + 1])
+            if n > 0:
+                quantise_z(1, *quarters[n - 1], z_last[-1])
+            z_last.append(combine(1, *cut))
+        quantise_z(1, *quarters[-1], z_last[-1])
+        for cut in quarters:
+            control(*cut)

@@ -22,15 +22,17 @@ P = 128
 PACK = 4
 PASS = P * PACK
 BANK = 512
-HALF = S // 2
+WORD = 4
 QUADRANTS = 4
-SHIFT_ROWS = 112
+SHIFT_ROWS = 32 * (QUADRANTS - 1) + 4
+TILES = 2 * PACK
 
-ROW_BYTES = 4 * T2
-ROW_BUFS = 8
+ROW_BUFS = PACK + PACK
 TRIG_BUFS = 4
 A_BANKS = 3
 PAIR_BANKS = 5
+Z_BUFS = 3
+RESULT_BUFS = 5
 
 
 def tile_list_ion_pulse_compensation_kernel(
@@ -46,6 +48,9 @@ def tile_list_ion_pulse_compensation_kernel(
 
         def tile(name, shape, dtype, tag=None, bufs=1):
             return sb.tile(shape, dtype, name=name, tag=tag or name, bufs=bufs, align_bytes=64)
+
+        def laid_words(name, width, first_word):
+            return laid.tile([P, width], U32, name=name, align_bytes=64, offset=WORD * first_word)
 
         def bank(name, tag, bufs):
             return ps.tile([P, BANK], F32, name=name, tag=tag, bufs=bufs)
@@ -76,15 +81,15 @@ def tile_list_ion_pulse_compensation_kernel(
 
         raws = {}
 
-        def load_raw(name, a, g, planes=slice(0, PACK)):
+        def load_raw(name, a, g, which=slice(0, PACK)):
             key = (name, a, g)
             if key not in raws:
                 raws[key] = tile("%s_raw%d%d" % key, [P, PACK, PASS], F32)
             rows = {"wp": wp, "wth": wth}[name][PASS * a : PASS * (a + 1), PASS * g : PASS * (g + 1)]
-            nc.sync.dma_start(out=raws[key][:, planes], in_=rows.rearrange("(p t) c -> p t c", t=PACK)[:, planes])
+            nc.sync.dma_start(out=raws[key][:, which], in_=rows.rearrange("(p t) c -> p t c", t=PACK)[:, which])
 
         def load_table(a):
-            words = laid.tile([P, T], U32, name="tab%d" % a, align_bytes=64, offset=4 * T * a)
+            words = laid_words("tab%d" % a, T, T * a)
             nc.sync.dma_start(
                 out=words[:].bitcast(I32),
                 in_=tab_words[a].rearrange("p t i -> p (t i)").bitcast(I32),
@@ -103,7 +108,6 @@ def tile_list_ion_pulse_compensation_kernel(
         tab_sc = zeroed("tab_sc", T, nc.gpsimd)
         v_sc_second = zeroed("v_sc_second", S)
         wc_sc = zeroed("wc_sc", 2 * N)
-
         for q in range(QUADRANTS):
             nc.gpsimd.dma_start(
                 out=tab_sc[:].bitcast(I32)[32 * q : 32 * q + 8, :],
@@ -120,26 +124,33 @@ def tile_list_ion_pulse_compensation_kernel(
         list3 = load_list("list3", offs3)
         tab = [load_table(a) for a in range(2)]
 
-        def quantise(name, rounded, width, codes_tag=None, codes=None, offset=None):
-            if offset is not None:
-                codes = laid.tile([P, width], U32, name=name + "_codes", align_bytes=64, offset=offset)[:]
-            if codes is None:
-                codes = tile(name + "_codes", [P, width], U32, tag=codes_tag)[:]
+        def quantise(name, rounded, width, first_word=None):
+            if first_word is None:
+                codes = tile(name + "_codes", [P, width], U32)
+            else:
+                codes = laid_words(name + "_codes", width, first_word)
             scales = tile(name + "_scales", [P, width], U8)
-            nc.vector.quantize_mx(out=codes.bitcast(FP8X4), scales=scales[:], in_=rounded)
-            return codes, scales[:]
+            nc.vector.quantize_mx(out=codes[:].bitcast(FP8X4), scales=scales[:], in_=rounded)
+            return codes[:], scales[:]
 
-        def round_weights(rounded, raw, copy=nc.scalar.copy):
+        def quantise_two(name, rounded, first_word=None):
+            codes, scales = quantise(name, rounded[:].rearrange("p n c -> p (n c)"), 2 * PASS, first_word)
+            return [(codes[:, PASS * n : PASS * (n + 1)], scales[:, PASS * n : PASS * (n + 1)]) for n in range(2)]
+
+        def round_weights(rounded, key, copy):
             copy(
                 out=rounded.rearrange("p (t m k) -> p m k t", t=PACK, k=PACK),
-                in_=raw[:, :].rearrange("p k (m t) -> p m k t", t=PACK),
+                in_=raws[key][:].rearrange("p k (m t) -> p m k t", t=PACK),
+            )
+
+        def order_columns(ordered, natural):
+            nc.vector.tensor_copy(
+                out=ordered.rearrange("p (b t m) -> p b t m", b=4, t=PACK),
+                in_=natural.rearrange("p (b m t) -> p b t m", b=4, t=PACK),
             )
 
         wb_sc_ordered = tile("wb_sc_ordered", [P, 2 * H], U8)
-        nc.vector.tensor_copy(
-            out=wb_sc_ordered[:].rearrange("p (b t m) -> p b t m", b=4, t=PACK),
-            in_=wb_sc[:].rearrange("p (b m t) -> p b t m", b=4, t=PACK),
-        )
+        order_columns(wb_sc_ordered[:], wb_sc[:])
 
         pairs = tile("pairs", [P, 2, 2, BANK, 2], BF16)
 
@@ -151,9 +162,6 @@ def tile_list_ion_pulse_compensation_kernel(
                     pairs[:, h, t // 2, :, t % 2], page[:, BANK * h : BANK * (h + 1)], 1.0, 0.0, MULT, ADD
                 )
 
-        def pieces(codes, scales):
-            return [(codes[:, PASS * n : PASS * (n + 1)], scales[:, PASS * n : PASS * (n + 1)]) for n in range(2)]
-
         def gather_words(a):
             codes = tile("v_codes%d" % a, [P, S], U32)
             nc.vector.tensor_copy(codes[:], tab[a][:].indirect(list1[:]))
@@ -161,15 +169,15 @@ def tile_list_ion_pulse_compensation_kernel(
 
         wp_bf = tile("wp_bf", [P, PACK * PASS], BF16)
         early_bf = tile("early_bf", [P, 2, PACK * PASS], BF16)
-        scatter(0)
-        scatter(1)
-        scatter(2)
-        round_weights(wp_bf[:], raws[("wp", 0, 0)])
+        for t in range(PACK - 1):
+            scatter(t)
+        round_weights(wp_bf[:], ("wp", 0, 0), nc.scalar.copy)
         wp_q = [quantise("wp0", wp_bf[:], PASS)]
-        scatter(3)
-        round_weights(early_bf[:, 0], raws[("wth", 0, 0)])
+        scatter(PACK - 1)
+        round_weights(early_bf[:, 0], ("wth", 0, 0), nc.scalar.copy)
         v_sc = tile("v_sc", [P, S], U8, tag="wth_raw00")
         nc.vector.tensor_copy(v_sc[:], tab_sc[:].indirect(list1[:]))
+
         wb_w = tile("wb_w", [P, 2 * 2 * H], U8)
         nc.sync.dma_start(
             out=wb_w[:].bitcast(I32).rearrange("p (a c) -> p a c", a=2),
@@ -188,8 +196,7 @@ def tile_list_ion_pulse_compensation_kernel(
         )
         load_scales(nc.sync, wc_sc, wc_scales)
 
-
-        round_weights(early_bf[:, 1], raws[("wth", 1, 0)])
+        round_weights(early_bf[:, 1], ("wth", 1, 0), nc.scalar.copy)
         page_bf = tile("page_bf", [P, 2, PACK * BANK], BF16, tag="wth_raw10")
         for h in range(2):
             nc.scalar.copy(
@@ -197,13 +204,31 @@ def tile_list_ion_pulse_compensation_kernel(
                 in_=pairs[:, h].rearrange("p u c e -> p u (c e)").bitcast(U32).rearrange("p u c -> p c u"),
             )
         v_codes = [gather_words(0)]
-        page_q = [quantise("page0", page_bf[:, 0], BANK, offset=0)]
-        wth_q = [pieces(*quantise("wth0", early_bf[:].rearrange("p n c -> p (n c)"), 2 * PASS, offset=4 * BANK))]
-        page_q.append(quantise("page1", page_bf[:, 1], BANK, offset=4 * (BANK + 2 * PASS)))
+        page_q = [quantise("page0", page_bf[:, 0], BANK, first_word=0)]
+        wth_q = [quantise_two("wth0", early_bf, first_word=BANK)]
+        page_q.append(quantise("page1", page_bf[:, 1], BANK, first_word=BANK + 2 * PASS))
         v_codes.append(gather_words(1))
-        a_rows = {}
 
-        def project(i, which=(0, 1)):
+        wb_ordered = tile("wb_ordered", [P, 2 * 2 * H], U8)
+        order_columns(wb_ordered[:].bitcast(U16), wb_w[:].bitcast(U16))
+
+        late_bf = tile("late_bf", [P, 2, PACK * PASS], BF16, tag="early_bf")
+        for n, key in enumerate((("wp", 0, 1), ("wth", 0, 1))):
+            round_weights(late_bf[:, n], key, nc.vector.tensor_copy)
+        late_q = quantise_two("late", late_bf)
+        wp_q.append(late_q[0])
+        z_q = [(tile("z_codes%d" % g, [P, S], U32), tile("z_scales%d" % g, [P, S], U8)) for g in range(2)]
+        last_bf = tile("last_bf", [P, PACK * PASS], BF16, tag="wp_bf")
+        round_weights(last_bf[:], ("wth", 1, 1), nc.vector.tensor_copy)
+        wth_q.append([late_q[1], quantise("last", last_bf[:], PASS)])
+
+        first_terms = tile("first_terms", [P, 2, PACK, S], F32, tag="wth_raw01")
+        last_terms = tile("last_terms", [P, PACK, S], F32, tag="early_bf")
+        terms_x = [first_terms[:, 0], last_terms[:]]
+        terms_b = [first_terms[:, 1], tile("term_b1", [P, PACK, S], F32, tag="wp_raw00")[:]]
+        a_rows, angles = {}, {}
+
+        def project(i, which):
             codes, scales = wp_q[i // PACK]
             cols = slice(P * (i % PACK), P * (i % PACK + 1))
             if i not in a_rows:
@@ -217,68 +242,38 @@ def tile_list_ion_pulse_compensation_kernel(
                 )
                 nc.scalar.copy(out=a_rows[i][:, BANK * h : BANK * (h + 1)], in_=acc[:])
 
-        wb_ordered = tile("wb_ordered", [P, 2 * 2 * H], U8)
-        nc.vector.tensor_copy(
-            out=wb_ordered[:].bitcast(U16).rearrange("p (b t m) -> p b t m", b=4, t=PACK),
-            in_=wb_w[:].bitcast(U16).rearrange("p (b m t) -> p b t m", b=4, t=PACK),
-        )
-
-        late_bf = tile("late_bf", [P, 2, PACK * PASS], BF16, tag="early_bf")
-        for n, key in enumerate((("wp", 0, 1), ("wth", 0, 1))):
-            round_weights(late_bf[:, n], raws[key], nc.vector.tensor_copy)
-        late_q = pieces(*quantise("late", late_bf[:].rearrange("p n c -> p (n c)"), 2 * PASS))
-        wp_q.append(late_q[0])
-        z_q = [(tile("z_codes%d" % g, [P, S], U32), tile("z_scales%d" % g, [P, S], U8)) for g in range(2)]
-        last_bf = tile("last_bf", [P, PACK * PASS], BF16, tag="wp_bf")
-        round_weights(last_bf[:], raws[("wth", 1, 1)], nc.vector.tensor_copy)
-        wth_q.append([late_q[1], quantise("last", last_bf[:], PASS)])
-        first_terms = tile("first_terms", [P, 2, PACK, S], F32, tag="wth_raw01")
-        last_terms = tile("last_terms", [P, PACK, S], F32, tag="early_bf")
-        terms_x = [first_terms[:, 0], last_terms[:]]
-        terms_b = [first_terms[:, 1], tile("term_b1", [P, PACK, S], F32, tag="wp_raw00")[:]]
-
-        angles = {}
-
         def angle(i):
             g, t = divmod(i, PACK)
             cols = slice(P * t, P * (t + 1))
-            angles[i] = th = bank("th", "pair", PAIR_BANKS)
+            angles[i] = bank("th", "pair", PAIR_BANKS)
             for a in range(2):
                 codes, scales = wth_q[g][a]
                 nc.tensor.matmul_mx(
-                    out=th[:], lhsT=codes[:, cols].bitcast(FP8X4), lhsT_scale=scales[:, cols],
+                    out=angles[i][:], lhsT=codes[:, cols].bitcast(FP8X4), lhsT_scale=scales[:, cols],
                     rhs=v_codes[a][:].bitcast(FP8X4), rhs_scale=v_sc[4 * a : P, :],
                     start=(a == 0), stop=(a == 1),
                 )
 
-        def weigh(i, j0, j1):
+        def weigh(i):
             g, t = divmod(i, PACK)
-            cols = slice(P * t, P * (t + 1))
-            js = slice(j0, j1)
-            width = j1 - j0
-            th = angles[i]
-            if i + 1 < 2 * PACK:
+            if i + 1 < TILES:
                 angle(i + 1)
             b = bank("b", "pair", PAIR_BANKS)
-            step = width if width == S else P
-            for s0 in range(0, width, step):
-                for a in range(2):
-                    c0 = H * a + P * i
-                    nc.tensor.matmul_mx(
-                        out=b[:, s0 : s0 + step],
-                        lhsT=wb_ordered[:, 2 * c0 : 2 * (c0 + P)].bitcast(FP4X4),
-                        lhsT_scale=wb_sc_ordered[:, c0 : c0 + P],
-                        rhs=v_codes[a][:, j0 + s0 : j0 + s0 + step].bitcast(FP8X4),
-                        rhs_scale=(v_sc, v_sc_second)[a][:, j0 + s0 : j0 + s0 + step],
-                        start=(a == 0), stop=(a == 1),
-                    )
-            size = tile("size", [P, width], F32, bufs=2)
-            sine = tile("sine", [P, width], F32, bufs=TRIG_BUFS)
-            cosine = tile("cosine", [P, width], F32, bufs=TRIG_BUFS)
-            nc.scalar.activation(sine[:], th[:, 0:width], ACT.Sin)
-            nc.scalar.activation(size[:], th[:, 0:width], ACT.Abs, bias=zero[:, 0:1])
+            for a in range(2):
+                c0 = H * a + P * i
+                nc.tensor.matmul_mx(
+                    out=b[:],
+                    lhsT=wb_ordered[:, 2 * c0 : 2 * (c0 + P)].bitcast(FP4X4), lhsT_scale=wb_sc_ordered[:, c0 : c0 + P],
+                    rhs=v_codes[a][:].bitcast(FP8X4), rhs_scale=(v_sc, v_sc_second)[a][:],
+                    start=(a == 0), stop=(a == 1),
+                )
+            size = tile("size", [P, S], F32, bufs=2)
+            sine = tile("sine", [P, S], F32, bufs=TRIG_BUFS)
+            cosine = tile("cosine", [P, S], F32, bufs=TRIG_BUFS)
+            nc.scalar.activation(sine[:], angles[i][:], ACT.Sin)
+            nc.scalar.activation(size[:], angles[i][:], ACT.Abs, bias=zero[:, 0:1])
             nc.scalar.activation(cosine[:], size[:], ACT.Sin, bias=math.pi / 2, scale=-1.0)
-            nc.vector.tensor_tensor(terms_b[g][:, t, js], b[:, 0:width], sine[:], MULT)
+            nc.vector.tensor_tensor(terms_b[g][:, t, :], b[:], sine[:], MULT)
             return cosine
 
         def turn(i, cosine, j0, j1):
@@ -288,7 +283,7 @@ def tile_list_ion_pulse_compensation_kernel(
             )
 
         def combine(g, j0, j1):
-            z_bf = tile("z_bf", [P, PACK * (j1 - j0)], BF16, bufs=3)
+            z_bf = tile("z_bf", [P, PACK * (j1 - j0)], BF16, bufs=Z_BUFS)
             nc.vector.tensor_tensor(
                 z_bf[:].rearrange("p (c i t) -> p c t i", i=4, t=PACK),
                 terms_x[g][:, :, j0:j1].rearrange("p t (c i) -> p c t i", i=4),
@@ -315,8 +310,8 @@ def tile_list_ion_pulse_compensation_kernel(
                             rhs=z_q[g][0][:, j0:j1].bitcast(FP8X4), rhs_scale=z_q[g][1][:, j0:j1],
                             start=(g == 0 and k == 0), stop=(g == 1 and k == per_bank - 1),
                         )
-                result = tile("result", [P, per_bank, width], F32, bufs=5)
-                copy = nc.vector.tensor_copy if j1 == S and n0 > 0 else nc.scalar.copy
+                result = tile("result", [P, per_bank, width], F32, bufs=RESULT_BUFS)
+                copy = nc.vector.tensor_copy if n0 > 0 else nc.scalar.copy
                 copy(out=result[:].rearrange("p n j -> p (n j)"), in_=acc[:, 0 : per_bank * width])
                 nc.sync.dma_start(
                     out=out.rearrange("(n p) j -> p n j", p=P)[:, n0 : n0 + per_bank, j0:j1], in_=result[:]
@@ -326,13 +321,14 @@ def tile_list_ion_pulse_compensation_kernel(
             project(i, (0,))
         angle(0)
         project(0, (1,))
-        for i in range(2 * PACK - 1):
+        last = TILES - 1
+        for i in range(last):
             if i == PACK:
                 quantise_z(0, 0, S, combine(0, 0, S))
-            turn(i, weigh(i, 0, S), 0, S)
+            turn(i, weigh(i), 0, S)
             project(i + 1, (1,) if i + 1 < A_BANKS else (0, 1))
-        last = 2 * PACK - 1
-        cosine = weigh(last, 0, S)
+
+        cosine = weigh(last)
         quarters = [(j0, j0 + P) for j0 in range(0, S, P)]
         turn(last, cosine, *quarters[0])
         z_last = []

@@ -25,12 +25,11 @@ BANK = 512
 WORD = 4
 QUADRANTS = 4
 SHIFT_ROWS = 32 * (QUADRANTS - 1) + 4
-TILES = 2 * PACK
+HALF = S // 2
 
 ROW_BUFS = PACK + PACK
 TRIG_BUFS = 4
-A_BANKS = 3
-PAIR_BANKS = 5
+RING = 4
 Z_BUFS = 3
 RESULT_BUFS = 5
 
@@ -143,23 +142,26 @@ def tile_list_ion_pulse_compensation_kernel(
                 in_=raws[key][:].rearrange("p k (m t) -> p m k t", t=PACK),
             )
 
-        def order_columns(ordered, natural):
-            nc.vector.tensor_copy(
+        def order_columns(ordered, natural, engine):
+            engine.tensor_copy(
                 out=ordered.rearrange("p (b t m) -> p b t m", b=4, t=PACK),
                 in_=natural.rearrange("p (b m t) -> p b t m", b=4, t=PACK),
             )
 
         wb_sc_ordered = tile("wb_sc_ordered", [P, 2 * H], U8)
-        order_columns(wb_sc_ordered[:], wb_sc[:])
+        order_columns(wb_sc_ordered[:], wb_sc[:], nc.gpsimd)
 
-        pairs = tile("pairs", [P, 2, 2, BANK, 2], BF16)
+        pairs = [
+            laid.tile([P, 2, BANK, 2], BF16, name="pairs%d" % h, align_bytes=64, offset=WORD * (2 * T + T2 * h))
+            for h in range(2)
+        ]
 
         def scatter(t):
             page, new = planes[t]
             nc.vector.tensor_copy(page[:].indirect(list2[:]), new[:])
             for h in range(2):
                 nc.gpsimd.tensor_scalar(
-                    pairs[:, h, t // 2, :, t % 2], page[:, BANK * h : BANK * (h + 1)], 1.0, 0.0, MULT, ADD
+                    pairs[h][:, t // 2, :, t % 2], page[:, BANK * h : BANK * (h + 1)], 1.0, 0.0, MULT, ADD
                 )
 
         def gather_words(a):
@@ -201,16 +203,16 @@ def tile_list_ion_pulse_compensation_kernel(
         for h in range(2):
             nc.scalar.copy(
                 out=page_bf[:, h].bitcast(U32).rearrange("p (c u) -> p c u", u=2),
-                in_=pairs[:, h].rearrange("p u c e -> p u (c e)").bitcast(U32).rearrange("p u c -> p c u"),
+                in_=pairs[h][:].rearrange("p u c e -> p u (c e)").bitcast(U32).rearrange("p u c -> p c u"),
             )
         v_codes = [gather_words(0)]
         page_q = [quantise("page0", page_bf[:, 0], BANK, first_word=0)]
-        wth_q = [quantise_two("wth0", early_bf, first_word=BANK)]
-        page_q.append(quantise("page1", page_bf[:, 1], BANK, first_word=BANK + 2 * PASS))
+        wth_q = [quantise_two("wth0", early_bf, first_word=2 * T)]
+        page_q.append(quantise("page1", page_bf[:, 1], BANK, first_word=BANK))
         v_codes.append(gather_words(1))
 
         wb_ordered = tile("wb_ordered", [P, 2 * 2 * H], U8)
-        order_columns(wb_ordered[:].bitcast(U16), wb_w[:].bitcast(U16))
+        order_columns(wb_ordered[:].bitcast(U16), wb_w[:].bitcast(U16), nc.vector)
 
         late_bf = tile("late_bf", [P, 2, PACK * PASS], BF16, tag="early_bf")
         for n, key in enumerate((("wp", 0, 1), ("wth", 0, 1))):
@@ -234,7 +236,7 @@ def tile_list_ion_pulse_compensation_kernel(
             if i not in a_rows:
                 a_rows[i] = tile("a%d" % i, [P, T2], F32, tag="rows", bufs=ROW_BUFS)
             for h in which:
-                acc = bank("a_acc", "a", A_BANKS)
+                acc = bank("a_acc", "scalar", RING)
                 nc.tensor.matmul_mx(
                     out=acc[:], lhsT=codes[:, cols].bitcast(FP8X4), lhsT_scale=scales[:, cols],
                     rhs=page_q[h][0].bitcast(FP8X4), rhs_scale=page_q[h][1],
@@ -242,44 +244,61 @@ def tile_list_ion_pulse_compensation_kernel(
                 )
                 nc.scalar.copy(out=a_rows[i][:, BANK * h : BANK * (h + 1)], in_=acc[:])
 
-        def angle(i):
-            g, t = divmod(i, PACK)
-            cols = slice(P * t, P * (t + 1))
-            angles[i] = bank("th", "pair", PAIR_BANKS)
-            for a in range(2):
-                codes, scales = wth_q[g][a]
-                nc.tensor.matmul_mx(
-                    out=angles[i][:], lhsT=codes[:, cols].bitcast(FP8X4), lhsT_scale=scales[:, cols],
-                    rhs=v_codes[a][:].bitcast(FP8X4), rhs_scale=v_sc[4 * a : P, :],
-                    start=(a == 0), stop=(a == 1),
-                )
+        units = [(0, t, 1, 0, S) for t in range(PACK)]
+        units.extend((1, t0, 2, j0, j0 + HALF) for j0 in (0, HALF) for t0 in (0, 2))
 
-        def weigh(i):
-            g, t = divmod(i, PACK)
-            if i + 1 < TILES:
-                angle(i + 1)
-            b = bank("b", "pair", PAIR_BANKS)
-            for a in range(2):
-                c0 = H * a + P * i
-                nc.tensor.matmul_mx(
-                    out=b[:],
-                    lhsT=wb_ordered[:, 2 * c0 : 2 * (c0 + P)].bitcast(FP4X4), lhsT_scale=wb_sc_ordered[:, c0 : c0 + P],
-                    rhs=v_codes[a][:].bitcast(FP8X4), rhs_scale=(v_sc, v_sc_second)[a][:],
-                    start=(a == 0), stop=(a == 1),
-                )
+        def angle(u):
+            g, t0, n, j0, j1 = units[u]
+            angles[u] = bank("th", "scalar", RING)
+            for k in range(n):
+                cols = slice(P * (t0 + k), P * (t0 + k + 1))
+                for a in range(2):
+                    codes, scales = wth_q[g][a]
+                    nc.tensor.matmul_mx(
+                        out=angles[u][:, (j1 - j0) * k : (j1 - j0) * (k + 1)],
+                        lhsT=codes[:, cols].bitcast(FP8X4), lhsT_scale=scales[:, cols],
+                        rhs=v_codes[a][:, j0:j1].bitcast(FP8X4), rhs_scale=v_sc[4 * a : P, j0:j1],
+                        start=(a == 0), stop=(a == 1),
+                    )
+
+        def weigh(u, tiles=()):
+            g, t0, n, j0, j1 = units[u]
+            b = bank("b", "vector", RING)
+            for k in range(n):
+                for a in range(2):
+                    c0 = H * a + PASS * g + P * (t0 + k)
+                    nc.tensor.matmul_mx(
+                        out=b[:, (j1 - j0) * k : (j1 - j0) * (k + 1)],
+                        lhsT=wb_ordered[:, 2 * c0 : 2 * (c0 + P)].bitcast(FP4X4),
+                        lhsT_scale=wb_sc_ordered[:, c0 : c0 + P],
+                        rhs=v_codes[a][:, j0:j1].bitcast(FP8X4), rhs_scale=(v_sc, v_sc_second)[a][:, j0:j1],
+                        start=(a == 0), stop=(a == 1),
+                    )
             size = tile("size", [P, S], F32, bufs=2)
             sine = tile("sine", [P, S], F32, bufs=TRIG_BUFS)
             cosine = tile("cosine", [P, S], F32, bufs=TRIG_BUFS)
-            nc.scalar.activation(sine[:], angles[i][:], ACT.Sin)
-            nc.scalar.activation(size[:], angles[i][:], ACT.Abs, bias=zero[:, 0:1])
+            nc.scalar.activation(sine[:], angles[u][:], ACT.Sin)
+            nc.scalar.activation(size[:], angles[u][:], ACT.Abs, bias=zero[:, 0:1])
+            for i in tiles:
+                project(i, (0,))
             nc.scalar.activation(cosine[:], size[:], ACT.Sin, bias=math.pi / 2, scale=-1.0)
-            nc.vector.tensor_tensor(terms_b[g][:, t, :], b[:], sine[:], MULT)
+            for i in tiles:
+                project(i, (1,))
+            if u + 1 < len(units):
+                angle(u + 1)
+            nc.vector.tensor_tensor(
+                terms_b[g][:, t0 : t0 + n, j0:j1],
+                b[:].rearrange("p (k j) -> p k j", k=n), sine[:].rearrange("p (k j) -> p k j", k=n), MULT,
+            )
             return cosine
 
-        def turn(i, cosine, j0, j1):
-            g, t = divmod(i, PACK)
+        def turn(u, k, cosine, j0, j1):
+            g, t0, n, first, end = units[u]
+            c0 = (end - first) * k - first
             nc.vector.tensor_tensor(
-                terms_x[g][:, t, j0:j1], a_rows[i][:].indirect(list3[:, j0 // 16 : j1 // 16]), cosine[:, j0:j1], MULT
+                terms_x[g][:, t0 + k, j0:j1],
+                a_rows[PACK * g + t0 + k][:].indirect(list3[:, j0 // 16 : j1 // 16]),
+                cosine[:, c0 + j0 : c0 + j1], MULT,
             )
 
         def combine(g, j0, j1):
@@ -296,11 +315,10 @@ def tile_list_ion_pulse_compensation_kernel(
             codes, scales = z_q[g]
             nc.vector.quantize_mx(out=codes[:, j0:j1].bitcast(FP8X4), scales=scales[:, j0:j1], in_=z_bf[:])
 
-        def control(j0, j1):
+        def control(j0, j1, per_bank, copies):
             width = j1 - j0
-            per_bank = 2 if j1 == S else BANK // width
             for n0 in range(0, N // P, per_bank):
-                acc = bank("out_acc", "pair", PAIR_BANKS)
+                acc = bank("out_acc", "scalar", RING)
                 for g in range(2):
                     for k in range(per_bank):
                         c0 = N * g + P * (n0 + k)
@@ -311,33 +329,41 @@ def tile_list_ion_pulse_compensation_kernel(
                             start=(g == 0 and k == 0), stop=(g == 1 and k == per_bank - 1),
                         )
                 result = tile("result", [P, per_bank, width], F32, bufs=RESULT_BUFS)
-                copy = nc.vector.tensor_copy if n0 > 0 else nc.scalar.copy
+                copy = copies[n0 // per_bank]
                 copy(out=result[:].rearrange("p n j -> p (n j)"), in_=acc[:, 0 : per_bank * width])
                 nc.sync.dma_start(
                     out=out.rearrange("(n p) j -> p n j", p=P)[:, n0 : n0 + per_bank, j0:j1], in_=result[:]
                 )
 
-        for i in range(A_BANKS):
-            project(i, (0,))
+        for h in range(2):
+            for i in range(2):
+                project(i, (h,))
+        project(2, (0, 1))
         angle(0)
-        project(0, (1,))
-        last = TILES - 1
-        for i in range(last):
-            if i == PACK:
-                quantise_z(0, 0, S, combine(0, 0, S))
-            turn(i, weigh(i), 0, S)
-            project(i + 1, (1,) if i + 1 < A_BANKS else (0, 1))
+        for u in range(PACK):
+            turn(u, 0, weigh(u, (u + 2,) if u > 0 else ()), 0, S)
+        quantise_z(0, 0, S, combine(0, 0, S))
 
-        cosine = weigh(last)
-        quarters = [(j0, j0 + P) for j0 in range(0, S, P)]
-        turn(last, cosine, *quarters[0])
-        z_last = []
-        for n, cut in enumerate(quarters):
-            if n + 1 < len(quarters):
-                turn(last, cosine, *quarters[n + 1])
-            if n > 0:
-                quantise_z(1, *quarters[n - 1], z_last[-1])
-            z_last.append(combine(1, *cut))
-        quantise_z(1, *quarters[-1], z_last[-1])
-        for cut in quarters:
-            control(*cut)
+        cosine = weigh(PACK, (PACK + 2, PACK + 3))
+        for k in range(2):
+            turn(PACK, k, cosine, 0, HALF)
+        cosine = weigh(PACK + 1)
+        for k in range(2):
+            turn(PACK + 1, k, cosine, 0, HALF)
+        cosine = weigh(PACK + 2)
+        z_bf = combine(1, 0, HALF)
+        turn(PACK + 2, 0, cosine, HALF, S)
+        quantise_z(1, 0, HALF, z_bf)
+        turn(PACK + 2, 1, cosine, HALF, S)
+        cosine = weigh(PACK + 3)
+        control(0, HALF, 2, (nc.scalar.copy, nc.scalar.copy))
+        third, fourth = (HALF, HALF + P), (HALF + P, S)
+        for k in range(2):
+            turn(PACK + 3, k, cosine, *third)
+        turn(PACK + 3, 0, cosine, *fourth)
+        z_third = combine(1, *third)
+        turn(PACK + 3, 1, cosine, *fourth)
+        quantise_z(1, *third, z_third)
+        quantise_z(1, *fourth, combine(1, *fourth))
+        control(*third, 4, (nc.scalar.copy,))
+        control(*fourth, 2, (nc.scalar.copy, nc.vector.tensor_copy))

@@ -121,7 +121,13 @@ def tile_list_ion_pulse_compensation_kernel(
             else:
                 load_raw("wth", t - 2, 0)
         list3 = load_list("list3", offs3)
-        tab = [load_table(a) for a in range(2)]
+        tab = [load_table(0)]
+        wb_w = tile("wb_w", [P, 2 * 2 * H], U8)
+        nc.sync.dma_start(
+            out=wb_w[:].bitcast(I32).rearrange("p (a c) -> p a c", a=2),
+            in_=wb_words.bitcast(I32).rearrange("a p c -> p a c"),
+        )
+        tab.append(load_table(1))
 
         def quantise(name, rounded, width, first_word=None):
             if first_word is None:
@@ -142,14 +148,14 @@ def tile_list_ion_pulse_compensation_kernel(
                 in_=raws[key][:].rearrange("p k (m t) -> p m k t", t=PACK),
             )
 
-        def order_columns(ordered, natural, engine):
-            engine.tensor_copy(
-                out=ordered.rearrange("p (b t m) -> p b t m", b=4, t=PACK),
-                in_=natural.rearrange("p (b m t) -> p b t m", b=4, t=PACK),
+        def order_columns(ordered, natural, copy):
+            copy(
+                out=ordered.rearrange("p (b t m) -> p b t m", m=P, t=PACK),
+                in_=natural.rearrange("p (b m t) -> p b t m", m=P, t=PACK),
             )
 
         wb_sc_ordered = tile("wb_sc_ordered", [P, 2 * H], U8)
-        order_columns(wb_sc_ordered[:], wb_sc[:], nc.gpsimd)
+        order_columns(wb_sc_ordered[:], wb_sc[:], nc.gpsimd.tensor_copy)
 
         pairs = [
             laid.tile([P, 2, BANK, 2], BF16, name="pairs%d" % h, align_bytes=64, offset=WORD * (2 * T + T2 * h))
@@ -180,11 +186,6 @@ def tile_list_ion_pulse_compensation_kernel(
         v_sc = tile("v_sc", [P, S], U8, tag="wth_raw00")
         nc.vector.tensor_copy(v_sc[:], tab_sc[:].indirect(list1[:]))
 
-        wb_w = tile("wb_w", [P, 2 * 2 * H], U8)
-        nc.sync.dma_start(
-            out=wb_w[:].bitcast(I32).rearrange("p (a c) -> p a c", a=2),
-            in_=wb_words.bitcast(I32).rearrange("a p c -> p a c"),
-        )
         load_raw("wp", 0, 1)
         nc.sync.dma_start(
             out=v_sc_second[:].bitcast(I32)[0:SHIFT_ROWS, :], in_=v_sc[:].bitcast(I32)[4 : 4 + SHIFT_ROWS, :]
@@ -205,14 +206,15 @@ def tile_list_ion_pulse_compensation_kernel(
                 out=page_bf[:, h].bitcast(U32).rearrange("p (c u) -> p c u", u=2),
                 in_=pairs[h][:].rearrange("p u c e -> p u (c e)").bitcast(U32).rearrange("p u c -> p c u"),
             )
+        wb_ordered = tile("wb_ordered", [P, 2 * 2 * H], U8)
+        order_columns(wb_ordered[:].bitcast(U16)[:, 0:H], wb_w[:].bitcast(U16)[:, 0:H], nc.scalar.copy)
         v_codes = [gather_words(0)]
         page_q = [quantise("page0", page_bf[:, 0], BANK, first_word=0)]
         wth_q = [quantise_two("wth0", early_bf, first_word=2 * T)]
         page_q.append(quantise("page1", page_bf[:, 1], BANK, first_word=BANK))
         v_codes.append(gather_words(1))
 
-        wb_ordered = tile("wb_ordered", [P, 2 * 2 * H], U8)
-        order_columns(wb_ordered[:].bitcast(U16), wb_w[:].bitcast(U16), nc.vector)
+        order_columns(wb_ordered[:].bitcast(U16)[:, H:], wb_w[:].bitcast(U16)[:, H:], nc.vector.tensor_copy)
 
         late_bf = tile("late_bf", [P, 2, PACK * PASS], BF16, tag="early_bf")
         for n, key in enumerate((("wp", 0, 1), ("wth", 0, 1))):
@@ -245,7 +247,8 @@ def tile_list_ion_pulse_compensation_kernel(
                 nc.scalar.copy(out=a_rows[i][:, BANK * h : BANK * (h + 1)], in_=acc[:])
 
         units = [(0, t, 1, 0, S) for t in range(PACK)]
-        units.extend((1, t0, 2, j0, j0 + HALF) for j0 in (0, HALF) for t0 in (0, 2))
+        units.extend((1, t0, 2, 0, HALF) for t0 in (0, 2))
+        units.extend((1, 0, PACK, j0, j0 + P) for j0 in (HALF, HALF + P))
 
         def angle(u):
             g, t0, n, j0, j1 = units[u]
@@ -350,20 +353,20 @@ def tile_list_ion_pulse_compensation_kernel(
         cosine = weigh(PACK + 1)
         for k in range(2):
             turn(PACK + 1, k, cosine, 0, HALF)
+        third, fourth = (HALF, HALF + P), (HALF + P, S)
         cosine = weigh(PACK + 2)
         z_bf = combine(1, 0, HALF)
-        turn(PACK + 2, 0, cosine, HALF, S)
+        turn(PACK + 2, 0, cosine, *third)
         quantise_z(1, 0, HALF, z_bf)
-        turn(PACK + 2, 1, cosine, HALF, S)
+        for k in range(1, PACK):
+            turn(PACK + 2, k, cosine, *third)
         cosine = weigh(PACK + 3)
         control(0, HALF, 2, (nc.scalar.copy, nc.scalar.copy))
-        third, fourth = (HALF, HALF + P), (HALF + P, S)
-        for k in range(2):
-            turn(PACK + 3, k, cosine, *third)
+        z_bf = combine(1, *third)
         turn(PACK + 3, 0, cosine, *fourth)
-        z_third = combine(1, *third)
-        turn(PACK + 3, 1, cosine, *fourth)
-        quantise_z(1, *third, z_third)
+        quantise_z(1, *third, z_bf)
+        for k in range(1, PACK):
+            turn(PACK + 3, k, cosine, *fourth)
         quantise_z(1, *fourth, combine(1, *fourth))
         control(*third, 4, (nc.scalar.copy,))
         control(*fourth, 2, (nc.scalar.copy, nc.vector.tensor_copy))

@@ -27,6 +27,7 @@ QUADRANTS = 4
 SHIFT_ROWS = 32 * (QUADRANTS - 1) + 4
 HALF = S // 2
 
+LAST_CUTS = ((0, BANK // 2), (BANK // 2, BANK), (BANK, T2))
 ROW_BUFS = PACK + PACK
 TRIG_BUFS = 4
 RING = 4
@@ -121,13 +122,12 @@ def tile_list_ion_pulse_compensation_kernel(
             else:
                 load_raw("wth", t - 2, 0)
         list3 = load_list("list3", offs3)
-        tab = [load_table(0)]
+        tab = [load_table(a) for a in range(2)]
         wb_w = tile("wb_w", [P, 2 * 2 * H], U8)
         nc.sync.dma_start(
             out=wb_w[:].bitcast(I32).rearrange("p (a c) -> p a c", a=2),
             in_=wb_words.bitcast(I32).rearrange("a p c -> p a c"),
         )
-        tab.append(load_table(1))
 
         def quantise(name, rounded, width, first_word=None):
             if first_word is None:
@@ -165,9 +165,10 @@ def tile_list_ion_pulse_compensation_kernel(
         def scatter(t):
             page, new = planes[t]
             nc.vector.tensor_copy(page[:].indirect(list2[:]), new[:])
-            for h in range(2):
+            for c0, c1 in LAST_CUTS if t == PACK - 1 else ((0, BANK), (BANK, T2)):
+                h = c0 // BANK
                 nc.gpsimd.tensor_scalar(
-                    pairs[h][:, t // 2, :, t % 2], page[:, BANK * h : BANK * (h + 1)], 1.0, 0.0, MULT, ADD
+                    pairs[h][:, t // 2, c0 - BANK * h : c1 - BANK * h, t % 2], page[:, c0:c1], 1.0, 0.0, MULT, ADD
                 )
 
         def gather_words(a):
@@ -201,20 +202,21 @@ def tile_list_ion_pulse_compensation_kernel(
 
         round_weights(early_bf[:, 1], ("wth", 1, 0), nc.scalar.copy)
         page_bf = tile("page_bf", [P, 2, PACK * BANK], BF16, tag="wth_raw10")
-        for h in range(2):
+        for c0, c1 in LAST_CUTS:
+            h = c0 // BANK
+            cols = slice(c0 - BANK * h, c1 - BANK * h)
             nc.scalar.copy(
-                out=page_bf[:, h].bitcast(U32).rearrange("p (c u) -> p c u", u=2),
-                in_=pairs[h][:].rearrange("p u c e -> p u (c e)").bitcast(U32).rearrange("p u c -> p c u"),
+                out=page_bf[:, h].bitcast(U32).rearrange("p (c u) -> p c u", u=2)[:, cols],
+                in_=pairs[h][:].rearrange("p u c e -> p u (c e)").bitcast(U32).rearrange("p u c -> p c u")[:, cols],
             )
-        wb_ordered = tile("wb_ordered", [P, 2 * 2 * H], U8)
-        order_columns(wb_ordered[:].bitcast(U16)[:, 0:H], wb_w[:].bitcast(U16)[:, 0:H], nc.scalar.copy)
         v_codes = [gather_words(0)]
         page_q = [quantise("page0", page_bf[:, 0], BANK, first_word=0)]
         wth_q = [quantise_two("wth0", early_bf, first_word=2 * T)]
         page_q.append(quantise("page1", page_bf[:, 1], BANK, first_word=BANK))
         v_codes.append(gather_words(1))
 
-        order_columns(wb_ordered[:].bitcast(U16)[:, H:], wb_w[:].bitcast(U16)[:, H:], nc.vector.tensor_copy)
+        wb_ordered = tile("wb_ordered", [P, 2 * 2 * H], U8)
+        order_columns(wb_ordered[:].bitcast(U16), wb_w[:].bitcast(U16), nc.vector.tensor_copy)
 
         late_bf = tile("late_bf", [P, 2, PACK * PASS], BF16, tag="early_bf")
         for n, key in enumerate((("wp", 0, 1), ("wth", 0, 1))):
@@ -339,9 +341,8 @@ def tile_list_ion_pulse_compensation_kernel(
                 )
 
         for h in range(2):
-            for i in range(2):
+            for i in range(3):
                 project(i, (h,))
-        project(2, (0, 1))
         angle(0)
         for u in range(PACK):
             turn(u, 0, weigh(u, (u + 2,) if u > 0 else ()), 0, S)

@@ -123,11 +123,6 @@ def tile_list_ion_pulse_compensation_kernel(
                 load_raw("wth", t - 2, 0)
         list3 = load_list("list3", offs3)
         tab = [load_table(a) for a in range(2)]
-        wb_w = tile("wb_w", [P, 2 * 2 * H], U8)
-        nc.sync.dma_start(
-            out=wb_w[:].bitcast(I32).rearrange("p (a c) -> p a c", a=2),
-            in_=wb_words.bitcast(I32).rearrange("a p c -> p a c"),
-        )
 
         def quantise(name, rounded, width, first_word=None):
             if first_word is None:
@@ -187,10 +182,15 @@ def tile_list_ion_pulse_compensation_kernel(
         v_sc = tile("v_sc", [P, S], U8, tag="wth_raw00")
         nc.vector.tensor_copy(v_sc[:], tab_sc[:].indirect(list1[:]))
 
-        load_raw("wp", 0, 1)
+        wb_w = tile("wb_w", [P, 2 * 2 * H], U8)
+        nc.sync.dma_start(
+            out=wb_w[:].bitcast(I32).rearrange("p (a c) -> p a c", a=2),
+            in_=wb_words.bitcast(I32).rearrange("a p c -> p a c"),
+        )
         nc.sync.dma_start(
             out=v_sc_second[:].bitcast(I32)[0:SHIFT_ROWS, :], in_=v_sc[:].bitcast(I32)[4 : 4 + SHIFT_ROWS, :]
         )
+        load_raw("wp", 0, 1)
         for a in range(2):
             load_raw("wth", a, 1)
         wc_w = tile("wc_w", [P, 2 * N], U32)
@@ -218,17 +218,22 @@ def tile_list_ion_pulse_compensation_kernel(
         wb_ordered = tile("wb_ordered", [P, 2 * 2 * H], U8)
         order_columns(wb_ordered[:].bitcast(U16), wb_w[:].bitcast(U16), nc.vector.tensor_copy)
 
-        late_bf = tile("late_bf", [P, 2, PACK * PASS], BF16, tag="early_bf")
-        for n, key in enumerate((("wp", 0, 1), ("wth", 0, 1))):
-            round_weights(late_bf[:, n], key, nc.vector.tensor_copy)
-        late_q = quantise_two("late", late_bf)
-        wp_q.append(late_q[0])
         z_q = [(tile("z_codes%d" % g, [P, S], U32), tile("z_scales%d" % g, [P, S], U8)) for g in range(2)]
-        last_bf = tile("last_bf", [P, PACK * PASS], BF16, tag="wp_bf")
-        round_weights(last_bf[:], ("wth", 1, 1), nc.vector.tensor_copy)
-        wth_q.append([late_q[1], quantise("last", last_bf[:], PASS)])
+        wp_late_bf = tile("wp_late_bf", [P, PACK * PASS], BF16, tag="wp_bf")
+        round_weights(wp_late_bf[:], ("wp", 0, 1), nc.vector.tensor_copy)
+        late_bf = tile("late_bf", [P, 2, PACK * PASS], BF16, tag="early_bf")
 
-        first_terms = tile("first_terms", [P, 2, PACK, S], F32, tag="wth_raw01")
+        def late_work(u):
+            if u == 0:
+                wp_q.append(quantise("wp1", wp_late_bf[:], PASS))
+                round_weights(late_bf[:, 0], ("wth", 0, 1), nc.vector.tensor_copy)
+            if u == 1:
+                wth_q.append([quantise("wth01", late_bf[:, 0], PASS)])
+                round_weights(late_bf[:, 1], ("wth", 1, 1), nc.vector.tensor_copy)
+            if u == 2:
+                wth_q[1].append(quantise("wth11", late_bf[:, 1], PASS))
+
+        first_terms = tile("first_terms", [P, 2, PACK, S], F32, tag="wp_raw01")
         last_terms = tile("last_terms", [P, PACK, S], F32, tag="early_bf")
         terms_x = [first_terms[:, 0], last_terms[:]]
         terms_b = [first_terms[:, 1], tile("term_b1", [P, PACK, S], F32, tag="wp_raw00")[:]]
@@ -257,13 +262,13 @@ def tile_list_ion_pulse_compensation_kernel(
             angles[u] = bank("th", "scalar", RING)
             for k in range(n):
                 cols = slice(P * (t0 + k), P * (t0 + k + 1))
-                for a in range(2):
+                for a in (g, 1 - g):
                     codes, scales = wth_q[g][a]
                     nc.tensor.matmul_mx(
                         out=angles[u][:, (j1 - j0) * k : (j1 - j0) * (k + 1)],
                         lhsT=codes[:, cols].bitcast(FP8X4), lhsT_scale=scales[:, cols],
                         rhs=v_codes[a][:, j0:j1].bitcast(FP8X4), rhs_scale=v_sc[4 * a : P, j0:j1],
-                        start=(a == 0), stop=(a == 1),
+                        start=(a == g), stop=(a != g),
                     )
 
         def weigh(u, tiles=()):
@@ -284,17 +289,20 @@ def tile_list_ion_pulse_compensation_kernel(
             cosine = tile("cosine", [P, S], F32, bufs=TRIG_BUFS)
             nc.scalar.activation(sine[:], angles[u][:], ACT.Sin)
             nc.scalar.activation(size[:], angles[u][:], ACT.Abs, bias=zero[:, 0:1])
-            for i in tiles:
-                project(i, (0,))
-            nc.scalar.activation(cosine[:], size[:], ACT.Sin, bias=math.pi / 2, scale=-1.0)
-            for i in tiles:
-                project(i, (1,))
-            if u + 1 < len(units):
-                angle(u + 1)
             nc.vector.tensor_tensor(
                 terms_b[g][:, t0 : t0 + n, j0:j1],
                 b[:].rearrange("p (k j) -> p k j", k=n), sine[:].rearrange("p (k j) -> p k j", k=n), MULT,
             )
+            late_work(u)
+            for i in tiles[:1]:
+                project(i, (0,))
+            nc.scalar.activation(cosine[:], size[:], ACT.Sin, bias=math.pi / 2, scale=-1.0)
+            for i in tiles[:1]:
+                project(i, (1,))
+            for i in tiles[1:]:
+                project(i, (0, 1))
+            if u + 1 < len(units):
+                angle(u + 1)
             return cosine
 
         def turn(u, k, cosine, j0, j1):
@@ -341,14 +349,14 @@ def tile_list_ion_pulse_compensation_kernel(
                 )
 
         for h in range(2):
-            for i in range(3):
+            for i in range(2):
                 project(i, (h,))
         angle(0)
         for u in range(PACK):
-            turn(u, 0, weigh(u, (u + 2,) if u > 0 else ()), 0, S)
+            turn(u, 0, weigh(u, ((2,), (3,), (), (4, 5, 6))[u]), 0, S)
         quantise_z(0, 0, S, combine(0, 0, S))
 
-        cosine = weigh(PACK, (PACK + 2, PACK + 3))
+        cosine = weigh(PACK, (PACK + 3,))
         for k in range(2):
             turn(PACK, k, cosine, 0, HALF)
         cosine = weigh(PACK + 1)

@@ -28,6 +28,7 @@ SHIFT_ROWS = 32 * (QUADRANTS - 1) + 4
 HALF = S // 2
 
 LAST_CUTS = ((0, BANK // 2), (BANK // 2, BANK), (BANK, T2))
+EARLY_HALVES = (((2, 1),), ((3, 0), (3, 1)), ((4, 0), (4, 1)), ((5, 0), (5, 1), (6, 0), (6, 1)))
 ROW_BUFS = PACK + PACK
 TRIG_BUFS = 4
 RING = 4
@@ -97,8 +98,8 @@ def tile_list_ion_pulse_compensation_kernel(
             return words
 
         wb_sc = zeroed("wb_sc", 2 * H)
+        planes = [load_plane(0)]
         list2 = load_list("list2", offs2)
-        list1 = load_list("list1", offs)
         load_scales(nc.scalar, wb_sc, wb_scales)
         angle_zero = tile("angle_zero", [P, 8], F32)
         nc.vector.memset(angle_zero[:], 0.0)
@@ -114,12 +115,14 @@ def tile_list_ion_pulse_compensation_kernel(
                 in_=tab_scales.bitcast(I32)[:, 4 * q : 4 * q + 4, :],
             )
 
-        planes = []
         for t in range(PACK):
-            planes.append(load_plane(t))
-            if t < 2:
-                load_raw("wp", 0, 0, slice(2 * t, 2 * t + 2))
-            else:
+            if t > 0:
+                planes.append(load_plane(t))
+            if t == 1:
+                list1 = load_list("list1", offs)
+            if t in (1, 2):
+                load_raw("wp", 0, 0, slice(2 * t - 2, 2 * t))
+            if t >= 2:
                 load_raw("wth", t - 2, 0)
         list3 = load_list("list3", offs3)
         tab = [load_table(a) for a in range(2)]
@@ -271,9 +274,9 @@ def tile_list_ion_pulse_compensation_kernel(
                         start=(a == g), stop=(a != g),
                     )
 
-        def weigh(u, tiles=()):
+        def weigh(u, halves=()):
             g, t0, n, j0, j1 = units[u]
-            b = bank("b", "vector", RING)
+            b = bank("b", "vector" if u < PACK + 2 else "scalar", RING)
             for k in range(n):
                 for a in range(2):
                     c0 = H * a + PASS * g + P * (t0 + k)
@@ -294,13 +297,11 @@ def tile_list_ion_pulse_compensation_kernel(
                 b[:].rearrange("p (k j) -> p k j", k=n), sine[:].rearrange("p (k j) -> p k j", k=n), MULT,
             )
             late_work(u)
-            for i in tiles[:1]:
-                project(i, (0,))
+            for i, h in halves[:1]:
+                project(i, (h,))
             nc.scalar.activation(cosine[:], size[:], ACT.Sin, bias=math.pi / 2, scale=-1.0)
-            for i in tiles[:1]:
-                project(i, (1,))
-            for i in tiles[1:]:
-                project(i, (0, 1))
+            for i, h in halves[1:]:
+                project(i, (h,))
             if u + 1 < len(units):
                 angle(u + 1)
             return cosine
@@ -331,15 +332,16 @@ def tile_list_ion_pulse_compensation_kernel(
         def control(j0, j1, per_bank, copies):
             width = j1 - j0
             for n0 in range(0, N // P, per_bank):
-                acc = bank("out_acc", "scalar", RING)
-                for g in range(2):
+                acc = bank("out_acc", "scalar" if j1 == S else "vector", RING)
+                passes = (0, 1) if j1 == S else (1, 0)
+                for g in passes:
                     for k in range(per_bank):
                         c0 = N * g + P * (n0 + k)
                         nc.tensor.matmul_mx(
                             out=acc[:, width * k : width * (k + 1)],
                             lhsT=wc_w[:, c0 : c0 + P].bitcast(FP8X4), lhsT_scale=wc_sc[:, c0 : c0 + P],
                             rhs=z_q[g][0][:, j0:j1].bitcast(FP8X4), rhs_scale=z_q[g][1][:, j0:j1],
-                            start=(g == 0 and k == 0), stop=(g == 1 and k == per_bank - 1),
+                            start=(g == passes[0] and k == 0), stop=(g == passes[1] and k == per_bank - 1),
                         )
                 result = tile("result", [P, per_bank, width], F32, bufs=RESULT_BUFS)
                 copy = copies[n0 // per_bank]
@@ -348,15 +350,16 @@ def tile_list_ion_pulse_compensation_kernel(
                     out=out.rearrange("(n p) j -> p n j", p=P)[:, n0 : n0 + per_bank, j0:j1], in_=result[:]
                 )
 
-        for h in range(2):
-            for i in range(2):
-                project(i, (h,))
+        for i in range(3):
+            project(i, (0,))
+        for i in range(2):
+            project(i, (1,))
         angle(0)
         for u in range(PACK):
-            turn(u, 0, weigh(u, ((2,), (3,), (), (4, 5, 6))[u]), 0, S)
+            turn(u, 0, weigh(u, EARLY_HALVES[u]), 0, S)
         quantise_z(0, 0, S, combine(0, 0, S))
 
-        cosine = weigh(PACK, (PACK + 3,))
+        cosine = weigh(PACK, ((7, 0), (7, 1)))
         for k in range(2):
             turn(PACK, k, cosine, 0, HALF)
         cosine = weigh(PACK + 1)

@@ -28,7 +28,7 @@ SHIFT_ROWS = 32 * (QUADRANTS - 1) + 4
 HALF = S // 2
 
 LAST_CUTS = ((0, BANK // 2), (BANK // 2, BANK), (BANK, T2))
-EARLY_HALVES = (((2, 1),), ((3, 0), (3, 1)), ((4, 0), (4, 1)), ((5, 0), (5, 1), (6, 0), (6, 1)))
+EARLY_HALVES = (((1, 1), (2, 1)), ((3, 0), (3, 1)), ((4, 0), (4, 1)), ((5, 0),))
 ROW_BUFS = PACK + PACK
 TRIG_BUFS = 4
 RING = 4
@@ -61,8 +61,11 @@ def tile_list_ion_pulse_compensation_kernel(
             nc.sync.dma_start(offsets[:], src)
             return offsets
 
-        def zeroed(name, width, engine=nc.vector):
-            scales = tile(name, [P, width], U8)
+        def zeroed(name, width, engine=nc.vector, first_word=None):
+            if first_word is None:
+                scales = tile(name, [P, width], U8)
+            else:
+                scales = laid.tile([P, width], U8, name=name, align_bytes=64, offset=WORD * first_word)
             engine.memset(scales[:].bitcast(I32), 0)
             return scales
 
@@ -97,7 +100,7 @@ def tile_list_ion_pulse_compensation_kernel(
             )
             return words
 
-        wb_sc = zeroed("wb_sc", 2 * H)
+        wb_sc = zeroed("wb_sc", 2 * H, first_word=2 * T + T2 - HALF)
         planes = [load_plane(0)]
         list2 = load_list("list2", offs2)
         load_scales(nc.scalar, wb_sc, wb_scales)
@@ -135,10 +138,6 @@ def tile_list_ion_pulse_compensation_kernel(
             scales = tile(name + "_scales", [P, width], U8)
             nc.vector.quantize_mx(out=codes[:].bitcast(FP8X4), scales=scales[:], in_=rounded)
             return codes[:], scales[:]
-
-        def quantise_two(name, rounded, first_word=None):
-            codes, scales = quantise(name, rounded[:].rearrange("p n c -> p (n c)"), 2 * PASS, first_word)
-            return [(codes[:, PASS * n : PASS * (n + 1)], scales[:, PASS * n : PASS * (n + 1)]) for n in range(2)]
 
         def round_weights(rounded, key, copy):
             copy(
@@ -213,8 +212,9 @@ def tile_list_ion_pulse_compensation_kernel(
                 in_=pairs[h][:].rearrange("p u c e -> p u (c e)").bitcast(U32).rearrange("p u c -> p c u")[:, cols],
             )
         v_codes = [gather_words(0)]
+        wth_q = [[quantise("wth00", early_bf[:, 0], PASS, first_word=2 * BANK)]]
         page_q = [quantise("page0", page_bf[:, 0], BANK, first_word=0)]
-        wth_q = [quantise_two("wth0", early_bf, first_word=2 * T)]
+        wth_q[0].append(quantise("wth10", early_bf[:, 1], PASS, first_word=2 * T))
         page_q.append(quantise("page1", page_bf[:, 1], BANK, first_word=BANK))
         v_codes.append(gather_words(1))
 
@@ -233,13 +233,12 @@ def tile_list_ion_pulse_compensation_kernel(
             if u == 1:
                 wth_q.append([quantise("wth01", late_bf[:, 0], PASS)])
                 round_weights(late_bf[:, 1], ("wth", 1, 1), nc.vector.tensor_copy)
-            if u == 2:
-                wth_q[1].append(quantise("wth11", late_bf[:, 1], PASS))
+
 
         first_terms = tile("first_terms", [P, 2, PACK, S], F32, tag="wp_raw01")
         last_terms = tile("last_terms", [P, PACK, S], F32, tag="early_bf")
         terms_x = [first_terms[:, 0], last_terms[:]]
-        terms_b = [first_terms[:, 1], tile("term_b1", [P, PACK, S], F32, tag="wp_raw00")[:]]
+        terms_b = {(0, 0): first_terms[:, 1], (1, 0): tile("term_b1", [P, PACK, HALF], F32, tag="wp_raw00")[:]}
         a_rows, angles = {}, {}
 
         def project(i, which):
@@ -259,6 +258,9 @@ def tile_list_ion_pulse_compensation_kernel(
         units = [(0, t, 1, 0, S) for t in range(PACK)]
         units.extend((1, t0, 2, 0, HALF) for t0 in (0, 2))
         units.extend((1, 0, PACK, j0, j0 + P) for j0 in (HALF, HALF + P))
+
+        def held_word(u):
+            return (2 * T + T2, T, T + S)[u - PACK]
 
         def angle(u):
             g, t0, n, j0, j1 = units[u]
@@ -287,13 +289,19 @@ def tile_list_ion_pulse_compensation_kernel(
                         rhs=v_codes[a][:, j0:j1].bitcast(FP8X4), rhs_scale=(v_sc, v_sc_second)[a][:, j0:j1],
                         start=(a == 0), stop=(a == 1),
                     )
-            size = tile("size", [P, S], F32, bufs=2)
+            if PACK <= u < PACK + 3:
+                size = laid.tile([P, S], F32, name="size%d" % u, align_bytes=64, offset=WORD * held_word(u))
+            else:
+                size = tile("size", [P, S], F32, bufs=2)
             sine = tile("sine", [P, S], F32, bufs=TRIG_BUFS)
             cosine = tile("cosine", [P, S], F32, bufs=TRIG_BUFS)
             nc.scalar.activation(sine[:], angles[u][:], ACT.Sin)
             nc.scalar.activation(size[:], angles[u][:], ACT.Abs, bias=zero[:, 0:1])
+            if (g, j0) not in terms_b:
+                term = laid.tile([P, PACK, P], F32, name="term_b%d" % u, align_bytes=64, offset=WORD * held_word(u - 1))
+                terms_b[g, j0] = term[:]
             nc.vector.tensor_tensor(
-                terms_b[g][:, t0 : t0 + n, j0:j1],
+                terms_b[g, j0][:, t0 : t0 + n],
                 b[:].rearrange("p (k j) -> p k j", k=n), sine[:].rearrange("p (k j) -> p k j", k=n), MULT,
             )
             late_work(u)
@@ -316,11 +324,14 @@ def tile_list_ion_pulse_compensation_kernel(
             )
 
         def combine(g, j0, j1):
-            z_bf = tile("z_bf", [P, PACK * (j1 - j0)], BF16, bufs=Z_BUFS)
+            if g == 0:
+                z_bf = laid.tile([P, PACK * S], BF16, name="z_first", align_bytes=64, offset=WORD * held_word(PACK))
+            else:
+                z_bf = tile("z_bf", [P, PACK * (j1 - j0)], BF16, bufs=Z_BUFS)
             nc.vector.tensor_tensor(
                 z_bf[:].rearrange("p (c i t) -> p c t i", i=4, t=PACK),
                 terms_x[g][:, :, j0:j1].rearrange("p t (c i) -> p c t i", i=4),
-                terms_b[g][:, :, j0:j1].rearrange("p t (c i) -> p c t i", i=4),
+                terms_b[g, j0].rearrange("p t (c i) -> p c t i", i=4),
                 ADD,
             )
             return z_bf
@@ -352,16 +363,18 @@ def tile_list_ion_pulse_compensation_kernel(
 
         for i in range(3):
             project(i, (0,))
-        for i in range(2):
-            project(i, (1,))
+        project(0, (1,))
         angle(0)
         for u in range(PACK):
             turn(u, 0, weigh(u, EARLY_HALVES[u]), 0, S)
-        quantise_z(0, 0, S, combine(0, 0, S))
+            if u == 1:
+                wth_q[1].append(quantise("wth11", late_bf[:, 1], PASS))
 
-        cosine = weigh(PACK, ((7, 0), (7, 1)))
-        for k in range(2):
-            turn(PACK, k, cosine, 0, HALF)
+        cosine = weigh(PACK, ((5, 1), (6, 0), (6, 1), (7, 0), (7, 1)))
+        z_bf = combine(0, 0, S)
+        turn(PACK, 0, cosine, 0, HALF)
+        quantise_z(0, 0, S, z_bf)
+        turn(PACK, 1, cosine, 0, HALF)
         cosine = weigh(PACK + 1)
         for k in range(2):
             turn(PACK + 1, k, cosine, 0, HALF)

@@ -24,11 +24,11 @@ PASS = P * PACK
 BANK = 512
 WORD = 4
 QUADRANTS = 4
-SHIFT_ROWS = 32 * (QUADRANTS - 1) + 4
+SCALE_ROWS = K // 32
 HALF = S // 2
 
 LAST_CUTS = ((0, BANK // 2), (BANK // 2, BANK), (BANK, T2))
-EARLY_HALVES = (((1, 1), (2, 1)), ((3, 0), (3, 1)), ((4, 0), (4, 1)), ((5, 0),))
+EARLY_HALVES = (((0, 1), (1, 1)), ((2, 1), (3, 1)), ((4, 0), (4, 1)), ((5, 0),))
 ROW_BUFS = PACK + PACK
 TRIG_BUFS = 4
 RING = 4
@@ -100,39 +100,60 @@ def tile_list_ion_pulse_compensation_kernel(
             )
             return words
 
-        wb_sc = zeroed("wb_sc", 2 * H, first_word=2 * T + T2 - HALF)
+        list1 = load_list("list1", offs)
+        tab_sc = tile("tab_sc", [P, T], U8)
+        nc.sync.dma_start(
+            out=tab_sc[:].bitcast(I32)[0:SCALE_ROWS, :], in_=tab_scales.bitcast(I32).rearrange("a q c -> (a q) c")
+        )
+        for p0, p1 in ((SCALE_ROWS, 64), (64, P)):
+            nc.vector.memset(tab_sc[:].bitcast(I32)[p0:p1, :], 0)
+        picked_sc = tile("picked_sc", [P, S], U8)
+        nc.vector.tensor_copy(picked_sc[:], tab_sc[:].indirect(list1[:]))
+
         planes = [load_plane(0)]
         list2 = load_list("list2", offs2)
-        load_scales(nc.scalar, wb_sc, wb_scales)
         angle_zero = tile("angle_zero", [P, 8], F32)
         nc.vector.memset(angle_zero[:], 0.0)
         zero = tile("zero", [P, 8], F32)
         nc.scalar.activation(zero[:], angle_zero[:], ACT.Sin)
 
-        tab_sc = zeroed("tab_sc", T, nc.gpsimd)
-        v_sc_second = zeroed("v_sc_second", S)
+        wb_sc = zeroed("wb_sc", 2 * H, nc.gpsimd, first_word=2 * T + T2 - HALF)
+        load_scales(nc.gpsimd, wb_sc, wb_scales)
+        v_sc = zeroed("v_sc", 2 * S)
         wc_sc = zeroed("wc_sc", 2 * N)
-        for q in range(QUADRANTS):
-            nc.gpsimd.dma_start(
-                out=tab_sc[:].bitcast(I32)[32 * q : 32 * q + 8, :],
-                in_=tab_scales.bitcast(I32)[:, 4 * q : 4 * q + 4, :],
+
+        def place_scales(a, q):
+            row = 16 * a + 4 * q
+            nc.sync.dma_start(
+                out=v_sc[:, S * a : S * (a + 1)].bitcast(I32)[32 * q : 32 * q + 4, :],
+                in_=picked_sc[:].bitcast(I32)[row : row + 4, :],
             )
 
-        for t in range(PACK):
-            if t > 0:
-                planes.append(load_plane(t))
-            if t == 1:
-                list1 = load_list("list1", offs)
-            if t in (1, 2):
-                load_raw("wp", 0, 0, slice(2 * t - 2, 2 * t))
-            if t >= 2:
-                load_raw("wth", t - 2, 0)
-        list3 = load_list("list3", offs3)
-        tab = [load_table(a) for a in range(2)]
+        planes.append(load_plane(1))
+        load_raw("wp", 0, 0, slice(0, 2))
+        planes.append(load_plane(2))
+        place_scales(0, 0)
+        load_raw("wp", 0, 0, slice(2, 4))
+        place_scales(0, 1)
+        load_raw("wth", 0, 0)
+        place_scales(0, 2)
+        planes.append(load_plane(3))
+        place_scales(0, 3)
+        wb_w = tile("wb_w", [P, 2 * 2 * H], U8)
+        nc.sync.dma_start(
+            out=wb_w[:].bitcast(I32).rearrange("p (a c) -> p a c", a=2),
+            in_=wb_words.bitcast(I32).rearrange("a p c -> p a c"),
+        )
+        tab = [load_table(0)]
+        place_scales(1, 0)
+        tab.append(load_table(1))
+        place_scales(1, 1)
+        load_raw("wth", 1, 0)
+        place_scales(1, 2)
 
-        def quantise(name, rounded, width, first_word=None):
+        def quantise(name, rounded, width, first_word=None, tag=None):
             if first_word is None:
-                codes = tile(name + "_codes", [P, width], U32)
+                codes = tile(name + "_codes", [P, width], U32, tag=tag)
             else:
                 codes = laid_words(name + "_codes", width, first_word)
             scales = tile(name + "_scales", [P, width], U8)
@@ -181,18 +202,10 @@ def tile_list_ion_pulse_compensation_kernel(
         wp_q = [quantise("wp0", wp_bf[:], PASS)]
         scatter(PACK - 1)
         round_weights(early_bf[:, 0], ("wth", 0, 0), nc.scalar.copy)
-        v_sc = tile("v_sc", [P, S], U8, tag="wth_raw00")
-        nc.vector.tensor_copy(v_sc[:], tab_sc[:].indirect(list1[:]))
 
-        wb_w = tile("wb_w", [P, 2 * 2 * H], U8)
-        nc.sync.dma_start(
-            out=wb_w[:].bitcast(I32).rearrange("p (a c) -> p a c", a=2),
-            in_=wb_words.bitcast(I32).rearrange("a p c -> p a c"),
-        )
-        nc.sync.dma_start(
-            out=v_sc_second[:].bitcast(I32)[0:SHIFT_ROWS, :], in_=v_sc[:].bitcast(I32)[4 : 4 + SHIFT_ROWS, :]
-        )
+        place_scales(1, 3)
         load_raw("wp", 0, 1)
+        list3 = load_list("list3", offs3)
         for a in range(2):
             load_raw("wth", a, 1)
         wc_w = tile("wc_w", [P, 2 * N], U32)
@@ -202,8 +215,9 @@ def tile_list_ion_pulse_compensation_kernel(
         )
         load_scales(nc.sync, wc_sc, wc_scales)
 
-        round_weights(early_bf[:, 1], ("wth", 1, 0), nc.scalar.copy)
-        page_bf = tile("page_bf", [P, 2, PACK * BANK], BF16, tag="wth_raw10")
+        wb_ordered = tile("wb_ordered", [P, 2 * 2 * H], U8)
+        order_columns(wb_ordered[:].bitcast(U16), wb_w[:].bitcast(U16), nc.scalar.copy)
+        page_bf = tile("page_bf", [P, 2, PACK * BANK], BF16, tag="wb_w")
         for c0, c1 in LAST_CUTS:
             h = c0 // BANK
             cols = slice(c0 - BANK * h, c1 - BANK * h)
@@ -211,15 +225,13 @@ def tile_list_ion_pulse_compensation_kernel(
                 out=page_bf[:, h].bitcast(U32).rearrange("p (c u) -> p c u", u=2)[:, cols],
                 in_=pairs[h][:].rearrange("p u c e -> p u (c e)").bitcast(U32).rearrange("p u c -> p c u")[:, cols],
             )
+        wth_q = [[quantise("wth00", early_bf[:, 0], PASS)]]
         v_codes = [gather_words(0)]
-        wth_q = [[quantise("wth00", early_bf[:, 0], PASS, first_word=2 * BANK)]]
-        page_q = [quantise("page0", page_bf[:, 0], BANK, first_word=0)]
-        wth_q[0].append(quantise("wth10", early_bf[:, 1], PASS, first_word=2 * T))
-        page_q.append(quantise("page1", page_bf[:, 1], BANK, first_word=BANK))
         v_codes.append(gather_words(1))
-
-        wb_ordered = tile("wb_ordered", [P, 2 * 2 * H], U8)
-        order_columns(wb_ordered[:].bitcast(U16), wb_w[:].bitcast(U16), nc.vector.tensor_copy)
+        page_q = [quantise("page0", page_bf[:, 0], BANK, first_word=T)]
+        round_weights(early_bf[:, 1], ("wth", 1, 0), nc.vector.tensor_copy)
+        wth_q[0].append(quantise("wth10", early_bf[:, 1], PASS))
+        page_q.append(quantise("page1", page_bf[:, 1], BANK, tag="wth_raw10"))
 
         z_q = [(tile("z_codes%d" % g, [P, S], U32), tile("z_scales%d" % g, [P, S], U8)) for g in range(2)]
         wp_late_bf = tile("wp_late_bf", [P, PACK * PASS], BF16, tag="wp_bf")
@@ -247,7 +259,7 @@ def tile_list_ion_pulse_compensation_kernel(
             if i not in a_rows:
                 a_rows[i] = tile("a%d" % i, [P, T2], F32, tag="rows", bufs=ROW_BUFS)
             for h in which:
-                acc = bank("a_acc", "scalar", RING)
+                acc = bank("a_acc%d%d" % (i, h), "scalar", RING)
                 nc.tensor.matmul_mx(
                     out=acc[:], lhsT=codes[:, cols].bitcast(FP8X4), lhsT_scale=scales[:, cols],
                     rhs=page_q[h][0].bitcast(FP8X4), rhs_scale=page_q[h][1],
@@ -260,25 +272,25 @@ def tile_list_ion_pulse_compensation_kernel(
         units.extend((1, 0, PACK, j0, j0 + P) for j0 in (HALF, HALF + P))
 
         def held_word(u):
-            return (2 * T + T2, T, T + S)[u - PACK]
+            return (2 * T + T2, 0, S)[u - PACK]
 
         def angle(u):
             g, t0, n, j0, j1 = units[u]
-            angles[u] = bank("th", "scalar", RING)
+            angles[u] = bank("th%d" % u, "scalar", RING)
             for k in range(n):
                 cols = slice(P * (t0 + k), P * (t0 + k + 1))
-                for a in (g, 1 - g):
+                for a in (1, 0):
                     codes, scales = wth_q[g][a]
                     nc.tensor.matmul_mx(
                         out=angles[u][:, (j1 - j0) * k : (j1 - j0) * (k + 1)],
                         lhsT=codes[:, cols].bitcast(FP8X4), lhsT_scale=scales[:, cols],
-                        rhs=v_codes[a][:, j0:j1].bitcast(FP8X4), rhs_scale=v_sc[4 * a : P, j0:j1],
-                        start=(a == g), stop=(a != g),
+                        rhs=v_codes[a][:, j0:j1].bitcast(FP8X4), rhs_scale=v_sc[:, S * a + j0 : S * a + j1],
+                        start=(a == 1), stop=(a == 0),
                     )
 
         def weigh(u, halves=()):
             g, t0, n, j0, j1 = units[u]
-            b = bank("b", "vector" if u < PACK + 2 else "scalar", RING)
+            b = bank("b%d" % u, "vector" if u < PACK + 2 else "scalar", RING)
             for k in range(n):
                 for a in range(2):
                     c0 = H * a + PASS * g + P * (t0 + k)
@@ -286,7 +298,7 @@ def tile_list_ion_pulse_compensation_kernel(
                         out=b[:, (j1 - j0) * k : (j1 - j0) * (k + 1)],
                         lhsT=wb_ordered[:, 2 * c0 : 2 * (c0 + P)].bitcast(FP4X4),
                         lhsT_scale=wb_sc_ordered[:, c0 : c0 + P],
-                        rhs=v_codes[a][:, j0:j1].bitcast(FP8X4), rhs_scale=(v_sc, v_sc_second)[a][:, j0:j1],
+                        rhs=v_codes[a][:, j0:j1].bitcast(FP8X4), rhs_scale=v_sc[:, S * a + j0 : S * a + j1],
                         start=(a == 0), stop=(a == 1),
                     )
             if PACK <= u < PACK + 3:
@@ -325,7 +337,7 @@ def tile_list_ion_pulse_compensation_kernel(
 
         def combine(g, j0, j1):
             if g == 0:
-                z_bf = laid.tile([P, PACK * S], BF16, name="z_first", align_bytes=64, offset=WORD * held_word(PACK))
+                z_bf = tile("z_first", [P, PACK * S], BF16, tag="wp_bf")
             else:
                 z_bf = tile("z_bf", [P, PACK * (j1 - j0)], BF16, bufs=Z_BUFS)
             nc.vector.tensor_tensor(
@@ -361,9 +373,8 @@ def tile_list_ion_pulse_compensation_kernel(
                     out=out.rearrange("(n p) j -> p n j", p=P)[:, n0 : n0 + per_bank, j0:j1], in_=result[:]
                 )
 
-        for i in range(3):
+        for i in range(PACK):
             project(i, (0,))
-        project(0, (1,))
         angle(0)
         for u in range(PACK):
             turn(u, 0, weigh(u, EARLY_HALVES[u]), 0, S)

@@ -78,10 +78,13 @@ def tile_list_ion_pulse_compensation_kernel(
 
         def load_plane(t):
             page = tile("page%d" % t, [P, T2], F32, tag="rows", bufs=ROW_BUFS)
-            new = tile("new%d" % t, [P, S], F32)
             nc.sync.dma_start(out=page[:], in_=base.rearrange("(p t) c -> p t c", t=PACK)[:, t, :])
-            nc.sync.dma_start(out=new[:], in_=xs.rearrange("(p t) c -> p t c", t=PACK)[:, t, :])
-            return page, new
+            return page
+
+        def load_new(t0, t1):
+            new = tile("new%d" % t0, [P, t1 - t0, S], F32)
+            nc.sync.dma_start(out=new[:], in_=xs.rearrange("(p t) c -> p t c", t=PACK)[:, t0:t1, :])
+            return [new[:, t, :] for t in range(t1 - t0)]
 
         raws = {}
 
@@ -111,6 +114,7 @@ def tile_list_ion_pulse_compensation_kernel(
         nc.vector.tensor_copy(picked_sc[:], tab_sc[:].indirect(list1[:]))
 
         planes = [load_plane(0)]
+        news = load_new(0, 1)
         list2 = load_list("list2", offs2)
         angle_zero = tile("angle_zero", [P, 8], F32)
         nc.vector.memset(angle_zero[:], 0.0)
@@ -122,34 +126,32 @@ def tile_list_ion_pulse_compensation_kernel(
         v_sc = zeroed("v_sc", 2 * S)
         wc_sc = zeroed("wc_sc", 2 * N)
 
-        def place_scales(a, q):
+        def place_scales(queue, a, q):
             row = 16 * a + 4 * q
-            nc.sync.dma_start(
+            queue.dma_start(
                 out=v_sc[:, S * a : S * (a + 1)].bitcast(I32)[32 * q : 32 * q + 4, :],
                 in_=picked_sc[:].bitcast(I32)[row : row + 4, :],
             )
 
+        for q in range(QUADRANTS):
+            place_scales(nc.scalar, 0, q)
+
         planes.append(load_plane(1))
-        load_raw("wp", 0, 0, slice(0, 2))
+        news.extend(load_new(1, PACK - 1))
         planes.append(load_plane(2))
-        place_scales(0, 0)
-        load_raw("wp", 0, 0, slice(2, 4))
-        place_scales(0, 1)
+        load_raw("wp", 0, 0)
         load_raw("wth", 0, 0)
-        place_scales(0, 2)
         planes.append(load_plane(3))
-        place_scales(0, 3)
+        news.extend(load_new(PACK - 1, PACK))
         wb_w = tile("wb_w", [P, 2 * 2 * H], U8)
         nc.sync.dma_start(
             out=wb_w[:].bitcast(I32).rearrange("p (a c) -> p a c", a=2),
             in_=wb_words.bitcast(I32).rearrange("a p c -> p a c"),
         )
-        tab = [load_table(0)]
-        place_scales(1, 0)
-        tab.append(load_table(1))
-        place_scales(1, 1)
+        tab = [load_table(a) for a in range(2)]
         load_raw("wth", 1, 0)
-        place_scales(1, 2)
+        for q in range(QUADRANTS):
+            place_scales(nc.sync, 1, q)
 
         def quantise(name, rounded, width, first_word=None, tag=None):
             if first_word is None:
@@ -181,8 +183,8 @@ def tile_list_ion_pulse_compensation_kernel(
         ]
 
         def scatter(t):
-            page, new = planes[t]
-            nc.vector.tensor_copy(page[:].indirect(list2[:]), new[:])
+            page = planes[t]
+            nc.vector.tensor_copy(page[:].indirect(list2[:]), news[t])
             for c0, c1 in LAST_CUTS if t == PACK - 1 else ((0, BANK), (BANK, T2)):
                 h = c0 // BANK
                 nc.gpsimd.tensor_scalar(
@@ -195,15 +197,14 @@ def tile_list_ion_pulse_compensation_kernel(
             return codes
 
         wp_bf = tile("wp_bf", [P, PACK * PASS], BF16)
-        early_bf = tile("early_bf", [P, 2, PACK * PASS], BF16)
+        early_bf = tile("early_bf", [P, PACK * PASS], BF16)
         for t in range(PACK - 1):
             scatter(t)
         round_weights(wp_bf[:], ("wp", 0, 0), nc.scalar.copy)
         wp_q = [quantise("wp0", wp_bf[:], PASS)]
         scatter(PACK - 1)
-        round_weights(early_bf[:, 0], ("wth", 0, 0), nc.scalar.copy)
+        round_weights(early_bf[:], ("wth", 0, 0), nc.scalar.copy)
 
-        place_scales(1, 3)
         load_raw("wp", 0, 1)
         list3 = load_list("list3", offs3)
         for a in range(2):
@@ -217,21 +218,22 @@ def tile_list_ion_pulse_compensation_kernel(
 
         wb_ordered = tile("wb_ordered", [P, 2 * 2 * H], U8)
         order_columns(wb_ordered[:].bitcast(U16), wb_w[:].bitcast(U16), nc.scalar.copy)
-        page_bf = tile("page_bf", [P, 2, PACK * BANK], BF16, tag="wb_w")
+        page_bf = [tile("page_bf%d" % h, [P, PACK * BANK], BF16, tag=("wb_w", "wth_raw00")[h]) for h in range(2)]
         for c0, c1 in LAST_CUTS:
             h = c0 // BANK
             cols = slice(c0 - BANK * h, c1 - BANK * h)
             nc.scalar.copy(
-                out=page_bf[:, h].bitcast(U32).rearrange("p (c u) -> p c u", u=2)[:, cols],
+                out=page_bf[h][:].bitcast(U32).rearrange("p (c u) -> p c u", u=2)[:, cols],
                 in_=pairs[h][:].rearrange("p u c e -> p u (c e)").bitcast(U32).rearrange("p u c -> p c u")[:, cols],
             )
-        wth_q = [[quantise("wth00", early_bf[:, 0], PASS)]]
+        wth_q = [[quantise("wth00", early_bf[:], PASS)]]
         v_codes = [gather_words(0)]
         v_codes.append(gather_words(1))
-        page_q = [quantise("page0", page_bf[:, 0], BANK, first_word=T)]
-        round_weights(early_bf[:, 1], ("wth", 1, 0), nc.vector.tensor_copy)
-        wth_q[0].append(quantise("wth10", early_bf[:, 1], PASS))
-        page_q.append(quantise("page1", page_bf[:, 1], BANK, tag="wth_raw10"))
+        page_q = [quantise("page0", page_bf[0][:], BANK, first_word=T)]
+        second_bf = tile("second_bf", [P, PACK * PASS], BF16, tag="wb_w")
+        round_weights(second_bf[:], ("wth", 1, 0), nc.vector.tensor_copy)
+        wth_q[0].append(quantise("wth10", second_bf[:], PASS))
+        page_q.append(quantise("page1", page_bf[1][:], BANK, tag="wth_raw10"))
 
         z_q = [(tile("z_codes%d" % g, [P, S], U32), tile("z_scales%d" % g, [P, S], U8)) for g in range(2)]
         wp_late_bf = tile("wp_late_bf", [P, PACK * PASS], BF16, tag="wp_bf")

@@ -70,10 +70,10 @@ def tile_list_ion_pulse_compensation_kernel(
             return scales
 
         def load_scales(queue, scales, src):
-            for q in range(QUADRANTS):
+            for j in range(4):
                 queue.dma_start(
-                    out=scales[:].bitcast(I32)[32 * q : 32 * q + 4, :].rearrange("p (a c) -> p a c", a=2),
-                    in_=src.bitcast(I32)[:, 4 * q : 4 * q + 4, :].rearrange("a q c -> q a c"),
+                    out=scales[:].bitcast(I32)[j:P:32, :].rearrange("p (a c) -> p a c", a=2),
+                    in_=src.bitcast(I32)[:, j:16:4, :].rearrange("a q c -> q a c"),
                 )
 
         def load_plane(t):
@@ -122,25 +122,24 @@ def tile_list_ion_pulse_compensation_kernel(
         nc.scalar.activation(zero[:], angle_zero[:], ACT.Sin)
 
         wb_sc = zeroed("wb_sc", 2 * H, nc.gpsimd, first_word=2 * T + T2 - HALF)
-        load_scales(nc.gpsimd, wb_sc, wb_scales)
+        load_scales(nc.sync, wb_sc, wb_scales)
         v_sc = zeroed("v_sc", 2 * S)
         wc_sc = zeroed("wc_sc", 2 * N)
 
-        def place_scales(queue, a, q):
-            row = 16 * a + 4 * q
-            queue.dma_start(
-                out=v_sc[:, S * a : S * (a + 1)].bitcast(I32)[32 * q : 32 * q + 4, :],
-                in_=picked_sc[:].bitcast(I32)[row : row + 4, :],
+        def place_scales(a, j):
+            nc.sync.dma_start(
+                out=v_sc[:, S * a : S * (a + 1)].bitcast(I32)[j:P:32, :],
+                in_=picked_sc[:].bitcast(I32)[16 * a + j : 16 * (a + 1) : 4, :],
             )
 
-        for q in range(QUADRANTS):
-            place_scales(nc.scalar, 0, q)
 
         planes.append(load_plane(1))
         news.extend(load_new(1, PACK - 1))
         planes.append(load_plane(2))
         load_raw("wp", 0, 0)
+        place_scales(0, 0)
         load_raw("wth", 0, 0)
+        place_scales(0, 1)
         planes.append(load_plane(3))
         news.extend(load_new(PACK - 1, PACK))
         wb_w = tile("wb_w", [P, 2 * 2 * H], U8)
@@ -148,10 +147,13 @@ def tile_list_ion_pulse_compensation_kernel(
             out=wb_w[:].bitcast(I32).rearrange("p (a c) -> p a c", a=2),
             in_=wb_words.bitcast(I32).rearrange("a p c -> p a c"),
         )
-        tab = [load_table(a) for a in range(2)]
+        place_scales(0, 2)
+        tab = [load_table(0)]
+        place_scales(0, 3)
+        tab.append(load_table(1))
         load_raw("wth", 1, 0)
-        for q in range(QUADRANTS):
-            place_scales(nc.sync, 1, q)
+        for j in range(4):
+            place_scales(1, j)
 
         def quantise(name, rounded, width, first_word=None, tag=None):
             if first_word is None:
@@ -218,22 +220,22 @@ def tile_list_ion_pulse_compensation_kernel(
 
         wb_ordered = tile("wb_ordered", [P, 2 * 2 * H], U8)
         order_columns(wb_ordered[:].bitcast(U16), wb_w[:].bitcast(U16), nc.scalar.copy)
-        page_bf = [tile("page_bf%d" % h, [P, PACK * BANK], BF16, tag=("wb_w", "wth_raw00")[h]) for h in range(2)]
+        page_bf = tile("page_bf", [P, 2, PACK * BANK], BF16, tag="wb_w")
         for c0, c1 in LAST_CUTS:
             h = c0 // BANK
             cols = slice(c0 - BANK * h, c1 - BANK * h)
             nc.scalar.copy(
-                out=page_bf[h][:].bitcast(U32).rearrange("p (c u) -> p c u", u=2)[:, cols],
+                out=page_bf[:, h].bitcast(U32).rearrange("p (c u) -> p c u", u=2)[:, cols],
                 in_=pairs[h][:].rearrange("p u c e -> p u (c e)").bitcast(U32).rearrange("p u c -> p c u")[:, cols],
             )
         wth_q = [[quantise("wth00", early_bf[:], PASS)]]
         v_codes = [gather_words(0)]
         v_codes.append(gather_words(1))
-        page_q = [quantise("page0", page_bf[0][:], BANK, first_word=T)]
-        second_bf = tile("second_bf", [P, PACK * PASS], BF16, tag="wb_w")
+        page_q = [quantise("page0", page_bf[:, 0], BANK, first_word=T)]
+        second_bf = tile("second_bf", [P, PACK * PASS], BF16)
         round_weights(second_bf[:], ("wth", 1, 0), nc.vector.tensor_copy)
         wth_q[0].append(quantise("wth10", second_bf[:], PASS))
-        page_q.append(quantise("page1", page_bf[1][:], BANK, tag="wth_raw10"))
+        page_q.append(quantise("page1", page_bf[:, 1], BANK, tag="wth_raw10"))
 
         z_q = [(tile("z_codes%d" % g, [P, S], U32), tile("z_scales%d" % g, [P, S], U8)) for g in range(2)]
         wp_late_bf = tile("wp_late_bf", [P, PACK * PASS], BF16, tag="wp_bf")

@@ -24,13 +24,14 @@ PASS = P * PACK
 BANK = 512
 WORD = 4
 QUADRANTS = 4
-SCALE_ROWS = K // 32
+SHIFT_ROWS = 32 * (QUADRANTS - 1) + 4
+JOIN_WORD = 2 * T + 2 * T2
 HALF = S // 2
 
 LAST_CUTS = ((0, BANK // 2), (BANK // 2, BANK), (BANK, T2))
-EARLY_HALVES = (((0, 1), (1, 1)), ((2, 1), (3, 1)), ((4, 0), (4, 1)), ((5, 0),))
-ROW_BUFS = PACK + PACK
-TRIG_BUFS = 4
+EARLY_HALVES = (((3, 1),), (), (), ())
+ROW_BUFS = PACK + 2
+TRIG_BUFS = 6
 RING = 4
 Z_BUFS = 3
 RESULT_BUFS = 5
@@ -91,7 +92,10 @@ def tile_list_ion_pulse_compensation_kernel(
         def load_raw(name, a, g, which=slice(0, PACK)):
             key = (name, a, g)
             if key not in raws:
-                raws[key] = tile("%s_raw%d%d" % key, [P, PACK, PASS], F32)
+                if key == ("wth", 0, 0):
+                    raws[key] = laid.tile([P, PACK, PASS], F32, name="wth_raw00", align_bytes=64, offset=WORD * JOIN_WORD)
+                else:
+                    raws[key] = tile("%s_raw%d%d" % key, [P, PACK, PASS], F32)
             rows = {"wp": wp, "wth": wth}[name][PASS * a : PASS * (a + 1), PASS * g : PASS * (g + 1)]
             nc.sync.dma_start(out=raws[key][:, which], in_=rows.rearrange("(p t) c -> p t c", t=PACK)[:, which])
 
@@ -103,16 +107,6 @@ def tile_list_ion_pulse_compensation_kernel(
             )
             return words
 
-        list1 = load_list("list1", offs)
-        tab_sc = tile("tab_sc", [P, T], U8)
-        nc.sync.dma_start(
-            out=tab_sc[:].bitcast(I32)[0:SCALE_ROWS, :], in_=tab_scales.bitcast(I32).rearrange("a q c -> (a q) c")
-        )
-        for p0, p1 in ((SCALE_ROWS, 64), (64, P)):
-            nc.vector.memset(tab_sc[:].bitcast(I32)[p0:p1, :], 0)
-        picked_sc = tile("picked_sc", [P, S], U8)
-        nc.vector.tensor_copy(picked_sc[:], tab_sc[:].indirect(list1[:]))
-
         planes = [load_plane(0)]
         news = load_new(0, 1)
         list2 = load_list("list2", offs2)
@@ -121,39 +115,33 @@ def tile_list_ion_pulse_compensation_kernel(
         zero = tile("zero", [P, 8], F32)
         nc.scalar.activation(zero[:], angle_zero[:], ACT.Sin)
 
-        wb_sc = zeroed("wb_sc", 2 * H, nc.gpsimd, first_word=2 * T + T2 - HALF)
-        load_scales(nc.sync, wb_sc, wb_scales)
-        v_sc = zeroed("v_sc", 2 * S)
+        wb_sc = zeroed("wb_sc", 2 * H, nc.vector, first_word=2 * T + T2 - HALF)
+        tab_sc = zeroed("tab_sc", T, nc.gpsimd)
+        for q in range(QUADRANTS):
+            nc.gpsimd.dma_start(
+                out=tab_sc[:].bitcast(I32)[32 * q : 32 * q + 8, :],
+                in_=tab_scales.bitcast(I32)[:, 4 * q : 4 * q + 4, :],
+            )
+        v_sc_second = zeroed("v_sc_second", S)
         wc_sc = zeroed("wc_sc", 2 * N)
 
-        def place_scales(a, j):
-            nc.sync.dma_start(
-                out=v_sc[:, S * a : S * (a + 1)].bitcast(I32)[j:P:32, :],
-                in_=picked_sc[:].bitcast(I32)[16 * a + j : 16 * (a + 1) : 4, :],
-            )
-
-
         planes.append(load_plane(1))
-        news.extend(load_new(1, PACK - 1))
-        planes.append(load_plane(2))
-        load_raw("wp", 0, 0)
-        place_scales(0, 0)
-        load_raw("wth", 0, 0)
-        place_scales(0, 1)
-        planes.append(load_plane(3))
-        news.extend(load_new(PACK - 1, PACK))
+        news.extend(load_new(1, 2))
+        load_scales(nc.sync, wb_sc, wb_scales)
         wb_w = tile("wb_w", [P, 2 * 2 * H], U8)
         nc.sync.dma_start(
             out=wb_w[:].bitcast(I32).rearrange("p (a c) -> p a c", a=2),
             in_=wb_words.bitcast(I32).rearrange("a p c -> p a c"),
         )
-        place_scales(0, 2)
+        planes.append(load_plane(2))
+        news.extend(load_new(2, PACK))
+        load_raw("wp", 0, 0)
+        planes.append(load_plane(3))
+        load_raw("wth", 0, 0)
+        list1 = load_list("list1", offs)
         tab = [load_table(0)]
-        place_scales(0, 3)
         tab.append(load_table(1))
         load_raw("wth", 1, 0)
-        for j in range(4):
-            place_scales(1, j)
 
         def quantise(name, rounded, width, first_word=None, tag=None):
             if first_word is None:
@@ -164,10 +152,10 @@ def tile_list_ion_pulse_compensation_kernel(
             nc.vector.quantize_mx(out=codes[:].bitcast(FP8X4), scales=scales[:], in_=rounded)
             return codes[:], scales[:]
 
-        def round_weights(rounded, key, copy):
+        def round_weights(rounded, key, copy, part=slice(0, P)):
             copy(
-                out=rounded.rearrange("p (t m k) -> p m k t", t=PACK, k=PACK),
-                in_=raws[key][:].rearrange("p k (m t) -> p m k t", t=PACK),
+                out=rounded.rearrange("p (t m k) -> p m k t", t=PACK, k=PACK)[:, part],
+                in_=raws[key][:].rearrange("p k (m t) -> p m k t", t=PACK)[:, part],
             )
 
         def order_columns(ordered, natural, copy):
@@ -200,17 +188,23 @@ def tile_list_ion_pulse_compensation_kernel(
 
         wp_bf = tile("wp_bf", [P, PACK * PASS], BF16)
         early_bf = tile("early_bf", [P, PACK * PASS], BF16)
-        for t in range(PACK - 1):
+        for t in range(PACK):
             scatter(t)
+        wb_ordered = tile("wb_ordered", [P, 2 * 2 * H], U8)
+        order_columns(wb_ordered[:].bitcast(U16), wb_w[:].bitcast(U16), nc.scalar.copy)
         round_weights(wp_bf[:], ("wp", 0, 0), nc.scalar.copy)
         wp_q = [quantise("wp0", wp_bf[:], PASS)]
-        scatter(PACK - 1)
         round_weights(early_bf[:], ("wth", 0, 0), nc.scalar.copy)
 
-        load_raw("wp", 0, 1)
+        v_sc = tile("v_sc", [P, S], U8, tag="wp_raw00")
+        nc.vector.tensor_copy(v_sc[:], tab_sc[:].indirect(list1[:]))
+        nc.sync.dma_start(
+            out=v_sc_second[:].bitcast(I32)[0:SHIFT_ROWS, :], in_=v_sc[:].bitcast(I32)[4 : 4 + SHIFT_ROWS, :]
+        )
+        load_raw("wth", 0, 1)
+        load_raw("wth", 1, 1)
         list3 = load_list("list3", offs3)
-        for a in range(2):
-            load_raw("wth", a, 1)
+        load_raw("wp", 0, 1)
         wc_w = tile("wc_w", [P, 2 * N], U32)
         nc.sync.dma_start(
             out=wc_w[:].bitcast(I32).rearrange("p (a c) -> p a c", a=2),
@@ -218,43 +212,41 @@ def tile_list_ion_pulse_compensation_kernel(
         )
         load_scales(nc.sync, wc_sc, wc_scales)
 
-        wb_ordered = tile("wb_ordered", [P, 2 * 2 * H], U8)
-        order_columns(wb_ordered[:].bitcast(U16), wb_w[:].bitcast(U16), nc.scalar.copy)
-        page_bf = tile("page_bf", [P, 2, PACK * BANK], BF16, tag="wb_w")
+        page_bf = [
+            laid.tile([P, PACK * BANK], BF16, name="page_bf%d" % h, align_bytes=64, offset=WORD * (JOIN_WORD + T2 * h))
+            for h in range(2)
+        ]
         for c0, c1 in LAST_CUTS:
             h = c0 // BANK
             cols = slice(c0 - BANK * h, c1 - BANK * h)
             nc.scalar.copy(
-                out=page_bf[:, h].bitcast(U32).rearrange("p (c u) -> p c u", u=2)[:, cols],
+                out=page_bf[h][:].bitcast(U32).rearrange("p (c u) -> p c u", u=2)[:, cols],
                 in_=pairs[h][:].rearrange("p u c e -> p u (c e)").bitcast(U32).rearrange("p u c -> p c u")[:, cols],
             )
-        wth_q = [[quantise("wth00", early_bf[:], PASS)]]
         v_codes = [gather_words(0)]
+        page_q = [quantise("page0", page_bf[0][:], BANK, first_word=2 * BANK)]
         v_codes.append(gather_words(1))
-        page_q = [quantise("page0", page_bf[:, 0], BANK, first_word=T)]
-        second_bf = tile("second_bf", [P, PACK * PASS], BF16)
+        wth_q = [[quantise("wth00", early_bf[:], PASS, first_word=T + BANK)]]
+        page_q.append(quantise("page1", page_bf[1][:], BANK, first_word=T))
+        second_bf = laid.tile([P, PACK * PASS], BF16, name="second_bf", align_bytes=64, offset=WORD * JOIN_WORD)
         round_weights(second_bf[:], ("wth", 1, 0), nc.vector.tensor_copy)
         wth_q[0].append(quantise("wth10", second_bf[:], PASS))
-        page_q.append(quantise("page1", page_bf[:, 1], BANK, tag="wth_raw10"))
 
         z_q = [(tile("z_codes%d" % g, [P, S], U32), tile("z_scales%d" % g, [P, S], U8)) for g in range(2)]
-        wp_late_bf = tile("wp_late_bf", [P, PACK * PASS], BF16, tag="wp_bf")
-        round_weights(wp_late_bf[:], ("wp", 0, 1), nc.vector.tensor_copy)
-        late_bf = tile("late_bf", [P, 2, PACK * PASS], BF16, tag="early_bf")
+        late_bf = tile("late_bf", [P, 2, PACK * PASS], BF16, tag="wth_raw10")
+        wth_q.append([])
+        for a in range(2):
+            round_weights(late_bf[:, a], ("wth", a, 1), nc.vector.tensor_copy)
+            wth_q[1].append(quantise("wth%d1" % a, late_bf[:, a], PASS))
+        wp_late_bf = tile("wp_late_bf", [P, PACK * PASS], BF16, tag="early_bf")
+        round_weights(wp_late_bf[:], ("wp", 0, 1), nc.vector.tensor_copy, slice(0, P // 2))
+        round_weights(wp_late_bf[:], ("wp", 0, 1), nc.scalar.copy, slice(P // 2, P))
+        wp_q.append(quantise("wp1", wp_late_bf[:], PASS))
 
-        def late_work(u):
-            if u == 0:
-                wp_q.append(quantise("wp1", wp_late_bf[:], PASS))
-                round_weights(late_bf[:, 0], ("wth", 0, 1), nc.vector.tensor_copy)
-            if u == 1:
-                wth_q.append([quantise("wth01", late_bf[:, 0], PASS)])
-                round_weights(late_bf[:, 1], ("wth", 1, 1), nc.vector.tensor_copy)
-
-
-        first_terms = tile("first_terms", [P, 2, PACK, S], F32, tag="wp_raw01")
-        last_terms = tile("last_terms", [P, PACK, S], F32, tag="early_bf")
+        first_terms = tile("first_terms", [P, 2, PACK, S], F32, tag="wth_raw11")
+        last_terms = tile("last_terms", [P, PACK, S], F32, tag="wp_raw01")
         terms_x = [first_terms[:, 0], last_terms[:]]
-        terms_b = {(0, 0): first_terms[:, 1], (1, 0): tile("term_b1", [P, PACK, HALF], F32, tag="wp_raw00")[:]}
+        terms_b = {(0, 0): first_terms[:, 1], (1, 0): tile("term_b1", [P, PACK, HALF], F32)[:]}
         a_rows, angles = {}, {}
 
         def project(i, which):
@@ -280,7 +272,7 @@ def tile_list_ion_pulse_compensation_kernel(
 
         def angle(u):
             g, t0, n, j0, j1 = units[u]
-            angles[u] = bank("th%d" % u, "scalar", RING)
+            angles[u] = bank("th%d" % u, "vector" if u < PACK else "scalar", RING)
             for k in range(n):
                 cols = slice(P * (t0 + k), P * (t0 + k + 1))
                 for a in (1, 0):
@@ -288,7 +280,7 @@ def tile_list_ion_pulse_compensation_kernel(
                     nc.tensor.matmul_mx(
                         out=angles[u][:, (j1 - j0) * k : (j1 - j0) * (k + 1)],
                         lhsT=codes[:, cols].bitcast(FP8X4), lhsT_scale=scales[:, cols],
-                        rhs=v_codes[a][:, j0:j1].bitcast(FP8X4), rhs_scale=v_sc[:, S * a + j0 : S * a + j1],
+                        rhs=v_codes[a][:, j0:j1].bitcast(FP8X4), rhs_scale=v_sc[4 * a : P, j0:j1],
                         start=(a == 1), stop=(a == 0),
                     )
 
@@ -296,14 +288,14 @@ def tile_list_ion_pulse_compensation_kernel(
             g, t0, n, j0, j1 = units[u]
             b = bank("b%d" % u, "vector" if u < PACK + 2 else "scalar", RING)
             for k in range(n):
-                for a in range(2):
+                for a in (1, 0):
                     c0 = H * a + PASS * g + P * (t0 + k)
                     nc.tensor.matmul_mx(
                         out=b[:, (j1 - j0) * k : (j1 - j0) * (k + 1)],
                         lhsT=wb_ordered[:, 2 * c0 : 2 * (c0 + P)].bitcast(FP4X4),
                         lhsT_scale=wb_sc_ordered[:, c0 : c0 + P],
-                        rhs=v_codes[a][:, j0:j1].bitcast(FP8X4), rhs_scale=v_sc[:, S * a + j0 : S * a + j1],
-                        start=(a == 0), stop=(a == 1),
+                        rhs=v_codes[a][:, j0:j1].bitcast(FP8X4), rhs_scale=(v_sc, v_sc_second)[a][:, j0:j1],
+                        start=(a == 1), stop=(a == 0),
                     )
             if PACK <= u < PACK + 3:
                 size = laid.tile([P, S], F32, name="size%d" % u, align_bytes=64, offset=WORD * held_word(u))
@@ -320,13 +312,12 @@ def tile_list_ion_pulse_compensation_kernel(
                 terms_b[g, j0][:, t0 : t0 + n],
                 b[:].rearrange("p (k j) -> p k j", k=n), sine[:].rearrange("p (k j) -> p k j", k=n), MULT,
             )
-            late_work(u)
             for i, h in halves[:1]:
                 project(i, (h,))
             nc.scalar.activation(cosine[:], size[:], ACT.Sin, bias=math.pi / 2, scale=-1.0)
             for i, h in halves[1:]:
                 project(i, (h,))
-            if u + 1 < len(units):
+            if PACK <= u + 1 < len(units):
                 angle(u + 1)
             return cosine
 
@@ -377,15 +368,15 @@ def tile_list_ion_pulse_compensation_kernel(
                     out=out.rearrange("(n p) j -> p n j", p=P)[:, n0 : n0 + per_bank, j0:j1], in_=result[:]
                 )
 
-        for i in range(PACK):
-            project(i, (0,))
-        angle(0)
+        for h in range(2):
+            for i in range(PACK - h):
+                project(i, (h,))
+        for u in range(PACK):
+            angle(u)
         for u in range(PACK):
             turn(u, 0, weigh(u, EARLY_HALVES[u]), 0, S)
-            if u == 1:
-                wth_q[1].append(quantise("wth11", late_bf[:, 1], PASS))
 
-        cosine = weigh(PACK, ((5, 1), (6, 0), (6, 1), (7, 0), (7, 1)))
+        cosine = weigh(PACK, [(i, h) for i in range(PACK, 2 * PACK) for h in range(2)])
         z_bf = combine(0, 0, S)
         turn(PACK, 0, cosine, 0, HALF)
         quantise_z(0, 0, S, z_bf)

@@ -31,6 +31,7 @@ HALF = S // 2
 LAST_CUTS = ((0, BANK // 2), (BANK // 2, BANK), (BANK, T2))
 EARLY_HALVES = (((3, 1),), (), (), ())
 ROW_BUFS = PACK + 2
+VECTOR_PART = 64
 TRIG_BUFS = 6
 RING = 4
 Z_BUFS = 3
@@ -158,6 +159,22 @@ def tile_list_ion_pulse_compensation_kernel(
                 in_=raws[key][:].rearrange("p k (m t) -> p m k t", t=PACK)[:, part],
             )
 
+        def round_and_quantise(name, rounded, key):
+            codes = tile(name + "_codes", [P, PASS], U32)
+            scales = tile(name + "_scales", [P, PASS], U8)
+            for t0 in (0, 2):
+                nc.vector.tensor_copy(
+                    out=rounded.rearrange("p (t m k) -> p m k t", t=PACK, k=PACK)[:, :, :, t0 : t0 + 2],
+                    in_=raws[key][:].rearrange("p k (m t) -> p m k t", t=PACK)[:, :, :, t0 : t0 + 2],
+                )
+            for t0 in (0, 2):
+                cols = slice(P * t0, P * (t0 + 2))
+                nc.vector.quantize_mx(
+                    out=codes[:, cols].bitcast(FP8X4), scales=scales[:, cols],
+                    in_=rounded[:, PACK * P * t0 : PACK * P * (t0 + 2)],
+                )
+            return codes[:], scales[:]
+
         def order_columns(ordered, natural, copy):
             copy(
                 out=ordered.rearrange("p (b t m) -> p b t m", m=P, t=PACK),
@@ -229,18 +246,16 @@ def tile_list_ion_pulse_compensation_kernel(
         wth_q = [[quantise("wth00", early_bf[:], PASS, first_word=T + BANK)]]
         page_q.append(quantise("page1", page_bf[1][:], BANK, first_word=T))
         second_bf = laid.tile([P, PACK * PASS], BF16, name="second_bf", align_bytes=64, offset=WORD * JOIN_WORD)
-        round_weights(second_bf[:], ("wth", 1, 0), nc.vector.tensor_copy)
-        wth_q[0].append(quantise("wth10", second_bf[:], PASS))
+        wth_q[0].append(round_and_quantise("wth10", second_bf[:], ("wth", 1, 0)))
 
         z_q = [(tile("z_codes%d" % g, [P, S], U32), tile("z_scales%d" % g, [P, S], U8)) for g in range(2)]
         late_bf = tile("late_bf", [P, 2, PACK * PASS], BF16, tag="wth_raw10")
         wth_q.append([])
         for a in range(2):
-            round_weights(late_bf[:, a], ("wth", a, 1), nc.vector.tensor_copy)
-            wth_q[1].append(quantise("wth%d1" % a, late_bf[:, a], PASS))
+            wth_q[1].append(round_and_quantise("wth%d1" % a, late_bf[:, a], ("wth", a, 1)))
         wp_late_bf = tile("wp_late_bf", [P, PACK * PASS], BF16, tag="early_bf")
-        round_weights(wp_late_bf[:], ("wp", 0, 1), nc.vector.tensor_copy, slice(0, P // 2))
-        round_weights(wp_late_bf[:], ("wp", 0, 1), nc.scalar.copy, slice(P // 2, P))
+        round_weights(wp_late_bf[:], ("wp", 0, 1), nc.vector.tensor_copy, slice(0, VECTOR_PART))
+        round_weights(wp_late_bf[:], ("wp", 0, 1), nc.scalar.copy, slice(VECTOR_PART, P))
         wp_q.append(quantise("wp1", wp_late_bf[:], PASS))
 
         first_terms = tile("first_terms", [P, 2, PACK, S], F32, tag="wth_raw11")
@@ -330,7 +345,8 @@ def tile_list_ion_pulse_compensation_kernel(
                 cosine[:, c0 + j0 : c0 + j1], MULT,
             )
 
-        def combine(g, j0, j1):
+        def combine(g, j0, j1, first=None):
+            first = j0 if first is None else first
             if g == 0:
                 z_bf = tile("z_first", [P, PACK * S], BF16, tag="wp_bf")
             else:
@@ -338,7 +354,7 @@ def tile_list_ion_pulse_compensation_kernel(
             nc.vector.tensor_tensor(
                 z_bf[:].rearrange("p (c i t) -> p c t i", i=4, t=PACK),
                 terms_x[g][:, :, j0:j1].rearrange("p t (c i) -> p c t i", i=4),
-                terms_b[g, j0].rearrange("p t (c i) -> p c t i", i=4),
+                terms_b[g, first][:, :, j0 - first : j1 - first].rearrange("p t (c i) -> p c t i", i=4),
                 ADD,
             )
             return z_bf
@@ -394,10 +410,15 @@ def tile_list_ion_pulse_compensation_kernel(
         cosine = weigh(PACK + 3)
         control(0, HALF, 2, (nc.scalar.copy, nc.scalar.copy))
         z_bf = combine(1, *third)
-        turn(PACK + 3, 0, cosine, *fourth)
+        eighths = ((S - P, S - P // 2), (S - P // 2, S))
+        turn(PACK + 3, 0, cosine, *eighths[0])
         quantise_z(1, *third, z_bf)
         for k in range(1, PACK):
-            turn(PACK + 3, k, cosine, *fourth)
-        quantise_z(1, *fourth, combine(1, *fourth))
+            turn(PACK + 3, k, cosine, *eighths[0])
+        for k in range(PACK):
+            turn(PACK + 3, k, cosine, *eighths[1])
+        sums = [combine(1, j0, j1, S - P) for j0, j1 in eighths]
+        for (j0, j1), z_bf in zip(eighths, sums):
+            quantise_z(1, j0, j1, z_bf)
         control(*third, 4, (nc.scalar.copy,))
         control(*fourth, 2, (nc.scalar.copy, nc.vector.tensor_copy))

@@ -31,7 +31,7 @@ HALF = S // 2
 LAST_CUTS = ((0, BANK // 2), (BANK // 2, BANK), (BANK, T2))
 EARLY_HALVES = (((3, 1),), (), (), ())
 ROW_BUFS = PACK + 2
-VECTOR_PART = 64
+VECTOR_PART = 96
 TRIG_BUFS = 6
 RING = 4
 Z_BUFS = 3
@@ -256,7 +256,6 @@ def tile_list_ion_pulse_compensation_kernel(
         wp_late_bf = tile("wp_late_bf", [P, PACK * PASS], BF16, tag="early_bf")
         round_weights(wp_late_bf[:], ("wp", 0, 1), nc.vector.tensor_copy, slice(0, VECTOR_PART))
         round_weights(wp_late_bf[:], ("wp", 0, 1), nc.scalar.copy, slice(VECTOR_PART, P))
-        wp_q.append(quantise("wp1", wp_late_bf[:], PASS))
 
         first_terms = tile("first_terms", [P, 2, PACK, S], F32, tag="wth_raw11")
         last_terms = tile("last_terms", [P, PACK, S], F32, tag="wp_raw01")
@@ -390,7 +389,10 @@ def tile_list_ion_pulse_compensation_kernel(
         for u in range(PACK):
             angle(u)
         for u in range(PACK):
-            turn(u, 0, weigh(u, EARLY_HALVES[u]), 0, S)
+            cosine = weigh(u, EARLY_HALVES[u])
+            if u == 2:
+                wp_q.append(quantise("wp1", wp_late_bf[:], PASS))
+            turn(u, 0, cosine, 0, S)
 
         cosine = weigh(PACK, [(i, h) for i in range(PACK, 2 * PACK) for h in range(2)])
         z_bf = combine(0, 0, S)

@@ -31,7 +31,7 @@ HALF = S // 2
 LAST_CUTS = ((0, BANK // 2), (BANK // 2, BANK), (BANK, T2))
 EARLY_HALVES = (((3, 1),), (), (), ())
 ROW_BUFS = PACK + 2
-VECTOR_PART = 96
+VECTOR_PART = 64
 TRIG_BUFS = 6
 RING = 4
 Z_BUFS = 3
@@ -348,6 +348,8 @@ def tile_list_ion_pulse_compensation_kernel(
             first = j0 if first is None else first
             if g == 0:
                 z_bf = tile("z_first", [P, PACK * S], BF16, tag="wp_bf")
+            elif j0 == 0:
+                z_bf = laid.tile([P, PACK * HALF], BF16, name="z_half", align_bytes=64, offset=WORD * held_word(PACK + 2))
             else:
                 z_bf = tile("z_bf", [P, PACK * (j1 - j0)], BF16, bufs=Z_BUFS)
             nc.vector.tensor_tensor(
@@ -366,7 +368,7 @@ def tile_list_ion_pulse_compensation_kernel(
             width = j1 - j0
             for n0 in range(0, N // P, per_bank):
                 acc = bank("out_acc", "scalar" if j1 == S else "vector", RING)
-                passes = (0, 1) if j1 == S else (1, 0)
+                passes = (1, 0) if per_bank == N // P else (0, 1)
                 for g in passes:
                     for k in range(per_bank):
                         c0 = N * g + P * (n0 + k)
@@ -390,26 +392,27 @@ def tile_list_ion_pulse_compensation_kernel(
             angle(u)
         for u in range(PACK):
             cosine = weigh(u, EARLY_HALVES[u])
+            turn(u, 0, cosine, 0, S)
             if u == 2:
                 wp_q.append(quantise("wp1", wp_late_bf[:], PASS))
-            turn(u, 0, cosine, 0, S)
 
-        cosine = weigh(PACK, [(i, h) for i in range(PACK, 2 * PACK) for h in range(2)])
+        late_halves = [(i, h) for i in range(PACK, 2 * PACK) for h in range(2)]
+        cosine = weigh(PACK)
+        before = weigh(PACK + 1, late_halves[:-3])
         z_bf = combine(0, 0, S)
         turn(PACK, 0, cosine, 0, HALF)
         quantise_z(0, 0, S, z_bf)
         turn(PACK, 1, cosine, 0, HALF)
-        cosine = weigh(PACK + 1)
-        for k in range(2):
-            turn(PACK + 1, k, cosine, 0, HALF)
         third, fourth = (HALF, HALF + P), (HALF + P, S)
-        cosine = weigh(PACK + 2)
-        z_bf = combine(1, 0, HALF)
-        turn(PACK + 2, 0, cosine, *third)
-        quantise_z(1, 0, HALF, z_bf)
-        for k in range(1, PACK):
+        cosine = weigh(PACK + 2, late_halves[-3:])
+        turn(PACK + 1, 0, before, 0, HALF)
+        for k in range(PACK - 1):
             turn(PACK + 2, k, cosine, *third)
+        turn(PACK + 1, 1, before, 0, HALF)
+        turn(PACK + 2, PACK - 1, cosine, *third)
+        z_bf = combine(1, 0, HALF)
         cosine = weigh(PACK + 3)
+        quantise_z(1, 0, HALF, z_bf)
         control(0, HALF, 2, (nc.scalar.copy, nc.scalar.copy))
         z_bf = combine(1, *third)
         eighths = ((S - P, S - P // 2), (S - P // 2, S))

@@ -31,7 +31,7 @@ HALF = S // 2
 LAST_CUTS = ((0, BANK // 2), (BANK // 2, BANK), (BANK, T2))
 EARLY_HALVES = (((3, 1),), (), (), ())
 ROW_BUFS = PACK + 2
-VECTOR_PART = 64
+VECTOR_PART = 80
 TRIG_BUFS = 6
 RING = 4
 Z_BUFS = 3

@@ -25,11 +25,11 @@ BANK = 512
 WORD = 4
 QUADRANTS = 4
 SHIFT_ROWS = 32 * (QUADRANTS - 1) + 4
-JOIN_WORD = 2 * T + 2 * T2
 HALF = S // 2
+PAIR_WORD = 2 * T
+JOIN_WORD = PAIR_WORD + 2 * T2
 
 LAST_CUTS = ((0, BANK // 2), (BANK // 2, BANK), (BANK, T2))
-EARLY_HALVES = (((3, 1),), (), (), ())
 ROW_BUFS = PACK + 2
 VECTOR_PART = 80
 TRIG_BUFS = 6
@@ -71,9 +71,9 @@ def tile_list_ion_pulse_compensation_kernel(
             engine.memset(scales[:].bitcast(I32), 0)
             return scales
 
-        def load_scales(queue, scales, src):
+        def load_scales(scales, src):
             for j in range(4):
-                queue.dma_start(
+                nc.sync.dma_start(
                     out=scales[:].bitcast(I32)[j:P:32, :].rearrange("p (a c) -> p a c", a=2),
                     in_=src.bitcast(I32)[:, j:16:4, :].rearrange("a q c -> q a c"),
                 )
@@ -90,15 +90,17 @@ def tile_list_ion_pulse_compensation_kernel(
 
         raws = {}
 
-        def load_raw(name, a, g, which=slice(0, PACK)):
-            key = (name, a, g)
-            if key not in raws:
-                if key == ("wth", 0, 0):
-                    raws[key] = laid.tile([P, PACK, PASS], F32, name="wth_raw00", align_bytes=64, offset=WORD * JOIN_WORD)
-                else:
-                    raws[key] = tile("%s_raw%d%d" % key, [P, PACK, PASS], F32)
+        def load_raw(name, a, g, first_word=None, parts=1):
+            label = "%s_raw%d%d" % (name, a, g)
+            if first_word is None:
+                raw = tile(label, [P, PACK, PASS], F32)
+            else:
+                raw = laid.tile([P, PACK, PASS], F32, name=label, align_bytes=64, offset=WORD * first_word)
             rows = {"wp": wp, "wth": wth}[name][PASS * a : PASS * (a + 1), PASS * g : PASS * (g + 1)]
-            nc.sync.dma_start(out=raws[key][:, which], in_=rows.rearrange("(p t) c -> p t c", t=PACK)[:, which])
+            for c0 in range(0, PASS, PASS // parts):
+                cols = slice(c0, c0 + PASS // parts)
+                nc.sync.dma_start(out=raw[:, :, cols], in_=rows.rearrange("(p t) c -> p t c", t=PACK)[:, :, cols])
+            raws[name, a, g] = raw
 
         def load_table(a):
             words = laid_words("tab%d" % a, T, T * a)
@@ -116,7 +118,7 @@ def tile_list_ion_pulse_compensation_kernel(
         zero = tile("zero", [P, 8], F32)
         nc.scalar.activation(zero[:], angle_zero[:], ACT.Sin)
 
-        wb_sc = zeroed("wb_sc", 2 * H, nc.vector, first_word=2 * T + T2 - HALF)
+        wb_sc = zeroed("wb_sc", 2 * H, first_word=PAIR_WORD + T2 - HALF)
         tab_sc = zeroed("tab_sc", T, nc.gpsimd)
         for q in range(QUADRANTS):
             nc.gpsimd.dma_start(
@@ -128,7 +130,7 @@ def tile_list_ion_pulse_compensation_kernel(
 
         planes.append(load_plane(1))
         news.extend(load_new(1, 2))
-        load_scales(nc.sync, wb_sc, wb_scales)
+        load_scales(wb_sc, wb_scales)
         wb_w = tile("wb_w", [P, 2 * 2 * H], U8)
         nc.sync.dma_start(
             out=wb_w[:].bitcast(I32).rearrange("p (a c) -> p a c", a=2),
@@ -138,15 +140,14 @@ def tile_list_ion_pulse_compensation_kernel(
         news.extend(load_new(2, PACK))
         load_raw("wp", 0, 0)
         planes.append(load_plane(3))
-        load_raw("wth", 0, 0)
+        load_raw("wth", 0, 0, JOIN_WORD)
         list1 = load_list("list1", offs)
-        tab = [load_table(0)]
-        tab.append(load_table(1))
+        tab = [load_table(a) for a in range(2)]
         load_raw("wth", 1, 0)
 
-        def quantise(name, rounded, width, first_word=None, tag=None):
+        def quantise(name, rounded, width, first_word=None):
             if first_word is None:
-                codes = tile(name + "_codes", [P, width], U32, tag=tag)
+                codes = tile(name + "_codes", [P, width], U32)
             else:
                 codes = laid_words(name + "_codes", width, first_word)
             scales = tile(name + "_scales", [P, width], U8)
@@ -159,14 +160,15 @@ def tile_list_ion_pulse_compensation_kernel(
                 in_=raws[key][:].rearrange("p k (m t) -> p m k t", t=PACK)[:, part],
             )
 
-        def round_and_quantise(name, rounded, key):
+        def round_and_quantise(name, rounded, key, landed=0):
             codes = tile(name + "_codes", [P, PASS], U32)
             scales = tile(name + "_scales", [P, PASS], U8)
+            into = rounded.rearrange("p (t m k) -> p m k t", t=PACK, k=PACK)
+            raw = raws[key][:].rearrange("p k (m t) -> p m k t", t=PACK)
+            if landed:
+                nc.vector.tensor_copy(out=into[:, 0:landed], in_=raw[:, 0:landed])
             for t0 in (0, 2):
-                nc.vector.tensor_copy(
-                    out=rounded.rearrange("p (t m k) -> p m k t", t=PACK, k=PACK)[:, :, :, t0 : t0 + 2],
-                    in_=raws[key][:].rearrange("p k (m t) -> p m k t", t=PACK)[:, :, :, t0 : t0 + 2],
-                )
+                nc.vector.tensor_copy(out=into[:, landed:, :, t0 : t0 + 2], in_=raw[:, landed:, :, t0 : t0 + 2])
             for t0 in (0, 2):
                 cols = slice(P * t0, P * (t0 + 2))
                 nc.vector.quantize_mx(
@@ -185,7 +187,7 @@ def tile_list_ion_pulse_compensation_kernel(
         order_columns(wb_sc_ordered[:], wb_sc[:], nc.gpsimd.tensor_copy)
 
         pairs = [
-            laid.tile([P, 2, BANK, 2], BF16, name="pairs%d" % h, align_bytes=64, offset=WORD * (2 * T + T2 * h))
+            laid.tile([P, 2, BANK, 2], BF16, name="pairs%d" % h, align_bytes=64, offset=WORD * (PAIR_WORD + T2 * h))
             for h in range(2)
         ]
 
@@ -219,7 +221,7 @@ def tile_list_ion_pulse_compensation_kernel(
             out=v_sc_second[:].bitcast(I32)[0:SHIFT_ROWS, :], in_=v_sc[:].bitcast(I32)[4 : 4 + SHIFT_ROWS, :]
         )
         load_raw("wth", 0, 1)
-        load_raw("wth", 1, 1)
+        load_raw("wth", 1, 1, parts=2)
         list3 = load_list("list3", offs3)
         load_raw("wp", 0, 1)
         wc_w = tile("wc_w", [P, 2 * N], U32)
@@ -227,7 +229,7 @@ def tile_list_ion_pulse_compensation_kernel(
             out=wc_w[:].bitcast(I32).rearrange("p (a c) -> p a c", a=2),
             in_=wc_words.rearrange("a p c i -> p a (c i)").bitcast(I32),
         )
-        load_scales(nc.sync, wc_sc, wc_scales)
+        load_scales(wc_sc, wc_scales)
 
         page_bf = [
             laid.tile([P, PACK * BANK], BF16, name="page_bf%d" % h, align_bytes=64, offset=WORD * (JOIN_WORD + T2 * h))
@@ -252,7 +254,7 @@ def tile_list_ion_pulse_compensation_kernel(
         late_bf = tile("late_bf", [P, 2, PACK * PASS], BF16, tag="wth_raw10")
         wth_q.append([])
         for a in range(2):
-            wth_q[1].append(round_and_quantise("wth%d1" % a, late_bf[:, a], ("wth", a, 1)))
+            wth_q[1].append(round_and_quantise("wth%d1" % a, late_bf[:, a], ("wth", a, 1), landed=a * P // 2))
         wp_late_bf = tile("wp_late_bf", [P, PACK * PASS], BF16, tag="early_bf")
         round_weights(wp_late_bf[:], ("wp", 0, 1), nc.vector.tensor_copy, slice(0, VECTOR_PART))
         round_weights(wp_late_bf[:], ("wp", 0, 1), nc.scalar.copy, slice(VECTOR_PART, P))
@@ -282,7 +284,7 @@ def tile_list_ion_pulse_compensation_kernel(
         units.extend((1, 0, PACK, j0, j0 + P) for j0 in (HALF, HALF + P))
 
         def held_word(u):
-            return (2 * T + T2, 0, S)[u - PACK]
+            return (PAIR_WORD + T2, 0, S)[u - PACK]
 
         def angle(u):
             g, t0, n, j0, j1 = units[u]
@@ -349,7 +351,8 @@ def tile_list_ion_pulse_compensation_kernel(
             if g == 0:
                 z_bf = tile("z_first", [P, PACK * S], BF16, tag="wp_bf")
             elif j0 == 0:
-                z_bf = laid.tile([P, PACK * HALF], BF16, name="z_half", align_bytes=64, offset=WORD * held_word(PACK + 2))
+                offset = WORD * held_word(PACK + 2)
+                z_bf = laid.tile([P, PACK * HALF], BF16, name="z_half", align_bytes=64, offset=offset)
             else:
                 z_bf = tile("z_bf", [P, PACK * (j1 - j0)], BF16, bufs=Z_BUFS)
             nc.vector.tensor_tensor(
@@ -391,37 +394,38 @@ def tile_list_ion_pulse_compensation_kernel(
         for u in range(PACK):
             angle(u)
         for u in range(PACK):
-            cosine = weigh(u, EARLY_HALVES[u])
+            cosine = weigh(u, ((PACK - 1, 1),) if u == 0 else ())
             turn(u, 0, cosine, 0, S)
             if u == 2:
                 wp_q.append(quantise("wp1", wp_late_bf[:], PASS))
 
+        half, third, fourth = (0, HALF), (HALF, HALF + P), (HALF + P, S)
         late_halves = [(i, h) for i in range(PACK, 2 * PACK) for h in range(2)]
-        cosine = weigh(PACK)
-        before = weigh(PACK + 1, late_halves[:-3])
+        cos_half_low = weigh(PACK)
+        cos_half_high = weigh(PACK + 1, late_halves[:-3])
         z_bf = combine(0, 0, S)
-        turn(PACK, 0, cosine, 0, HALF)
+        turn(PACK, 0, cos_half_low, *half)
         quantise_z(0, 0, S, z_bf)
-        turn(PACK, 1, cosine, 0, HALF)
-        third, fourth = (HALF, HALF + P), (HALF + P, S)
-        cosine = weigh(PACK + 2, late_halves[-3:])
-        turn(PACK + 1, 0, before, 0, HALF)
+        turn(PACK, 1, cos_half_low, *half)
+        cos_third = weigh(PACK + 2, late_halves[-3:])
+        turn(PACK + 1, 0, cos_half_high, *half)
         for k in range(PACK - 1):
-            turn(PACK + 2, k, cosine, *third)
-        turn(PACK + 1, 1, before, 0, HALF)
-        turn(PACK + 2, PACK - 1, cosine, *third)
-        z_bf = combine(1, 0, HALF)
-        cosine = weigh(PACK + 3)
-        quantise_z(1, 0, HALF, z_bf)
-        control(0, HALF, 2, (nc.scalar.copy, nc.scalar.copy))
+            turn(PACK + 2, k, cos_third, *third)
+        turn(PACK + 1, 1, cos_half_high, *half)
+        turn(PACK + 2, PACK - 1, cos_third, *third)
+        z_bf = combine(1, *half)
+        cos_fourth = weigh(PACK + 3)
+        quantise_z(1, *half, z_bf)
+        control(*half, 2, (nc.scalar.copy, nc.scalar.copy))
         z_bf = combine(1, *third)
+
         eighths = ((S - P, S - P // 2), (S - P // 2, S))
-        turn(PACK + 3, 0, cosine, *eighths[0])
+        turn(PACK + 3, 0, cos_fourth, *eighths[0])
         quantise_z(1, *third, z_bf)
         for k in range(1, PACK):
-            turn(PACK + 3, k, cosine, *eighths[0])
+            turn(PACK + 3, k, cos_fourth, *eighths[0])
         for k in range(PACK):
-            turn(PACK + 3, k, cosine, *eighths[1])
+            turn(PACK + 3, k, cos_fourth, *eighths[1])
         sums = [combine(1, j0, j1, S - P) for j0, j1 in eighths]
         for (j0, j1), z_bf in zip(eighths, sums):
             quantise_z(1, j0, j1, z_bf)

import math
from contextlib import ExitStack

import concourse.mybir as mybir

F32 = mybir.dt.float32
BF16 = mybir.dt.bfloat16
I32 = mybir.dt.int32
U32 = mybir.dt.uint32
U16 = mybir.dt.uint16
U8 = mybir.dt.uint8
FP8X4 = mybir.dt.float8_e4m3fn_x4
FP4X4 = mybir.dt.float4_e2m1fn_x4
ACT = mybir.ActivationFunctionType
MULT = mybir.AluOpType.mult
ADD = mybir.AluOpType.add

K, K2, H, N, T, T2, S = 1024, 512, 1024, 512, 2048, 1024, 512
FLOPS = 2 * (K2 * H * T2 + 2 * K * H * S + H * N * S)

P = 128
PACK = 4
PASS = P * PACK
BANK = 512
WORD = 4
QUADRANTS = 4
SHIFT_ROWS = 32 * (QUADRANTS - 1) + 4
HALF = S // 2
PAIR_WORD = 2 * T
JOIN_WORD = PAIR_WORD + 2 * T2

LAST_CUTS = ((0, BANK // 2), (BANK // 2, BANK), (BANK, T2))
ROW_BUFS = PACK + 2
VECTOR_PART = 80
TRIG_BUFS = 6
RING = 4
Z_BUFS = 3
RESULT_BUFS = 5


def tile_list_ion_pulse_compensation_kernel(
    tc, tab_words, tab_scales, offs, base, xs, offs2, offs3, wp, wth,
    wb_words, wb_scales, wc_words, wc_scales, out,
):
    nc = tc.nc
    with ExitStack() as ctx:
        lists = ctx.enter_context(tc.tile_pool(name="lists", bufs=1))
        sb = ctx.enter_context(tc.tile_pool(name="sb", bufs=1))
        laid = ctx.enter_context(tc.tile_pool(name="laid", bufs=1))
        ps = ctx.enter_context(tc.psum_pool(name="ps", bufs=1))

        def tile(name, shape, dtype, tag=None, bufs=1):
            return sb.tile(shape, dtype, name=name, tag=tag or name, bufs=bufs, align_bytes=64)

        def laid_words(name, width, first_word):
            return laid.tile([P, width], U32, name=name, align_bytes=64, offset=WORD * first_word)

        def bank(name, tag, bufs):
            return ps.tile([P, BANK], F32, name=name, tag=tag, bufs=bufs)

        def load_list(name, src):
            offsets = lists.tile([P, S // 16], U16, name=name, tag=name)
            nc.sync.dma_start(offsets[:], src)
            return offsets

        def zeroed(name, width, engine=nc.vector, first_word=None):
            if first_word is None:
                scales = tile(name, [P, width], U8)
            else:
                scales = laid.tile([P, width], U8, name=name, align_bytes=64, offset=WORD * first_word)
            engine.memset(scales[:].bitcast(I32), 0)
            return scales

        def load_scales(scales, src):
            for j in range(4):
                nc.sync.dma_start(
                    out=scales[:].bitcast(I32)[j:P:32, :].rearrange("p (a c) -> p a c", a=2),
                    in_=src.bitcast(I32)[:, j:16:4, :].rearrange("a q c -> q a c"),
                )

        def load_plane(t):
            page = tile("page%d" % t, [P, T2], F32, tag="rows", bufs=ROW_BUFS)
            nc.sync.dma_start(out=page[:], in_=base.rearrange("(p t) c -> p t c", t=PACK)[:, t, :])
            return page

        def load_new(t0, t1):
            new = tile("new%d" % t0, [P, t1 - t0, S], F32)
            nc.sync.dma_start(out=new[:], in_=xs.rearrange("(p t) c -> p t c", t=PACK)[:, t0:t1, :])
            return [new[:, t, :] for t in range(t1 - t0)]

        raws = {}

        def load_raw(name, a, g, first_word=None, parts=1):
            label = "%s_raw%d%d" % (name, a, g)
            if first_word is None:
                raw = tile(label, [P, PACK, PASS], F32)
            else:
                raw = laid.tile([P, PACK, PASS], F32, name=label, align_bytes=64, offset=WORD * first_word)
            rows = {"wp": wp, "wth": wth}[name][PASS * a : PASS * (a + 1), PASS * g : PASS * (g + 1)]
            for c0 in range(0, PASS, PASS // parts):
                cols = slice(c0, c0 + PASS // parts)
                nc.sync.dma_start(out=raw[:, :, cols], in_=rows.rearrange("(p t) c -> p t c", t=PACK)[:, :, cols])
            raws[name, a, g] = raw

        def load_table(a):
            words = laid_words("tab%d" % a, T, T * a)
            nc.sync.dma_start(
                out=words[:].bitcast(I32),
                in_=tab_words[a].rearrange("p t i -> p (t i)").bitcast(I32),
            )
            return words

        planes = [load_plane(0)]
        news = load_new(0, 1)
        list2 = load_list("list2", offs2)
        angle_zero = tile("angle_zero", [P, 8], F32)
        nc.vector.memset(angle_zero[:], 0.0)
        zero = tile("zero", [P, 8], F32)
        nc.scalar.activation(zero[:], angle_zero[:], ACT.Sin)

        wb_sc = zeroed("wb_sc", 2 * H, first_word=PAIR_WORD + T2 - HALF)
        tab_sc = zeroed("tab_sc", T, nc.gpsimd)
        for q in range(QUADRANTS):
            nc.gpsimd.dma_start(
                out=tab_sc[:].bitcast(I32)[32 * q : 32 * q + 8, :],
                in_=tab_scales.bitcast(I32)[:, 4 * q : 4 * q + 4, :],
            )
        v_sc_second = zeroed("v_sc_second", S)
        wc_sc = zeroed("wc_sc", 2 * N)

        planes.append(load_plane(1))
        news.extend(load_new(1, 2))
        load_scales(wb_sc, wb_scales)
        wb_w = tile("wb_w", [P, 2 * 2 * H], U8)
        nc.sync.dma_start(
            out=wb_w[:].bitcast(I32).rearrange("p (a c) -> p a c", a=2),
            in_=wb_words.bitcast(I32).rearrange("a p c -> p a c"),
        )
        planes.append(load_plane(2))
        news.extend(load_new(2, PACK))
        load_raw("wp", 0, 0)
        planes.append(load_plane(3))
        load_raw("wth", 0, 0, JOIN_WORD)
        list1 = load_list("list1", offs)
        tab = [load_table(a) for a in range(2)]
        load_raw("wth", 1, 0)

        def quantise(name, rounded, width, first_word=None):
            if first_word is None:
                codes = tile(name + "_codes", [P, width], U32)
            else:
                codes = laid_words(name + "_codes", width, first_word)
            scales = tile(name + "_scales", [P, width], U8)
            nc.vector.quantize_mx(out=codes[:].bitcast(FP8X4), scales=scales[:], in_=rounded)
            return codes[:], scales[:]

        def round_weights(rounded, key, copy, part=slice(0, P)):
            copy(
                out=rounded.rearrange("p (t m k) -> p m k t", t=PACK, k=PACK)[:, part],
                in_=raws[key][:].rearrange("p k (m t) -> p m k t", t=PACK)[:, part],
            )

        def round_and_quantise(name, rounded, key, landed=0):
            codes = tile(name + "_codes", [P, PASS], U32)
            scales = tile(name + "_scales", [P, PASS], U8)
            into = rounded.rearrange("p (t m k) -> p m k t", t=PACK, k=PACK)
            raw = raws[key][:].rearrange("p k (m t) -> p m k t", t=PACK)
            if landed:
                nc.vector.tensor_copy(out=into[:, 0:landed], in_=raw[:, 0:landed])
            for t0 in (0, 2):
                nc.vector.tensor_copy(out=into[:, landed:, :, t0 : t0 + 2], in_=raw[:, landed:, :, t0 : t0 + 2])
            for t0 in (0, 2):
                cols = slice(P * t0, P * (t0 + 2))
                nc.vector.quantize_mx(
                    out=codes[:, cols].bitcast(FP8X4), scales=scales[:, cols],
                    in_=rounded[:, PACK * P * t0 : PACK * P * (t0 + 2)],
                )
            return codes[:], scales[:]

        def order_columns(ordered, natural, copy):
            copy(
                out=ordered.rearrange("p (b t m) -> p b t m", m=P, t=PACK),
                in_=natural.rearrange("p (b m t) -> p b t m", m=P, t=PACK),
            )

        wb_sc_ordered = tile("wb_sc_ordered", [P, 2 * H], U8)
        order_columns(wb_sc_ordered[:], wb_sc[:], nc.gpsimd.tensor_copy)

        pairs = [
            laid.tile([P, 2, BANK, 2], BF16, name="pairs%d" % h, align_bytes=64, offset=WORD * (PAIR_WORD + T2 * h))
            for h in range(2)
        ]

        def scatter(t):
            page = planes[t]
            nc.vector.tensor_copy(page[:].indirect(list2[:]), news[t])
            for c0, c1 in LAST_CUTS if t == PACK - 1 else ((0, BANK), (BANK, T2)):
                h = c0 // BANK
                nc.gpsimd.tensor_scalar(
                    pairs[h][:, t // 2, c0 - BANK * h : c1 - BANK * h, t % 2], page[:, c0:c1], 1.0, 0.0, MULT, ADD
                )

        def gather_words(a):
            codes = tile("v_codes%d" % a, [P, S], U32)
            nc.vector.tensor_copy(codes[:], tab[a][:].indirect(list1[:]))
            return codes

        wp_bf = tile("wp_bf", [P, PACK * PASS], BF16)
        early_bf = tile("early_bf", [P, PACK * PASS], BF16)
        for t in range(PACK):
            scatter(t)
        wb_ordered = tile("wb_ordered", [P, 2 * 2 * H], U8)
        order_columns(wb_ordered[:].bitcast(U16), wb_w[:].bitcast(U16), nc.scalar.copy)
        round_weights(wp_bf[:], ("wp", 0, 0), nc.scalar.copy)
        wp_q = [quantise("wp0", wp_bf[:], PASS)]
        round_weights(early_bf[:], ("wth", 0, 0), nc.scalar.copy)

        v_sc = tile("v_sc", [P, S], U8, tag="wp_raw00")
        nc.vector.tensor_copy(v_sc[:], tab_sc[:].indirect(list1[:]))
        nc.sync.dma_start(
            out=v_sc_second[:].bitcast(I32)[0:SHIFT_ROWS, :], in_=v_sc[:].bitcast(I32)[4 : 4 + SHIFT_ROWS, :]
        )
        load_raw("wth", 0, 1)
        load_raw("wth", 1, 1, parts=2)
        list3 = load_list("list3", offs3)
        load_raw("wp", 0, 1)
        wc_w = tile("wc_w", [P, 2 * N], U32)
        nc.sync.dma_start(
            out=wc_w[:].bitcast(I32).rearrange("p (a c) -> p a c", a=2),
            in_=wc_words.rearrange("a p c i -> p a (c i)").bitcast(I32),
        )
        load_scales(wc_sc, wc_scales)

        page_bf = [
            laid.tile([P, PACK * BANK], BF16, name="page_bf%d" % h, align_bytes=64, offset=WORD * (JOIN_WORD + T2 * h))
            for h in range(2)
        ]
        for c0, c1 in LAST_CUTS:
            h = c0 // BANK
            cols = slice(c0 - BANK * h, c1 - BANK * h)
            nc.scalar.copy(
                out=page_bf[h][:].bitcast(U32).rearrange("p (c u) -> p c u", u=2)[:, cols],
                in_=pairs[h][:].rearrange("p u c e -> p u (c e)").bitcast(U32).rearrange("p u c -> p c u")[:, cols],
            )
        v_codes = [gather_words(0)]
        page_q = [quantise("page0", page_bf[0][:], BANK, first_word=2 * BANK)]
        v_codes.append(gather_words(1))
        wth_q = [[quantise("wth00", early_bf[:], PASS, first_word=T + BANK)]]
        page_q.append(quantise("page1", page_bf[1][:], BANK, first_word=T))
        second_bf = laid.tile([P, PACK * PASS], BF16, name="second_bf", align_bytes=64, offset=WORD * JOIN_WORD)
        wth_q[0].append(round_and_quantise("wth10", second_bf[:], ("wth", 1, 0)))

        z_q = [(tile("z_codes%d" % g, [P, S], U32), tile("z_scales%d" % g, [P, S], U8)) for g in range(2)]
        late_bf = tile("late_bf", [P, 2, PACK * PASS], BF16, tag="wth_raw10")
        wth_q.append([])
        for a in range(2):
            wth_q[1].append(round_and_quantise("wth%d1" % a, late_bf[:, a], ("wth", a, 1), landed=a * P // 2))
        wp_late_bf = tile("wp_late_bf", [P, PACK * PASS], BF16, tag="early_bf")
        round_weights(wp_late_bf[:], ("wp", 0, 1), nc.vector.tensor_copy, slice(0, VECTOR_PART))
        round_weights(wp_late_bf[:], ("wp", 0, 1), nc.scalar.copy, slice(VECTOR_PART, P))

        first_terms = tile("first_terms", [P, 2, PACK, S], F32, tag="wth_raw11")
        last_terms = tile("last_terms", [P, PACK, S], F32, tag="wp_raw01")
        terms_x = [first_terms[:, 0], last_terms[:]]
        terms_b = {(0, 0): first_terms[:, 1], (1, 0): tile("term_b1", [P, PACK, HALF], F32)[:]}
        a_rows, angles = {}, {}

        def project(i, which):
            codes, scales = wp_q[i // PACK]
            cols = slice(P * (i % PACK), P * (i % PACK + 1))
            if i not in a_rows:
                a_rows[i] = tile("a%d" % i, [P, T2], F32, tag="rows", bufs=ROW_BUFS)
            for h in which:
                acc = bank("a_acc%d%d" % (i, h), "scalar", RING)
                nc.tensor.matmul_mx(
                    out=acc[:], lhsT=codes[:, cols].bitcast(FP8X4), lhsT_scale=scales[:, cols],
                    rhs=page_q[h][0].bitcast(FP8X4), rhs_scale=page_q[h][1],
                    start=True, stop=True,
                )
                nc.scalar.copy(out=a_rows[i][:, BANK * h : BANK * (h + 1)], in_=acc[:])

        units = [(0, t, 1, 0, S) for t in range(PACK)]
        units.extend((1, t0, 2, 0, HALF) for t0 in (0, 2))
        units.extend((1, 0, PACK, j0, j0 + P) for j0 in (HALF, HALF + P))

        def held_word(u):
            return (PAIR_WORD + T2, 0, S)[u - PACK]

        def angle(u):
            g, t0, n, j0, j1 = units[u]
            angles[u] = bank("th%d" % u, "vector" if u < PACK else "scalar", RING)
            for k in range(n):
                cols = slice(P * (t0 + k), P * (t0 + k + 1))
                for a in (1, 0):
                    codes, scales = wth_q[g][a]
                    nc.tensor.matmul_mx(
                        out=angles[u][:, (j1 - j0) * k : (j1 - j0) * (k + 1)],
                        lhsT=codes[:, cols].bitcast(FP8X4), lhsT_scale=scales[:, cols],
                        rhs=v_codes[a][:, j0:j1].bitcast(FP8X4), rhs_scale=v_sc[4 * a : P, j0:j1],
                        start=(a == 1), stop=(a == 0),
                    )

        def weigh(u, halves=()):
            g, t0, n, j0, j1 = units[u]
            b = bank("b%d" % u, "vector" if u < PACK + 2 else "scalar", RING)
            for k in range(n):
                for a in (1, 0):
                    c0 = H * a + PASS * g + P * (t0 + k)
                    nc.tensor.matmul_mx(
                        out=b[:, (j1 - j0) * k : (j1 - j0) * (k + 1)],
                        lhsT=wb_ordered[:, 2 * c0 : 2 * (c0 + P)].bitcast(FP4X4),
                        lhsT_scale=wb_sc_ordered[:, c0 : c0 + P],
                        rhs=v_codes[a][:, j0:j1].bitcast(FP8X4), rhs_scale=(v_sc, v_sc_second)[a][:, j0:j1],
                        start=(a == 1), stop=(a == 0),
                    )
            if PACK <= u < PACK + 3:
                size = laid.tile([P, S], F32, name="size%d" % u, align_bytes=64, offset=WORD * held_word(u))
            else:
                size = tile("size", [P, S], F32, bufs=2)
            sine = tile("sine", [P, S], F32, bufs=TRIG_BUFS)
            cosine = tile("cosine", [P, S], F32, bufs=TRIG_BUFS)
            nc.scalar.activation(sine[:], angles[u][:], ACT.Sin)
            nc.scalar.activation(size[:], angles[u][:], ACT.Abs, bias=zero[:, 0:1])
            if (g, j0) not in terms_b:
                term = laid.tile([P, PACK, P], F32, name="term_b%d" % u, align_bytes=64, offset=WORD * held_word(u - 1))
                terms_b[g, j0] = term[:]
            nc.vector.tensor_tensor(
                terms_b[g, j0][:, t0 : t0 + n],
                b[:].rearrange("p (k j) -> p k j", k=n), sine[:].rearrange("p (k j) -> p k j", k=n), MULT,
            )
            for i, h in halves[:1]:
                project(i, (h,))
            nc.scalar.activation(cosine[:], size[:], ACT.Sin, bias=math.pi / 2, scale=-1.0)
            for i, h in halves[1:]:
                project(i, (h,))
            if PACK <= u + 1 < len(units):
                angle(u + 1)
            return cosine

        def turn(u, k, cosine, j0, j1):
            g, t0, n, first, end = units[u]
            c0 = (end - first) * k - first
            nc.vector.tensor_tensor(
                terms_x[g][:, t0 + k, j0:j1],
                a_rows[PACK * g + t0 + k][:].indirect(list3[:, j0 // 16 : j1 // 16]),
                cosine[:, c0 + j0 : c0 + j1], MULT,
            )

        def combine(g, j0, j1, first=None):
            first = j0 if first is None else first
            if g == 0:
                z_bf = tile("z_first", [P, PACK * S], BF16, tag="wp_bf")
            elif j0 == 0:
                offset = WORD * held_word(PACK + 2)
                z_bf = laid.tile([P, PACK * HALF], BF16, name="z_half", align_bytes=64, offset=offset)
            else:
                z_bf = tile("z_bf", [P, PACK * (j1 - j0)], BF16, bufs=Z_BUFS)
            nc.vector.tensor_tensor(
                z_bf[:].rearrange("p (c i t) -> p c t i", i=4, t=PACK),
                terms_x[g][:, :, j0:j1].rearrange("p t (c i) -> p c t i", i=4),
                terms_b[g, first][:, :, j0 - first : j1 - first].rearrange("p t (c i) -> p c t i", i=4),
                ADD,
            )
            return z_bf

        def quantise_z(g, j0, j1, z_bf):
            codes, scales = z_q[g]
            nc.vector.quantize_mx(out=codes[:, j0:j1].bitcast(FP8X4), scales=scales[:, j0:j1], in_=z_bf[:])

        def control(j0, j1, per_bank, copies):
            width = j1 - j0
            for n0 in range(0, N // P, per_bank):
                acc = bank("out_acc", "scalar" if j1 == S else "vector", RING)
                passes = (1, 0) if per_bank == N // P else (0, 1)
                for g in passes:
                    for k in range(per_bank):
                        c0 = N * g + P * (n0 + k)
                        nc.tensor.matmul_mx(
                            out=acc[:, width * k : width * (k + 1)],
                            lhsT=wc_w[:, c0 : c0 + P].bitcast(FP8X4), lhsT_scale=wc_sc[:, c0 : c0 + P],
                            rhs=z_q[g][0][:, j0:j1].bitcast(FP8X4), rhs_scale=z_q[g][1][:, j0:j1],
                            start=(g == passes[0] and k == 0), stop=(g == passes[1] and k == per_bank - 1),
                        )
                result = tile("result", [P, per_bank, width], F32, bufs=RESULT_BUFS)
                copy = copies[n0 // per_bank]
                copy(out=result[:].rearrange("p n j -> p (n j)"), in_=acc[:, 0 : per_bank * width])
                nc.sync.dma_start(
                    out=out.rearrange("(n p) j -> p n j", p=P)[:, n0 : n0 + per_bank, j0:j1], in_=result[:]
                )

        for h in range(2):
            for i in range(PACK - h):
                project(i, (h,))
        for u in range(PACK):
            angle(u)
        for u in range(PACK):
            cosine = weigh(u, ((PACK - 1, 1),) if u == 0 else ())
            turn(u, 0, cosine, 0, S)
            if u == 2:
                wp_q.append(quantise("wp1", wp_late_bf[:], PASS))

        half, third, fourth = (0, HALF), (HALF, HALF + P), (HALF + P, S)
        late_halves = [(i, h) for i in range(PACK, 2 * PACK) for h in range(2)]
        cos_half_low = weigh(PACK)
        cos_half_high = weigh(PACK + 1, late_halves[:-3])
        z_bf = combine(0, 0, S)
        turn(PACK, 0, cos_half_low, *half)
        quantise_z(0, 0, S, z_bf)
        turn(PACK, 1, cos_half_low, *half)
        cos_third = weigh(PACK + 2, late_halves[-3:])
        turn(PACK + 1, 0, cos_half_high, *half)
        for k in range(PACK - 1):
            turn(PACK + 2, k, cos_third, *third)
        turn(PACK + 1, 1, cos_half_high, *half)
        turn(PACK + 2, PACK - 1, cos_third, *third)
        z_bf = combine(1, *half)
        cos_fourth = weigh(PACK + 3)
        quantise_z(1, *half, z_bf)
        control(*half, 2, (nc.scalar.copy, nc.scalar.copy))
        z_bf = combine(1, *third)

        eighths = ((S - P, S - P // 2), (S - P // 2, S))
        turn(PACK + 3, 0, cos_fourth, *eighths[0])
        quantise_z(1, *third, z_bf)
        for k in range(1, PACK):
            turn(PACK + 3, k, cos_fourth, *eighths[0])
        for k in range(PACK):
            turn(PACK + 3, k, cos_fourth, *eighths[1])
        sums = [combine(1, j0, j1, S - P) for j0, j1 in eighths]
        for (j0, j1), z_bf in zip(eighths, sums):
            quantise_z(1, j0, j1, z_bf)
        control(*third, 4, (nc.scalar.copy,))
        control(*fourth, 2, (nc.scalar.copy, nc.vector.tensor_copy))
